import numpy as np, ml_dtypes
CORES = [9,25,41,57]
N = 4
BF = ml_dtypes.bfloat16
W, T, FC, SC, HB, RO, NB, LN = 4096, 256, 1024, 512, 4096, 3, 2, 64
def pick(tab, ix):
    return np.take_along_axis(tab, ix[:, :, None, :], 3)
def hashes(hw, z):
    return np.sum(hw * z, axis=-2) & (HB - 1)
def compose(a, b):
    return (((a * b) >> 5) + a + 37 * b) & (W - 1)
def parts(rng):
    x = rng.integers(0, 256, (N, 8, 16, W)); x[:, :, 15] = rng.integers(0, 16, (N, 8, W))
    fw = rng.integers(0, W, (N, 8, 16, FC)); sw = rng.integers(0, W, (N, 8, 16, SC)); aw = rng.integers(0, W, (N, 8, 16, SC))
    z = rng.integers(0, 256, (N, 8, 16, T)); z[:, :, 15] = 0
    q = rng.integers(0, W, (N, 8, T)); hw = rng.integers(1, 256, (N, 8, 16, 1)); hw[:, :, 15] = 0
    th = rng.integers(800, 1101, (N, 8, 1))
    return x, fw, sw, aw, z, q, hw, th
def pack(x, fw, sw, aw, z, q, hw, th):
    return {"lx": x.reshape(N, 128, W).astype(np.float32).astype(BF), "fw": fw.reshape(N, 128, FC).astype(np.int32), "sw": sw.reshape(N, 128, SC).astype(np.int32), "aw": aw.reshape(N, 128, SC).astype(np.int32),
            "z0": z.reshape(N, 128, T).astype(np.float32).astype(BF), "q0": q.astype(np.int32), "hw": hw.reshape(N, 128, 1).astype(np.int32), "th": th.astype(np.int32)}
def setup_inputs(rng):
    return pack(*parts(rng))
def setup_inputs_spread(rng):
    x, fw, sw, aw, z, q, hw, th = parts(rng)
    x[:, :, :15] = (np.exp2(8 * rng.random((N, 8, 1, W))) * rng.random((N, 8, 15, W))).astype(np.int64); x[:, :, 15] = (16 * rng.random((N, 8, W)) ** 2).astype(np.int64)
    z[:, :, :15] = (np.exp2(8 * rng.random((N, 8, 1, T))) * rng.random((N, 8, 15, T))).astype(np.int64)
    e = rng.choice(np.array([1.0, 2.0, 4.0]), (N, 8, 1, 1))
    fw, sw, aw = [np.minimum((W * rng.random(v.shape) ** e).astype(np.int64), W - 1) for v in (fw, sw, aw)]
    q = np.minimum((W * rng.random(q.shape) ** e[..., 0]).astype(np.int64), W - 1)
    hw[:, :, :15] = (np.exp2(8 * rng.random((N, 8, 15, 1))) * rng.random((N, 8, 15, 1))).astype(np.int64)
    th = rng.choice(np.array([150, 250, 400, 800, 1300, 2500, 4095]), (N, 8, 1))
    return pack(x, fw, sw, aw, z, q, hw, th)
def setup_inputs_ends(rng):
    def two(hi, *shape):
        return hi * rng.integers(0, 2, shape)
    x = two(255, N, 8, 16, W); k = rng.integers(0, 3, (N, 8, 1, W)); x = np.where(k == 0, x, np.where(k == 1, 0, 255)); x[:, :, 15] = two(15, N, 8, W)
    fw = two(W - 1, N, 8, 16, FC); sw = two(W - 1, N, 8, 16, SC); aw = two(W - 1, N, 8, 16, SC); sw[..., SC - 1] = W - 1; aw[..., SC - 1] = W - 1
    z = two(255, N, 8, 16, T); k = rng.integers(0, 3, (N, 8, 1, T)); z = np.where(k == 0, z, np.where(k == 1, 0, 255)); z[..., T - 1] = 255
    q = two(W - 1, N, 8, T); hw = two(255, N, 8, 16, 1); hw[:, 7] = 255; hw[:, 0, 0] = 0
    hw[:, 6] = 0; hw[:, 6, 0] = 255; hw[:, 6, 1] = 2; hw[:, :, 15] = 0
    th = np.full((N, 8, 1), 4095); used = np.array([0, W - 1, W - 37, compose(W - 1, W - 1)])
    for a in range(N):
        for g in range(8):
            m = (g + N - 1 - a) % 4
            if m == 0:
                x[a, g][:, 0] = 0; x[a, g][:15, W - 1] = 255; x[a, g, 15, W - 1] = 15
                if g < 4: th[a, g] = 0
            elif m == 2:
                x[a, g][:15, used] = 255; x[a, g][15, used] = 15
            elif m == 3:
                x[a, g][:, used] = 0; z[a, g][:, T // 2:] = 255
    z[:, :, 15] = 0
    return pack(x, fw, sw, aw, z, q, hw, th)
def setup_inputs_corners(rng):
    x, fw, sw, aw, z, q, hw, th = parts(rng); x[:, :, 15] = rng.choice(np.array([0, 1, 13, 14, 15]), (N, 8, W))
    for a in range(N):
        for g in range(8):
            m = (a + g) % 4
            if m == 0:
                v = rng.permutation(W)[:T]; d = rng.integers(99, 102, T); y = np.array(z[a, g]); y[0] = np.where(y[0] < 128, y[0] + d, y[0] - d); y[15] = 15
                x[a, g][:, v] = y; q[a, g] = v; th[a, g] = 100
            elif m == 1:
                h = hashes(hw[a, g], z[a, g]); fw[a, g][:, h >> 2] = compose(sw[a, g][:, h & (SC - 1)], aw[a, g][:, h >> 3]); th[a, g] = 4095
            elif m == 2:
                fw[a, g] = rng.choice(np.array([0, 1, W - 2, W - 1]), (16, FC)); q[a, g] = np.arange(T); hw[a, g, :15] = 255 * (a & 1); th[a, g] = 1200
            else:
                x[a, g][:15] = 128; th[a, g] = 1000
    return pack(x, fw, sw, aw, z, q, hw, th)
def setup_inputs_crowd(rng):
    x, fw, sw, aw, z, q, hw, th = parts(rng); mid = rng.integers(0, 80, (N, 8, 15, 1))
    for a in range(N):
        for g in range(8):
            t = int(rng.integers(0, T)); odd = np.array(z[a, g][:, t]); one = np.array(z[a, g][:, (t + 1) % T]); full = np.array(one); full[15] = 15
            if g == 4 or g == 5:
                to = (a + 1 + np.arange(T) // (T // NB)) % N; e = rng.multinomial(T - rng.integers(0, 3, T), np.full(15, 1.0 / 15)).T
                x[a, g][:15] = mid[a, g]; z[a, g][:15] = np.minimum(mid[a, g] + mid[:, g, :, 0][to].T + e, 255); th[a, g] = g - 4
                if g == 5: z[a, g][:15, t] = mid[a, g, :, 0]; x[a, g, 15, q[a, g, t]] = 15
            elif g == 7 and a & 1:
                hw[a, g] = 0; hw[a, g, 0] = 8; hw[a, g, 1] = 1; th[a, g] = 4095
                y = rng.integers(96, 160, (16, T)); y[0] = rng.permutation(256)[:T]; y[1] = rng.integers(0, 8, T); y[15] = 0; z[a, g] = y
                h = hashes(hw[a, g], y)[:LN]; cs = compose(sw[a, g][:, h & (SC - 1)], aw[a, g][:, h >> 3]); near = np.isin(np.arange(W), cs); rest = np.flatnonzero(~near)
                x[a, g][2:15] = np.where(near, rng.integers(96, 160, (13, W)), 255 * rng.integers(0, 2, (13, W))); x[a, g][15] = np.where(near, 15, 0)
                fw[a, g][:, h >> 2] = rng.choice(rest, (16, LN)); q[a, g, :LN] = rng.choice(rest, LN)
            elif g == 7:
                z[a, g] = z[a, g][:, np.arange(T) & 3]; th[a, g] = 4095
            else:
                z[a, g] = one[:, None]; h = int(hashes(hw[a, g], one[:, None])[0]); cs = compose(sw[a, g][:, h & (SC - 1)], aw[a, g][:, h >> 3])
                if g < 2:
                    v = int(rng.integers(0, W)); x[a, g][:, v] = full; q[a, g] = v; th[a, g] = 1
                elif g < 4:
                    v = int(cs[5]); o = (v + 1) & (W - 1); x[a, g][:, v] = full; q[a, g] = o; c = fw[a, g][:, h >> 2]; fw[a, g][:, h >> 2] = np.where(c == v, o, c); th[a, g] = 4095 if g == 2 else 1
                else:
                    p = rng.permutation(W); p = p[~np.isin(p, cs)][:T]; x[a, g][:, p] = full[:, None]; q[a, g] = p; fw[a, g][:, h >> 2] = cs; th[a, g] = 4095
                if g in (1, 3): z[a, g][:, t] = odd
    return pack(x, fw, sw, aw, z, q, hw, th)
def setup_inputs_ties(rng):
    x, fw, sw, aw, z, q, hw, th = parts(rng)
    x[:, :, :15] = rng.integers(100, 102, (N, 8, 15, W)); x[:, :, 15] = rng.integers(3, 5, (N, 8, W)); z[:, :, :15] = rng.integers(100, 102, (N, 8, 15, T)); th = rng.integers(178, 187, (N, 8, 1))
    x[:, 2::3, :15] = rng.integers(0, 4, (N, 2, 15, W)); x[:, 2::3, 15] = 0; th[:, 2::3] = rng.integers(3985, 4006, (N, 2, 1))
    less = (np.arange(T) & 7) == rng.integers(0, 8, (N, 2, 1, 1))
    z[:, 2::3, :15] = np.where(less, rng.integers(200, 256, (N, 2, 15, T)), rng.integers(254, 256, (N, 2, 15, T)))
    mid = rng.integers(140, 160, (N, 8, 15)); goal = 2049 + 2 * rng.integers(0, 4, (N, 8))
    for a in range(N):
        to = (a + 1 + np.arange(T) // (T // NB)) % N
        for g in (1, 6):
            n = (a + g // 3) % 4
            least = goal[to, g] + rng.integers(-2, 2, T)
            d = rng.multinomial(np.sum(mid[to, g], axis=1) - least, np.full(15, 1.0 / 15)).T
            x[a, g][:15] = mid[a, g][:, None]; x[a, g][15] = 15; z[a, g][:15] = np.minimum(mid[a, g][:, None] + d, 255)
            z[a, g][:, rng.permutation(T)[:n]] = 0; th[a, g] = goal[a, g] - n
    return pack(x, fw, sw, aw, z, q, hw, th)
def check_inputs(d):
    bad = []
    for k, lo, hi in (("lx", 0, 255), ("fw", 0, W - 1), ("sw", 0, W - 1), ("aw", 0, W - 1), ("z0", 0, 255), ("q0", 0, W - 1), ("hw", 0, 255), ("th", 0, 4095)):
        v = np.asarray(d[k]).astype(np.float64)
        if not (np.min(v) >= lo and np.max(v) <= hi): bad.append("range of " + k)
        elif np.any(v != np.floor(v)): bad.append("whole numbers of " + k)
    for k, hi in (("lx", 15), ("z0", 0), ("hw", 0)):
        v = np.asarray(d[k]).astype(np.float64)[:, 15::16]
        if not np.max(v) <= hi: bad.append("rows 16*g + 15 of " + k)
    return bad
def reference(lx, fw, sw, aw, z0, q0, hw, th):
    x = lx.astype(np.float32).astype(np.int64).reshape(N, 8, 16, W); fd = fw.astype(np.int64).reshape(N, 8, 16, FC)
    sd = sw.astype(np.int64).reshape(N, 8, 16, SC); ad = aw.astype(np.int64).reshape(N, 8, 16, SC)
    z = z0.astype(np.float32).astype(np.int64).reshape(N, 8, 16, T); q = q0.astype(np.int64).reshape(N, 8, T)
    wt = hw.astype(np.int64).reshape(N, 8, 16, 1); lim = th.astype(np.int64).reshape(N, 8, 1); none = np.zeros((N, 8, 1), np.int64)
    own = (np.arange(T)[None, :] & 15) == np.arange(16)[:, None]; BL = T // NB
    for s in range(RO):
        h = hashes(wt, z); col = h >> 2
        stored = np.where(own, q[:, :, None, :], pick(fd, col)); comp = compose(pick(sd, h & (SC - 1)), pick(ad, h >> 3))
        names = np.concatenate([stored, comp], axis=2)
        words = pick(x, names.reshape(N, 8, 32 * T)).reshape(N, 8, 16, 32, T)
        tm = np.sum(np.abs(words[:, :, :15] - z[:, :, :15, None, :]), axis=2) + 16 * (15 - words[:, :, 15])
        bs = np.argmin(tm[:, :, :16], axis=2); bc = 16 + np.argmin(tm[:, :, 16:], axis=2); slow = np.argmax(tm[:, :, :16], axis=2)
        ts, tc = [np.take_along_axis(tm, b[:, :, None, :], 2)[:, :, 0] for b in (bs, bc)]
        cw = tc < ts; win = np.minimum(ts, tc) < lim + none
        wn = np.take_along_axis(names, np.where(cw, bc, bs)[:, :, None, :], 2)[:, :, 0]; ln = np.take_along_axis(names, np.where(cw, bs, bc)[:, :, None, :], 2)[:, :, 0]
        xw = pick(x, wn); top = np.max(words[:, :, :, 16:], axis=3)
        xn = np.array(x); fn = np.array(fd); lo = LN * (s % (T // LN))
        for a in range(N):
            for g in range(8):
                le = np.arange(lo, lo + LN); le = le[win[a, g, le]]
                v = ln[a, g, le]; xn[a, g, 15, v] = np.maximum(x[a, g, 15, v] - 1, 0)
                v, i = np.unique(wn[a, g, le], return_index=True); t = le[i]
                xn[a, g][:15, v] = (x[a, g][:15, v] + z[a, g][:15, t]) >> 1; xn[a, g][15, v] = np.minimum(x[a, g][15, v] + 2, 15)
                le = le[cw[a, g, le]]; c, i = np.unique(col[a, g, le], return_index=True); t = le[i]
                fn[a, g][slow[a, g, t], c] = wn[a, g, t]
        z = np.abs(z - np.where(win[:, :, None, :], xw, top)); z[:, :, 15] = 0
        q = np.where(win, wn, q); none = T - np.sum(win.astype(np.int64), axis=2, keepdims=True); x, fd = xn, fn
        if s < RO - 1:
            z2, q2 = np.zeros_like(z), np.zeros_like(q)
            for a in range(N):
                for b in range(NB):
                    to = (a + 1 + b + s) % N; z2[to, :, :, b * BL:(b + 1) * BL] = z[a, :, :, b * BL:(b + 1) * BL]; q2[to, :, b * BL:(b + 1) * BL] = q[a, :, b * BL:(b + 1) * BL]
            z, q = z2, q2
    return {"yx": x.reshape(N, 128, W).astype(np.float32).astype(BF), "yf": fd.reshape(N, 128, FC).astype(np.float32), "yz": z.reshape(N, 128, T).astype(np.float32).astype(BF), "yq": q.astype(np.float32)}

@@ -1,0 +1,748 @@
+import numpy as np
+from concourse.mybir import AluOpType, ActivationFunctionType
+
+A = AluOpType
+F = ActivationFunctionType
+NR, W, RO = 4, 4096, 3
+UNITS = [[(0, 1), (2,), (3,)], [(1, 0), (2,), (3,)], [(2,), (0, 1), (3,)]]
+VSH = [[128, 32, 0], [128, 0, 32], [32, 128, 0]]
+ZG = [False, True, True]
+GCH = 32
+GS = 32
+SPLIT = SPLIT2 = SPLIT3 = [(0, 12)]
+BIG = float(2 ** 26)
+
+SCRATCH = {}
+SEMAPHORES = ["cV", "cS", "cP", "cG", "ls"]
+OPS = []
+SEEDS = (1, 12, 8000)
+GUESS = [(1.04, 1.56, 3.8, 0.55, 100.0, 1.0), (0.9, 1.1, 2.0, 0.45, 60.0, 0.8), (1.2, 2.0, 5.5, 0.6, 150.0, 1.3),
+         (1.04, 1.3, 3.8, 0.9, 150.0, 1.0)]
+
+
+def buf(name, cols, dtype, where="sbuf"):
+    SCRATCH[name] = (where, [128, cols], dtype)
+
+
+for _n, _c, _d in [
+        ("X0", 4160, "bfloat16"), ("X1", 4160, "bfloat16"), ("fwi", 1024, "int32"), ("FW", 1088, "float32"),
+        ("swi", 512, "int32"), ("SP", 512, "float32"), ("awi", 512, "int32"), ("RT0", 512, "int32"), ("RT", 512, "int32"),
+        ("zin", 256, "bfloat16"), ("hwi", 1, "int32"), ("thi", 8, "int32"), ("qi", 256, "int32"), ("qf", 256, "float32"),
+        ("Z0", 256, "bfloat16"), ("Z1", 256, "bfloat16"), ("Z2", 256, "bfloat16"),
+        ("Q0", 256, "float32"), ("Q1", 256, "float32"), ("Q2", 256, "float32"),
+        ("ZN0", 256, "bfloat16"), ("ZN1", 256, "bfloat16"), ("ZN2", 256, "bfloat16"),
+        ("QN0", 256, "float32"), ("QN1", 256, "float32"), ("QN2", 256, "float32"), ("YQ", 256, "float32"),
+        ("B", 256 * 48, "bfloat16"), ("RS", 4096, "bfloat16"), ("RC", 4096, "bfloat16"), ("RL", 4096, "bfloat16"),
+        ("ZR", 4096, "bfloat16"), ("IOT", 4160, "float32"),
+        ("UI", 16, "int32"), ("I3I", 48, "int32"), ("O3", 48, "uint16"), ("N1", 512, "int32"), ("PP", 256, "float32"),
+        ("AP1", 256, "float32"), ("NM", 512, "int32"), ("ON", 512, "uint16"), ("SC", 4 * 384, "float32"),
+        ("KM", 4 * 8, "float32"), ("KI", 4 * 24, "int32"), ("KC6", 4 * 24, "int32"), ("K64", 8, "int32"),
+        ("ZA", 528, "bfloat16"), ("ZJ", 144, "bfloat16"), ("NW", 4 * 8, "bfloat16"),
+        ("OW", 4 * 24, "uint16"), ("OL", 24, "uint16"), ("MN", 512, "float32"), ("ML", 128, "float32"),
+        ("LM", 64, "float32"), ("WB", 64, "float32"), ("SC2", 128, "float32"), ("E12", 12, "float32"),
+        ("V12", 12, "float32"), ("E13", 12, "float32"), ("VP", 12, "float32"), ("OV", 12, "uint16"), ("NB", 12, "float32"),
+        ("U", 192, "float32"), ("DD", 768, "bfloat16"), ("DS", 768, "bfloat16"), ("KP", 12, "float32"),
+        ("E14", 12, "float32"), ("VQ", 12, "float32"), ("OK0", 12, "uint16"), ("OK1", 12, "uint16"), ("OK2", 12, "uint16"),
+        ("T1", 64, "float32"), ("T2", 64, "int32"), ("T3", 64, "int32"), ("XW0", 64, "bfloat16"), ("XW1", 64, "bfloat16"),
+        ("XW2", 64, "bfloat16"), ("XL0", 64, "bfloat16"), ("XL1", 64, "bfloat16"), ("XL2", 64, "bfloat16"),
+        ("F1", 64, "float32"), ("F2", 64, "float32"), ("LIM", 24, "float32"), ("TH4", 8, "float32"),
+        ("ONE", 384, "bfloat16"), ("ONF", 128, "float32"), ("O4K", 128, "bfloat16"), ("I3", 384, "bfloat16"),
+        ("I3H", 192, "bfloat16"), ("NI", 128, "bfloat16"), ("I32", 128, "float32"), ("PI", 3, "int32"), ("CF", 16, "float32"),
+        ("I48", 768, "bfloat16"), ("OH", 928, "bfloat16"), ("G8", 8, "float32"), ("WS", 24, "bfloat16"), ("WR", 8, "bfloat16"),
+        ("IG", 128, "float32"), ("GB", 128, "float32"), ("G8T", 128, "float32"), ("IM", 128, "float32"), ("MO", 128, "float32"),
+        ("CW8", 48, "float32"), ("CW4", 24, "float32"), ("TW", 12, "float32"), ("DUM", 12, "float32"), ("D12", 12, "float32"),
+        ("TF", 192, "float32"), ("HZ", 144, "bfloat16"), ("KC32", 256, "bfloat16"),
+        ("KC48", 384, "bfloat16"), ("MK", 1024, "bfloat16"), ("M16", 384, "bfloat16"), ("M32", 256, "bfloat16"),
+        ("M64", 768, "bfloat16"), ("ZT", 512, "bfloat16"), ("EX", 2048, "bfloat16"), ("ZS", 1024, "bfloat16")]:
+    buf(_n, _c, _d)
+for _n in ["pH", "pK0", "pK1", "pW", "pQ", "pD0", "pD1", "pD2"]:
+    buf(_n, 512, "float32", "psum")
+
+
+def ap(name, a=0, b=None, step=1, p0=0, p1=128):
+    return (name, a, SCRATCH[name][1][1] if b is None else b, step, p0, p1)
+
+
+def ind(win, off):
+    return ("IND", win, off)
+
+
+def cnt(x):
+    return 16 * cnt(x[2]) if x[0] == "IND" else (x[2] - x[1] + x[3] - 1) // x[3]
+
+
+def wid(x):
+    return 2 if SCRATCH[x[0]][2] in ("bfloat16", "uint16") else 4
+
+
+def real(T, x):
+    if not isinstance(x, tuple):
+        return x
+    if x[0] == "IND":
+        return real(T, x[1]).indirect(real(T, x[2]))
+    if x[3] == 1:
+        return T[x[0]][x[4]:x[5], x[1]:x[2]]
+    return T[x[0]][x[4]:x[5], x[1]:x[2]:x[3]]
+
+
+def add(eng, cost, outs, ins, fn, sem=None, val=0, after=(), lat=0.0):
+    rd, wr = [], []
+    for x in ins:
+        if isinstance(x, tuple):
+            rd.extend([x[1], x[2]] if x[0] == "IND" else [x])
+    for x in outs:
+        if x[0] == "IND":
+            wr.append(x[1])
+            rd.append(x[2])
+        else:
+            wr.append(x)
+    OPS.append({"eng": eng, "c": cost, "rd": rd, "wr": wr, "fn": fn, "sem": sem, "val": val, "after": list(after), "lat": lat})
+    return len(OPS) - 1
+
+
+def vcost(out, ins, two=False):
+    if out[0] == "IND":
+        return (50, 0, 0, cnt(out), 0)
+    if ins[0][0] == "IND":
+        return (50, 0, cnt(out), 0, 0)
+    r = 2.0 if two else (0.5 if all(wid(x) == 2 for x in [out] + ins) else 1.0)
+    return (10, max(64, cnt(out) * r), 0, 0, 0)
+
+
+def tt(out, a, b, op):
+    two = a[0] != "IND" and SCRATCH[a[0]][0] == "sbuf" and SCRATCH[b[0]][0] == "sbuf"
+    c = vcost(out, [a, b], two) if (two or a[0] == "IND" or out[0] == "IND") else (10, max(64, cnt(out)), 0, 0, 0)
+    return add("V", c, [out], [a, b], lambda g, T, r: [g.vector.tensor_tensor(real(T, out), real(T, a), real(T, b), op)])
+
+
+def ts(out, a, s1, op0, s2=None, op1=None):
+    def fn(g, T, r):
+        if op1 is None:
+            return [g.vector.tensor_scalar(real(T, out), real(T, a), real(T, s1), None, op0)]
+        return [g.vector.tensor_scalar(real(T, out), real(T, a), real(T, s1), real(T, s2), op0, op1)]
+    return add("V", vcost(out, [a]), [out], [a, s1, s2], fn)
+
+
+def cp(out, a):
+    return add("V", vcost(out, [a]), [out], [a], lambda g, T, r: [g.vector.tensor_copy(real(T, out), real(T, a))])
+
+
+def ms(out, v):
+    return add("V", vcost(out, [out]), [out], [], lambda g, T, r: [g.vector.memset(real(T, out), v)])
+
+
+def scan(out, d0, d1, init, op0, op1):
+    return add("V", vcost(out, [d0, d1]), [out], [d0, d1],
+               lambda g, T, r: [g.vector.tensor_tensor_scan(real(T, out), real(T, d0), real(T, d1), init, op0, op1)])
+
+
+def act(out, a, func, bias=0.0, scale=1.0):
+    c = (65, 0, cnt(out), 0, 0) if a[0] == "IND" else (50, max(64, cnt(out)), 0, 0, 0)
+    return add("S", c, [out], [a, bias, scale],
+               lambda g, T, r: [g.scalar.activation(real(T, out), real(T, a), func, bias=real(T, bias), scale=real(T, scale))])
+
+
+def lin(out, a, scale, bias=0.0):
+    return act(out, a, F.Identity, bias=bias, scale=scale)
+
+
+def fill(out, v):
+    return lin(out, ap("ONE", 0, cnt(out)), v)
+
+
+def mm(lst):
+    return mmp(lst, True, True)
+
+
+def mmp(lst, first, last):
+    c = sum(max(min(64, cnt(l)), cnt(rh)) * (4 if wid(l) == 4 else 1) for o, l, rh in lst)
+    ins = [x for o, l, rh in lst for x in (l, rh)]
+    return add("P", (30, 0, 0, 0, c), [lst[0][0]], ins, lambda g, T, r: [
+        g.tensor.matmul(real(T, o), real(T, l), real(T, rh), first and i == 0, last and i == len(lst) - 1)
+        for i, (o, l, rh) in enumerate(lst)])
+
+
+def iota(out, pat, base=0, cm=0):
+    fl = SCRATCH[out[0]][2] != "int32"
+    def fn(g, T, r):
+        if fl:
+            return [g.iota(real(T, out), pat, base, cm, allow_small_or_imprecise_dtypes=True)]
+        return [g.iota(real(T, out), pat, base, cm)]
+    return add("G", (130, 2 * cnt(out), 0, 0, 0), [out], [], fn)
+
+
+def asel(out, a, pat, op, fill, base, cm):
+    return add("G", (170, 2 * cnt(out), 0, 0, 0), [out], [a],
+               lambda g, T, r: [g.affine_select(real(T, out), real(T, a), pat, op, fill, base, cm)])
+
+
+def dma(q, outs, ins, fn, nbytes, after=()):
+    sem = "d%d" % len(SEMAPHORES)
+    SEMAPHORES.append(sem)
+    qq = (lambda g: g.sync) if q == "Y" else (lambda g: g.scalar)
+    def f2(g, T, r):
+        o, i = fn(T)
+        qq(g).dma_start(o, i).then_inc(T.sem[sem], 16)
+        return []
+    return add(q, (60, 0, 0, 0, 0), outs, ins, f2, sem=sem, val=16, after=after, lat=2000 + nbytes / 180.0)
+
+
+def send(src, dst, hop):
+    sem = "a%d" % len(SEMAPHORES)
+    SEMAPHORES.append(sem)
+    def fn(g, T, r):
+        to = T.cores[(r["rank"] + hop) % NR]
+        rid, pid, se = r["topo"].addr(to)
+        m = r["topo"].mask(r["core"], to)
+        g.remote_dma(real(T, dst), real(T, src), T.sem[sem], T.sem["ls"], pid, rid, m)
+        r["ls"] += len(r["topo"].engines(r["core"], to))
+        return []
+    i = add("G", (600, 0, 0, 0, 0), [], [src], fn)
+    return add("R", (0, 0, 0, 0, 0), [dst], [], None, sem=sem, val=("eng", hop), after=[i], lat=2500)
+
+
+def col(i, p0=0, p1=128):
+    return ap("CF", i, i + 1, 1, p0, p1)
+
+
+PM3, PM31, PM66, PM, PG, C15, ZSC, VS, VB, VMIN, IS15, WCOL, PM48, HWF, PF, NWC = range(16)
+
+
+def setup():
+    dma("Y", [ap("zin")], [], lambda T: (T.zin[:], T.z0[:]), 65536)
+    dma("Y", [ap("hwi")], [], lambda T: (T.hwi[:], T.hw[:]), 512)
+    dma("S", [ap("awi")], [], lambda T: (T.awi[:], T.aw[:]), 262144)
+    dma("S", [ap("swi")], [], lambda T: (T.swi[:], T.sw[:]), 262144)
+    dma("Y", [ap("fwi")], [], lambda T: (T.fwi[:], T.fw[:]), 524288)
+    dma("S", [ap("qi")], [], lambda T: (T.qi[0:8, :], T.q0[:]), 8192)
+    dma("S", [ap("thi")], [], lambda T: (T.thi[0:1, :], T.th[:]), 32)
+    x0 = dma("Y", [ap("X0", 0, W)], [], lambda T: (T.X0[:, 0:W], T.lx[:]), 1.5 * 2 ** 20)
+    dma("Y", [ap("X1", 0, W)], [], lambda T: (T.X1[:, 0:W], T.lx[:]), 2 ** 20, after=[x0])
+    iota(ap("PI", 0, 1), [[0, 1]], 0, 1)
+    iota(ap("IOT", 0, 128), [[1, 128]])
+    ms(ap("ONE"), 1.0)
+    ts(ap("PI", 1, 2), ap("PI", 0, 1), 15, A.bitwise_and)
+    ts(ap("PI", 2, 3), ap("PI", 0, 1), 4, A.logical_shift_right)
+    cp(col(PM), ap("PI", 1, 2))
+    cp(col(PG), ap("PI", 2, 3))
+    cp(col(PF), ap("PI", 0, 1))
+    ts(col(IS15), col(PM), 15.0, A.is_equal)
+    lin(col(C15), col(IS15), 15.0)
+    ts(ap("G8"), ap("IOT", 0, 8), col(PG), A.is_equal)
+    ms(ap("HZ"), 0.0)
+    cp(col(HWF), ap("hwi"))
+    ts(ap("HZ", 15, 143, 16), ap("G8"), col(HWF), A.mult)
+    first = [h for u in UNITS[0] for h in u]
+    for a, q, k, b in runs(first, 0, [0, 1, 2, 3]):
+        ts(ap("Z0", 64 * a, 64 * (a + k)), ap("zin", 64 * q, 64 * (q + k)), col(C15), A.add)
+    cp(ap("FW", 0, 1024), ap("fwi"))
+    ts(ap("SP"), ap("swi"), 2048.0, A.subtract)
+    ts(ap("RT0"), ap("awi"), 3232.0, A.mult, 65536.0, A.add)
+    ts(ap("RT"), ap("RT0"), 131071, A.bitwise_and)
+    iota(ap("IG"), [[1, 8], [0, 16]])
+    iota(ap("IM"), [[0, 8], [1, 16]])
+    asel(ap("I3"), ap("ONE"), [[0, 3], [-1, 128]], A.is_equal, 0.0, 0, 1)
+    lin(ap("NI"), ap("I3", 0, 128), -1.0)
+    for i in range(16):
+        lin(ap("EX", i, 2048, 16), ap("I3", 0, 128), 1.0)
+    ts(ap("G8T", 0, 128, 1, 0, 8), ap("IG", 0, 128, 1, 0, 8), col(PF, 0, 8), A.is_equal)
+    ts(ap("GB"), ap("IM"), col(PM), A.not_equal, 8192.0, A.mult)
+    lin(ap("MO"), ap("GB"), 1.0, -4096.0)
+    cp(ap("qf", 0, 256, 1, 0, 8), ap("qi", 0, 256, 1, 0, 8))
+    mm([(ap("pQ", 0, 256), ap("G8T", 0, 128, 1, 0, 8), ap("qf", 0, 256, 1, 0, 8))])
+    for a, q, k, b in runs(first, 0, [0, 1, 2, 3]):
+        tt(ap("Q0", 64 * a, 64 * (a + k)), ap("pQ", 64 * q, 64 * (q + k)), ap("MO", 0, 64 * k), A.subtract)
+    ts(ap("GB"), ap("IG"), col(PG), A.is_equal)
+    for i, m, a in [(PM3, 3.0, 0.0), (PM31, 3.0, 1.0), (PM66, 3.0, 66.0), (PM48, 48.0, 0.0)]:
+        lin(col(i), col(PM), m, a)
+    for i, m, a in [(ZSC, -1.0, 1.0), (VS, 1.0, 1.0), (VB, -26.0, 0.0), (VMIN, -240.0, 255.0), (WCOL, 61440.0, 4096.0),
+                    (NWC, -61440.0, -4096.0)]:
+        lin(col(i), col(IS15), m, a)
+    fill(ap("WS", 1, 24, 3), 0.0)
+    lin(ap("WS", 0, 24, 3), ap("G8"), col(WCOL))
+    lin(ap("WS", 2, 24, 3), ap("G8"), col(NWC))
+    lin(ap("WR"), ap("G8"), 8192.0)
+    ms(ap("MK", 0, 16 * GCH), 0.0)
+    fill(ap("MK", 0, 16 * GCH, 16), -32768.0)
+    nz = max([0] + [v for s in range(RO) for v in VSH[s] if v <= 64 and not ZG[s]])
+    if nz:
+        ms(ap("ZS", 0, 16 * nz), 0.0)
+    for n, st in (("M16", 16), ("M32", 32), ("M64", 64)):
+        ms(ap(n), 0.0)
+        fill(ap(n, 0, None, st), BIG)
+    iota(ap("KC48", 0, None, 1, 0, 1), [[0, 8], [65, 3], [3, 16]])
+    iota(ap("KC32", 0, None, 1, 0, 1), [[0, 8], [65, 2], [3, 16]])
+    iota(ap("I48"), [[0, 16], [1, 48]])
+    ts(ap("OH", 0, 768), ap("I48"), col(PM3), A.is_equal)
+    ts(ap("OH", 47, 768, 48), ap("IOT", 0, 16), col(PM), A.is_equal)
+    ts(ap("OH", 768, 816), ap("IOT", 0, 48), col(PM31), A.is_equal)
+    ts(ap("OH", 816, 928), ap("IOT", 0, 112), col(PM66), A.not_equal)
+    lin(ap("I32"), ap("I3", 0, 128), 1.0)
+    ms(ap("ZA"), 0.0)
+    fill(ap("ZJ"), 0.0)
+    sizes = set(len(u) for us in UNITS for u in us)
+    for n, m in (("CW8", 8), ("CW4", 4)):
+        if m // 4 in sizes:
+            fill(ap(n), 768.0)
+            fill(ap(n, 5 * m, 6 * m), 816.0)
+            lin(ap(n, 0, m), ap("IOT", 0, m), 768.0, col(PM48))
+            for k in (1, 3):
+                lin(ap(n, k * m, k * m + m), ap("IOT", 0, m), 0.0, col(PM48))
+    if 1 in sizes:
+        asel(ap("I3H"), ap("ONE", 0, 192), [[0, 3], [-1, 64]], A.is_equal, 0.0, 0, 1)
+    fill(ap("ONF"), 1.0)
+    fill(ap("O4K"), 4096.0)
+    ts(ap("TH4", 0, 8, 1, 0, 1), ap("thi", 0, 8, 1, 0, 1), 4096.0, A.mult)
+    for k in range(3):
+        lin(ap("TW", 4 * k, 4 * k + 4), ap("IOT", 0, 4), 16.0, col(PM))
+        lin(ap("TF", 64 * k, 64 * k + 64), ap("IOT", 0, 64), 1.0 / 128)
+    lin(ap("DUM", 0, 8), ap("TW", 0, 8), 1.0, 4096.0)
+    lin(ap("D12", 0, 8), ap("TW", 0, 8), 1.0, 8192.0)
+    for n in ("DUM", "D12"):
+        lin(ap(n, 8, 12), ap("TW", 8, 12), 1.0, 1024.0)
+    fill(ap("X0", W, W + 64), 0.0)
+    fill(ap("X1", W, W + 64), 0.0)
+    fill(ap("FW", 1024, 1088), 0.0)
+    for k in range(4):
+        iota(ap("IOT", 128 + 1008 * k, 1136 + 1008 * k), [[1, 1008]], 128 + 1008 * k)
+
+
+def limit(s):
+    lst = [(ap("pW", 256, 264), ap("ONF", 0, 128, 1, 0, 1), ap("TH4", 0, 8, 1, 0, 1))]
+    if s > 0:
+        p = 0
+        for u in UNITS[s - 1]:
+            n = 64 * len(u)
+            lst.append((ap("pW", 256, 264), ap("O4K", 0, 128, 1, 0, n), ap("NW", 8 * p, 8 * p + 8, 1, 0, n)))
+            p += len(u)
+    mm(lst)
+    ts(ap("LIM", 8 * s, 8 * s + 8), ap("pW", 256, 264), 4090.0 * 4096, A.min, 81.0, A.subtract)
+
+
+def front(s, p, n, nv):
+    t0, m = 64 * p, n // 16
+    Z, Q = "Z%d" % s, "Q%d" % s
+    mm([(ap("pH", 0, m), ap("HZ", 15 - r, 143 - r), ap(Z, t0 + r, t0 + n, 16)) for r in range(16)])
+    ui = ap("UI", 4 * p, 4 * p + m)
+    cp(ui, ap("pH", 0, m))
+    o = 12 * p
+    ts(ap("I3I", o, o + m), ui, 2, A.logical_shift_right, 1023, A.bitwise_and)
+    ts(ap("I3I", o + m, o + 2 * m), ui, 511, A.bitwise_and)
+    ts(ap("I3I", o + 2 * m, o + 3 * m), ui, 3, A.logical_shift_right, 511, A.bitwise_and)
+    cp(ap("O3", o, o + 3 * m), ap("I3I", o, o + 3 * m))
+    ok, os_, oa = [ap("O3", o + k * m, o + k * m + m) for k in range(3)]
+    a, b, c = 2 * t0, 2 * t0 + n, 2 * t0 + 2 * n
+    tt(ap("N1", a, b), ind(ap("FW" if s else "fwi", 0, 1024), ok), ap(Q, t0, t0 + n), A.max)
+    ts(ap("NM", a, b), ap("N1", a, b), 4095, A.bitwise_and)
+    cp(ap("ON", a, b), ap("NM", a, b))
+    ts(ap("PP", t0, t0 + n), ind(ap("awi"), oa), 32.0, A.add)
+    tt(ap("AP1", t0, t0 + n), ind(ap("SP"), os_), ap("PP", t0, t0 + n), A.mult)
+    tt(ap("N1", b, c), ind(ap("RT"), oa), ap("AP1", t0, t0 + n), A.add)
+    ts(ap("NM", b, c), ap("N1", b, c), 5, A.arith_shift_right, 4095, A.bitwise_and)
+    cp(ap("ON", b, c), ap("NM", b, c))
+    zt = ap("pH", 128, 256, 1, 0, n)
+    mm([(zt, ap(Z, t0, t0 + n), ap("NI"))])
+    act(ap("ZT", 2 * t0, 2 * t0 + 128, 1, 0, n), zt, F.Identity)
+    v0, v1 = t0 + n - nv, t0 + n
+    if nv and ZG[s]:
+        for i in range(16):
+            asel(ap("ZR", 16 * v0 + i, 16 * v1, 16), ap(Z, v0, v1), [[0, nv]], A.is_ge, 0.0, 0, 0)
+    elif nv > 64:
+        for i in range(16):
+            cp(ap("ZR", 16 * v0 + i, 16 * v1, 16), ap(Z, v0, v1))
+    elif nv:
+        cp(ap("ZS", 0, 16 * nv, 16), ap(Z, v0, v1))
+        for a in range(0, nv, 32):
+            scan(ap("ZR", 16 * (v0 + a), 16 * (v0 + a + 32)), ap("MK", 0, 512), ap("ZS", 16 * a, 16 * a + 512), 0.0, A.add, A.max)
+
+
+DB = [0]
+
+
+def bulk(s, p, n, nv):
+    t0 = 64 * p
+    X = ap("X%d" % (s % 2))
+    ns = n - nv
+    so, co = 2 * t0, 2 * t0 + n
+    Z = "Z%d" % s
+
+    def lane(k, a, b):
+        return ap("B", 48 * (t0 + a) + k, 48 * (t0 + b), 3)
+
+    def flat(name, a, b):
+        return ap(name, 16 * (t0 + a), 16 * (t0 + b))
+
+    def viapsum(raw, k, func, a, b):
+        for x in range(a, b, 32):
+            y = min(b, x + 32)
+            d = ap("pD%d" % (DB[0] % 3), 0, 16 * (y - x))
+            DB[0] += 1
+            mm([(d, ap("ZT", 2 * t0, 2 * t0 + 128, 1, 0, n), ap("EX", 16 * x, 16 * y, 1, 0, n)), (d, ap("I3", 0, 128), flat(raw, x, y))])
+            act(lane(k, x, y), d, func)
+
+    for a in range(0, ns, GS):
+        b = min(ns, a + GS)
+        act(flat("RC", a, b), ind(X, ap("ON", co + a, co + b)), F.Identity)
+        viapsum("RC", 1, F.Abs, a, b)
+    for a in range(0, ns, GCH):
+        b = min(ns, a + GCH)
+        scan(lane(2, a, b), ap("MK", 0, 16 * (b - a)), flat("RC", a, b), 0.0, A.add, A.max)
+    if ns:
+        top = ap("B", 48 * t0 + 47, 48 * (t0 + ns), 48)
+        tt(top, top, ap(Z, t0, t0 + ns), A.subtract)
+    for a in range(0, n, GS):
+        b = min(n, a + GS)
+        act(flat("RS", a, b), ind(X, ap("ON", so + a, so + b)), F.Identity)
+        viapsum("RS", 0, F.Abs, a, b)
+    for a in range(ns, n, GCH):
+        b = min(n, a + GCH)
+        tt(lane(1, a, b), ind(X, ap("ON", co + a, co + b)), flat("ZR", a, b), A.subtract)
+        ts(flat("RL", a, b), lane(1, a, b), 0.0, A.max)
+        scan(lane(2, a, b), ap("MK", 0, 16 * (b - a)), lane(1, a, b), 0.0, A.add, A.max)
+
+
+def spread(out, zname, z0, rhs, n, w):
+    return [(out, ap(zname, z0 + 15 - r, z0 + 143 - r, 1, 0, n), ap(rhs, r, w * n, 16, 0, n)) for r in range(16)]
+
+
+def tail(s, p, n, nv, ui, lo):
+    t0, m, ns = 64 * p, n // 16, n - nv
+    K = "pK%d" % (ui % 2)
+    L = 32 if lo is None else 48
+    def sl(name, a, b, st=1):
+        return ap(name, a, b, st, 0, n)
+    bl = lambda k, i, a=0, b=n: ap("B", 48 * (t0 + a) + 3 * i + k, 48 * (t0 + b), 48)
+    mmp([(sl(K, 0, 8 * L), ap("ONE", 0, n, 1, 0, 1), ap("KC%d" % L, 0, None, 1, 0, 1))], True, False)
+    if ns:
+        mmp([(ap(K, 16 + i, 8 * L, L, 0, ns), bl(1, i, 0, ns), ap("WS", 0, 24, 3)) for i in range(16)], False, False)
+    if nv:
+        mmp([(ap(K, 16 + i, 8 * L, L, ns, n), bl(1, i, ns, n), ap("WS", 2, 24, 3)) for i in range(16)]
+            + [(ap(K, 16 + i, 8 * L, L, ns, n), ap("RL", 16 * (t0 + ns) + i, 16 * (t0 + n), 16), ap("WR")) for i in range(16)], False, False)
+    if lo is None:
+        mmp([(sl(K, i, 256, 32), bl(0, i), ap("WS", 0, 24, 3)) for i in range(16)], False, True)
+    else:
+        mmp([(sl(K, i, 384, 16), bl(0, i), ap("WS")) for i in range(16)], False, True)
+    c0 = 384 * p
+    scan(sl("SC", c0, c0 + 8 * L), sl("M32" if lo is None else "M16", 0, 8 * L), sl(K, 0, 8 * L), 0.0, A.add, A.min)
+    k0 = 24 * p
+    lim = sl("LIM", 8 * s, 8 * s + 8)
+    if lo is None:
+        tt(sl("KI", k0, k0 + 8), sl("SC", c0 + 31, c0 + 256, 32), lim, A.min)
+    else:
+        ks, kc, kn = [sl("SC", c0 + 15 + 16 * k, c0 + 384, 48) for k in range(3)]
+        tt(sl("KM", 8 * p, 8 * p + 8), ks, kc, A.min)
+        tt(sl("KI", k0, k0 + 8), sl("KM", 8 * p, 8 * p + 8), lim, A.min)
+        tt(sl("KI", k0 + 8, k0 + 16), ks, kc, A.max)
+        cp(sl("KI", k0 + 16, k0 + 24), kn)
+    w = 1 if lo is None else 2
+    ts(sl("KC6", k0, k0 + 16 * w - 8), sl("KI", k0, k0 + 16 * w - 8), 63, A.bitwise_and)
+    z0 = 256 * (ui % 2)
+    cp(sl("ZA", z0 + 15, z0 + 15 + 128 * w, 16), sl("KC6", k0, k0 + 8 * w))
+    cw, i3 = ("CW8", "I3") if n == 128 else ("CW4", "I3H")
+    mm([(ap("pW", 0, 3 * m), ap("I32"), ap(cw, 0, 3 * m))] + spread(ap("pW", 0, 3 * m), "ZA", z0, i3, n, 3))
+    ow = 24 * p
+    cp(ap("OW", ow, ow + 3 * m), ap("pW", 0, 3 * m))
+    if lo is not None:
+        c = lo // 16
+        for k in (0, 1):
+            act(ap("V12", 4 * k, 4 * k + 4), ap("pW", 2 * m + c, 2 * m + c + 4), F.Sign, bias=815.0, scale=-1.0)
+    last = s == RO - 1
+    act(ap("ZN%d" % s, t0, t0 + n), ind(ap("B", 48 * t0, 48 * (t0 + n)), ap("OW", ow, ow + m)), F.Abs,
+        bias=(0.0 if last else col(C15)), scale=col(ZSC))
+    a, b, c_ = 2 * t0, 2 * t0 + n, 2 * t0 + 2 * n
+    tt(ap("MN", a, c_), ind(ap("OH"), ap("OW", ow + m, ow + 3 * m)), ap("NM", a, c_), A.mult)
+    if not last or lo is not None:
+        mm([(ap("pQ", 0, n), ap("GB"), ap("MN", a, b)), (ap("pQ", 0, n), ap("GB"), ap("MN", b, c_))])
+        tt(ap("QN%d" % s, t0, t0 + n), ap("pQ", 0, n), ap("MO", 0, n), A.subtract)
+        if lo is not None:
+            act(ap("WB"), ap("pQ", lo, lo + 64), F.Identity)
+    if last:
+        o = ap("pQ", 256, 256 + n, 1, 0, 8)
+        mm([(o, ap("G8"), ap("MN", a, b)), (o, ap("G8"), ap("MN", b, c_))])
+        act(ap("YQ", t0, t0 + n, 1, 0, 8), o, F.Identity)
+    else:
+        act(sl("NW", 8 * p, 8 * p + 8), sl("ZA", z0 + 15, z0 + 143, 16), F.Relu, bias=-46.0)
+
+
+def learn(s, p, n, ui, lo):
+    t0, m, c = 64 * p, n // 16, lo // 16
+    def sl(name, a, b, st=1):
+        return ap(name, a, b, st, 0, n)
+    c0, k0 = 384 * p, 24 * p
+    ts(sl("K64", 0, 8), sl("KI", k0, k0 + 8), 64, A.bitwise_and)
+    tt(sl("ZJ", 15, 143, 16), sl("KC6", k0 + 16, k0 + 24), sl("K64", 0, 8), A.add)
+    cw, i3 = ("CW8", "I3") if n == 128 else ("CW4", "I3H")
+    mm([(ap("pW", 64, 64 + 3 * m), ap("I32"), ap(cw, 3 * m, 6 * m))] + spread(ap("pW", 64, 64 + 2 * m), "ZA", 256 * (ui % 2) + 128, i3, n, 2)
+       + spread(ap("pW", 64 + 2 * m, 64 + 3 * m), "ZJ", 0, i3, n, 1))
+    cp(ap("OL", 0, 3 * m), ap("pW", 64, 64 + 3 * m))
+    ts(ap("V12", 8, 12), ap("pW", 64 + 2 * m + c, 64 + 2 * m + c + 4), 880.0, A.is_ge)
+    a, b = 2 * t0 + lo, 2 * t0 + n + lo
+    if n == 64:
+        tt(ap("ML"), ind(ap("OH"), ap("OL", 0, 8)), ap("NM", a, a + 128), A.mult)
+    else:
+        tt(ap("ML", 0, 64), ind(ap("OH"), ap("OL", c, c + 4)), ap("NM", a, a + 64), A.mult)
+        tt(ap("ML", 64, 128), ind(ap("OH"), ap("OL", m + c, m + c + 4)), ap("NM", b, b + 64), A.mult)
+    mm([(ap("pQ", 128, 192), ap("GB"), ap("ML", 0, 64)), (ap("pQ", 128, 192), ap("GB"), ap("ML", 64, 128))])
+    tt(ap("LM"), ap("pQ", 128, 192), ap("MO", 0, 64), A.subtract)
+    scan(ap("SC2", 0, 64), ap("MK", 0, 64), ap("QN%d" % s, t0 + lo, t0 + lo + 64), 0.0, A.add, A.max)
+    scan(ap("SC2", 64, 128), ap("MK", 0, 64), ap("LM"), 0.0, A.add, A.max)
+    tt(ap("E12", 8, 12), ap("I3I", 12 * p + c, 12 * p + c + 4), ap("D12", 8, 12), A.subtract)
+    for x, y in SPLIT:
+        if x < 8:
+            z = min(y, 8)
+            tt(ap("E12", x, z), ap("SC2", 16 * x + 15, 16 * z, 16), ap("D12", x, z), A.subtract)
+        tt(ap("E13", x, y), ap("E12", x, y), ap("V12", x, y), A.mult)
+        tt(ap("VP", x, y), ap("E13", x, y), ap("DUM", x, y), A.add)
+        cp(ap("OV", x, y), ap("VP", x, y))
+        lin(ap("NB", x, y), ap("VP", x, y), -128.0)
+        tt(ap("U", 16 * x, 16 * y), ind(ap("IOT"), ap("OV", x, y)), ap("TF", 16 * x, 16 * y), A.add)
+        for k in range(x, y):
+            act(ap("DD", 64 * k, 64 * k + 64), ap("U", 64 * (k // 4), 64 * (k // 4) + 64), F.Abs, bias=ap("NB", k, k + 1), scale=128.0)
+    for x, y in SPLIT2:
+        scan(ap("DS", 64 * x, 64 * y), ap("M64", 64 * x, 64 * y), ap("DD", 64 * x, 64 * y), 0.0, A.add, A.min)
+    for x, y in SPLIT3:
+        tt(ap("KP", x, y), ap("DS", 64 * x + 63, 64 * y, 64), ap("TW", x, y), A.is_equal)
+        tt(ap("E14", x, y), ap("E13", x, y), ap("KP", x, y), A.mult)
+        tt(ap("VQ", x, y), ap("E14", x, y), ap("DUM", x, y), A.add)
+        cp(ap("OK%d" % s, x, y), ap("VQ", x, y))
+    X = ap("X%d" % (s % 2))
+    tt(ap("T1"), ind(X, ap("OV", 0, 4)), ap("Z%d" % s, t0 + lo, t0 + lo + 64), A.add)
+    ts(ap("T2"), ap("T1"), col(VS), A.mult, col(VB), A.add)
+    ts(ap("T3"), ap("T2"), 1, A.arith_shift_right)
+    ts(ap("XW%d" % s), ap("T3"), col(VMIN), A.min)
+    ts(ap("XL%d" % s), ind(X, ap("OV", 4, 8)), col(IS15), A.subtract, 0.0, A.max)
+    tt(ap("F1"), ind(ap("FW"), ap("OV", 8, 12)), ap("WB"), A.subtract)
+    tt(ap("F2"), ind(ap("OH"), ap("OL", 2 * m + c, 2 * m + c + 4)), ap("F1"), A.mult)
+    tt(ind(ap("FW"), ap("OK%d" % s, 8, 12)), ap("F2"), ap("WB"), A.add)
+
+
+def update(s, x):
+    cp(ind(ap("X%d" % x), ap("OK%d" % s, 4, 8)), ap("XL%d" % s))
+    cp(ind(ap("X%d" % x), ap("OK%d" % s, 0, 4)), ap("XW%d" % s))
+
+
+def runs(u, p, nxt):
+    out = []
+    for k, h in enumerate(u):
+        q = nxt.index(h)
+        if out and out[-1][3] == h // 2 and out[-1][1] + out[-1][2] == q:
+            out[-1] = (out[-1][0], out[-1][1], out[-1][2] + 1, out[-1][3])
+        else:
+            out.append((p + k, q, 1, h // 2))
+    return out
+
+
+def program():
+    setup()
+    ui = 0
+    for s in range(RO):
+        limit(s)
+        p = 0
+        for u, nv in zip(UNITS[s], VSH[s]):
+            front(s, p, 64 * len(u), nv)
+            p += len(u)
+        p = 0
+        last = s == RO - 1
+        nxt = [0, 1, 2, 3] if last else [h for u in UNITS[s + 1] for h in u]
+        for u, nv in zip(UNITS[s], VSH[s]):
+            n = 64 * len(u)
+            lo = 64 * u.index(s) if s in u else None
+            bulk(s, p, n, nv)
+            tail(s, p, n, nv, ui, lo)
+            for (a, q, k, b) in runs(u, p, nxt):
+                sa, sb, da, db = 64 * a, 64 * (a + k), 64 * q, 64 * (q + k)
+                if last:
+                    dma("Y", [], [ap("ZN2", sa, sb)], lambda T, sa=sa, sb=sb, da=da, db=db: (T.yz[:, da:db], T.ZN2[:, sa:sb]), 32768)
+                    dma("Y", [], [ap("YQ", sa, sb)], lambda T, sa=sa, sb=sb, da=da, db=db: (T.yq[:, da:db], T.YQ[0:8, sa:sb]), 4096)
+                else:
+                    send(ap("ZN%d" % s, sa, sb), ap("Z%d" % (s + 1), da, db), 1 + b + s)
+                    send(ap("QN%d" % s, sa, sb), ap("Q%d" % (s + 1), da, db), 1 + b + s)
+            if lo is not None:
+                learn(s, p, n, ui, lo)
+                update(s, (s + 1) % 2)
+                if last:
+                    dma("Y", [], [ap("X1")], lambda T: (T.yx[:], T.X1[:, 0:W]), 2 ** 20)
+                    dma("Y", [], [ap("FW")], lambda T: (T.yf[:], T.FW[:, 0:1024]), 2 ** 19)
+            p += len(u)
+            ui += 1
+        if not last:
+            update(s, s % 2)
+
+
+def meet(a, b):
+    if a[1] >= b[2] or b[1] >= a[2]:
+        return False
+    s = min(a[3], b[3])
+    if s > 1 and a[3] % s == 0 and b[3] % s == 0 and (a[1] - b[1]) % s:
+        return False
+    return True
+
+
+def depend():
+    hist = {}
+    for i, o in enumerate(OPS):
+        d = set(o["after"])
+        for x, w in [(x, False) for x in o["rd"]] + [(x, True) for x in o["wr"]]:
+            ps = SCRATCH[x[0]][0] == "psum"
+            for (j, y, wj) in hist.get(x[0], []):
+                if j == i:
+                    continue
+                if ps:
+                    if OPS[j]["eng"] != o["eng"] or o["eng"] == "P":
+                        d.add(j)
+                elif (w or wj) and meet(x, y):
+                    d.add(j)
+        for x, w in [(x, False) for x in o["rd"]] + [(x, True) for x in o["wr"]]:
+            hist.setdefault(x[0], []).append((i, x, w))
+        cover = 0
+        for j in d:
+            cover |= OPS[j]["reach"]
+        o["dep"] = sorted(j for j in d if not cover >> j & 1)
+        o["reach"] = 0 if o["eng"] == "R" else cover | sum(1 << j for j in d if not cover >> j & 1)
+
+
+def prices(m):
+    cost = [c[0] + (c[1] + c[2] * m[1] + c[3] * m[2]) * m[0] + c[4] * m[3] for c in [o["c"] for o in OPS]]
+    pred = [[(j, OPS[j]["lat"] * m[5] + (0.0 if "R" in (o["eng"], OPS[j]["eng"]) or o["eng"] + OPS[j]["eng"] == "PP" else m[4]))
+             for j in o["dep"]] for o in OPS]
+    return cost, pred, [o["lat"] * m[5] for o in OPS]
+
+
+def place(seq, cost, pred, rel):
+    t0 = [0.0] * len(OPS)
+    gaps = {}
+    for i in seq:
+        t = rel[i]
+        for j, d in pred[i]:
+            x = t0[j] + cost[j] + d
+            if x > t:
+                t = x
+        e = OPS[i]["eng"]
+        if e != "R":
+            iv = gaps.setdefault(e, [])
+            k = len(iv)
+            while k > 0 and iv[k - 1][1] > t:
+                k -= 1
+            c = cost[i]
+            while k < len(iv) and iv[k][0] < t + c:
+                t = max(t, iv[k][1])
+                k += 1
+            iv.insert(k, (t, t + c))
+        t0[i] = t
+    return t0
+
+
+def replay(order, cost, pred, lat):
+    t0 = [0.0] * len(OPS)
+    free = {}
+    for i in order:
+        e = OPS[i]["eng"]
+        t = free.get(e, 0.0)
+        for j, d in pred[i]:
+            x = t0[j] + cost[j] + d
+            if x > t:
+                t = x
+        t0[i] = t
+        if e != "R":
+            free[e] = t + cost[i]
+    return max(t0[i] + cost[i] + lat[i] for i in order), t0
+
+
+def schedule(seed, rounds, tries=0):
+    n = len(OPS)
+    pr = [prices(m) for m in GUESS]
+    cost, pred, lat = pr[0]
+    succ = [[] for _ in OPS]
+    for i in range(n):
+        for j, d in pred[i]:
+            succ[j].append((i, d))
+    rnd = np.random.RandomState(seed)
+    zero = [0.0] * n
+    best, base = None, None
+    t0 = place(range(n), cost, pred, zero)
+    for k in range(rounds):
+        c2 = [c * (1 + 0.25 * x) for c, x in zip(cost, rnd.rand(n))] if k % 3 == 2 else cost
+        back = place(sorted(range(n), key=lambda i: (-(t0[i] + cost[i]), -i)), c2, succ, lat)
+        t0 = place(sorted(range(n), key=lambda i: (-(back[i] + c2[i]), i)), cost, pred, zero)
+        order = sorted(range(n), key=lambda i: (t0[i], i))
+        ends = [replay(order, *p)[0] for p in pr]
+        base = base or ends
+        score = sum(a / b for a, b in zip(ends, base))
+        if best is None or score < best[0]:
+            best = (score, order, ends, t0)
+        elif k % 3 == 1:
+            t0 = best[3]
+    t0 = replay(best[1], *pr[0])[1]
+    for k in range(tries):
+        a, w, sg = rnd.rand() * best[2][0], [3e3, 8e3, 20e3][rnd.randint(3)], [300.0, 1000.0, 3000.0][rnd.randint(3)]
+        key = [t + z if a < t < a + w else t for t, z in zip(t0, (rnd.randn(n) * sg).tolist())]
+        for i in range(n):
+            for j, d in pred[i]:
+                if key[j] >= key[i]:
+                    key[i] = key[j] + 1e-3
+        m = pr[rnd.randint(len(pr))] if rnd.rand() < 0.3 else pr[0]
+        t1 = place(sorted(range(n), key=lambda i: (key[i], i)), m[0], m[1], zero)
+        order = sorted(range(n), key=lambda i: (t1[i], i))
+        ends = [replay(order, *p)[0] for p in pr]
+        score = sum(a / b for a, b in zip(ends, base))
+        if score < best[0]:
+            best = (score, order, ends)
+            t0 = replay(order, *pr[0])[1]
+    return best[1], best[2]
+
+
+def build():
+    del OPS[:]
+    del SEMAPHORES[5:]
+    DB[0] = 0
+    program()
+    depend()
+    return schedule(*SEEDS)
+
+
+ORDER, EST = build()
+
+
+def rank_program(g, core, T, topo):
+    rank = T.rank_of(core)
+    if rank is None:
+        return
+    r = {"rank": rank, "core": core, "topo": topo, "ls": 0}
+    queue = {"V": g.vector, "S": g.scalar, "P": g.tensor, "G": g, "Y": g.sync}
+    count = {"cV": 0, "cS": 0, "cP": 0, "cG": 0}
+    done = {}
+    seen = {}
+    for i in ORDER:
+        o = OPS[i]
+        e = o["eng"]
+        if e == "R":
+            src = T.cores[(rank - o["val"][1]) % NR]
+            done[i] = (o["sem"], len(topo.engines(src, core)))
+            continue
+        need = {}
+        for j in o["dep"]:
+            if done[j] is None or (e == "P" and OPS[j]["eng"] == "P"):
+                continue
+            need[done[j][0]] = max(need.get(done[j][0], 0), done[j][1])
+        for sem, v in need.items():
+            if seen.get((e, sem), 0) < v:
+                queue[e].wait_ge(T.sem[sem], v)
+                seen[(e, sem)] = v
+        ins = o["fn"](g, T, r)
+        if o["sem"] is not None:
+            done[i] = (o["sem"], o["val"])
+        elif ins:
+            for x in ins:
+                x.then_inc(T.sem["c" + e], 1)
+            count["c" + e] += len(ins)
+            done[i] = ("c" + e, count["c" + e])
+        else:
+            done[i] = None
+    final = dict(count)
+    final["ls"] = r["ls"]
+    for i in ORDER:
+        if OPS[i]["sem"] is not None:
+            final[done[i][0]] = done[i][1]
+    for sem, v in final.items():
+        if v and seen.get(("G", sem), 0) < v:
+            g.wait_ge(T.sem[sem], v)

@@ -5,19 +5,19 @@ A = AluOpType
 F = ActivationFunctionType
 NR, W, RO = 4, 4096, 3
 UNITS = [[(0, 1), (2,), (3,)], [(1, 0), (2,), (3,)], [(2,), (0, 1), (3,)]]
-VSH = [[128, 32, 0], [128, 0, 32], [32, 128, 0]]
-ZG = [False, True, True]
+VSH = [[128, 0, 32], [128, 0, 32], [0, 128, 0]]
+ZG = [False, False, False]
 GCH = 32
 GS = 32
-SPLIT = SPLIT2 = SPLIT3 = [(0, 12)]
 BIG = float(2 ** 26)
 
 SCRATCH = {}
 SEMAPHORES = ["cV", "cS", "cP", "cG", "ls"]
 OPS = []
-SEEDS = (1, 12, 8000)
-GUESS = [(1.04, 1.56, 3.8, 0.55, 100.0, 1.0), (0.9, 1.1, 2.0, 0.45, 60.0, 0.8), (1.2, 2.0, 5.5, 0.6, 150.0, 1.3),
-         (1.04, 1.3, 3.8, 0.9, 150.0, 1.0)]
+SEEDS = (1, 9, 7000)
+GUESS = [(0.9, 1.56, 3.8, 0.46, 130.0, 0.9, 10.0, 1.6), (0.83, 1.3, 3.0, 0.42, 200.0, 0.7, 0.0, 1.2),
+         (0.83, 1.4, 3.0, 0.42, 80.0, 1.0, 30.0, 1.2), (1.2, 1.9, 5.0, 0.6, 150.0, 1.1, 20.0, 1.8),
+         (0.83, 1.56, 3.8, 0.42, 80.0, 0.8, 0.0, 2.0)]
 
 
 def buf(name, cols, dtype, where="sbuf"):
@@ -39,10 +39,10 @@ for _n, _c, _d in [
         ("KM", 4 * 8, "float32"), ("KI", 4 * 24, "int32"), ("KC6", 4 * 24, "int32"), ("K64", 8, "int32"),
         ("ZA", 528, "bfloat16"), ("ZJ", 144, "bfloat16"), ("NW", 4 * 8, "bfloat16"),
         ("OW", 4 * 24, "uint16"), ("OL", 24, "uint16"), ("MN", 512, "float32"), ("ML", 128, "float32"),
-        ("LM", 64, "float32"), ("WB", 64, "float32"), ("SC2", 128, "float32"), ("E12", 12, "float32"),
-        ("V12", 12, "float32"), ("E13", 12, "float32"), ("VP", 12, "float32"), ("OV", 12, "uint16"), ("NB", 12, "float32"),
+        ("LM", 128, "float32"), ("WB", 64, "float32"), ("SC2", 128, "float32"), ("DN", 12, "float32"),
+        ("V12", 12, "float32"), ("VT", 12, "float32"), ("VP", 12, "float32"), ("OV", 12, "uint16"), ("NB", 12, "float32"),
         ("U", 192, "float32"), ("DD", 768, "bfloat16"), ("DS", 768, "bfloat16"), ("KP", 12, "float32"),
-        ("E14", 12, "float32"), ("VQ", 12, "float32"), ("OK0", 12, "uint16"), ("OK1", 12, "uint16"), ("OK2", 12, "uint16"),
+        ("M0", 64, "float32"), ("VQ", 12, "float32"), ("OK0", 12, "uint16"), ("OK1", 12, "uint16"), ("OK2", 12, "uint16"),
         ("T1", 64, "float32"), ("T2", 64, "int32"), ("T3", 64, "int32"), ("XW0", 64, "bfloat16"), ("XW1", 64, "bfloat16"),
         ("XW2", 64, "bfloat16"), ("XL0", 64, "bfloat16"), ("XL1", 64, "bfloat16"), ("XL2", 64, "bfloat16"),
         ("F1", 64, "float32"), ("F2", 64, "float32"), ("LIM", 24, "float32"), ("TH4", 8, "float32"),
@@ -50,7 +50,8 @@ for _n, _c, _d in [
         ("I3H", 192, "bfloat16"), ("NI", 128, "bfloat16"), ("I32", 128, "float32"), ("PI", 3, "int32"), ("CF", 16, "float32"),
         ("I48", 768, "bfloat16"), ("OH", 928, "bfloat16"), ("G8", 8, "float32"), ("WS", 24, "bfloat16"), ("WR", 8, "bfloat16"),
         ("IG", 128, "float32"), ("GB", 128, "float32"), ("G8T", 128, "float32"), ("IM", 128, "float32"), ("MO", 128, "float32"),
-        ("CW8", 48, "float32"), ("CW4", 24, "float32"), ("TW", 12, "float32"), ("DUM", 12, "float32"), ("D12", 12, "float32"),
+        ("CW8", 24, "float32"), ("CW4", 12, "float32"), ("TW", 12, "float32"), ("DUM", 12, "float32"),
+        ("CW8L", 24, "bfloat16"), ("CW4L", 12, "bfloat16"),
         ("TF", 192, "float32"), ("HZ", 144, "bfloat16"), ("KC32", 256, "bfloat16"),
         ("KC48", 384, "bfloat16"), ("MK", 1024, "bfloat16"), ("M16", 384, "bfloat16"), ("M32", 256, "bfloat16"),
         ("M64", 768, "bfloat16"), ("ZT", 512, "bfloat16"), ("EX", 2048, "bfloat16"), ("ZS", 1024, "bfloat16")]:
@@ -248,6 +249,7 @@ def setup():
     ts(ap("G8T", 0, 128, 1, 0, 8), ap("IG", 0, 128, 1, 0, 8), col(PF, 0, 8), A.is_equal)
     ts(ap("GB"), ap("IM"), col(PM), A.not_equal, 8192.0, A.mult)
     lin(ap("MO"), ap("GB"), 1.0, -4096.0)
+    lin(ap("M0"), ap("GB", 0, 64), 1.0)
     cp(ap("qf", 0, 256, 1, 0, 8), ap("qi", 0, 256, 1, 0, 8))
     mm([(ap("pQ", 0, 256), ap("G8T", 0, 128, 1, 0, 8), ap("qf", 0, 256, 1, 0, 8))])
     for a, q, k, b in runs(first, 0, [0, 1, 2, 3]):
@@ -262,14 +264,15 @@ def setup():
     lin(ap("WS", 0, 24, 3), ap("G8"), col(WCOL))
     lin(ap("WS", 2, 24, 3), ap("G8"), col(NWC))
     lin(ap("WR"), ap("G8"), 8192.0)
-    ms(ap("MK", 0, 16 * GCH), 0.0)
-    fill(ap("MK", 0, 16 * GCH, 16), -32768.0)
     nz = max([0] + [v for s in range(RO) for v in VSH[s] if v <= 64 and not ZG[s]])
-    if nz:
-        ms(ap("ZS", 0, 16 * nz), 0.0)
-    for n, st in (("M16", 16), ("M32", 32), ("M64", 64)):
-        ms(ap(n), 0.0)
+    ms(ap("MK"), 0.0)
+    for n, w in (("ZS", 16 * nz), ("ZA", 528), ("M16", 384), ("M32", 256), ("M64", 768)):
+        if w:
+            dma("Y", [ap(n, 0, w)], [ap("MK", 0, w)], lambda T, n=n, w=w: (T[n][:, 0:w], T.MK[:, 0:w]), 256 * w)
+    fill(ap("MK", 0, 16 * GCH, 16), -32768.0)
+    for n, st in (("M16", 16), ("M32", 32)):
         fill(ap(n, 0, None, st), BIG)
+    fill(ap("M64", 0, None, 64), float(2 ** 40))
     iota(ap("KC48", 0, None, 1, 0, 1), [[0, 8], [65, 3], [3, 16]])
     iota(ap("KC32", 0, None, 1, 0, 1), [[0, 8], [65, 2], [3, 16]])
     iota(ap("I48"), [[0, 16], [1, 48]])
@@ -278,28 +281,26 @@ def setup():
     ts(ap("OH", 768, 816), ap("IOT", 0, 48), col(PM31), A.is_equal)
     ts(ap("OH", 816, 928), ap("IOT", 0, 112), col(PM66), A.not_equal)
     lin(ap("I32"), ap("I3", 0, 128), 1.0)
-    ms(ap("ZA"), 0.0)
     fill(ap("ZJ"), 0.0)
     sizes = set(len(u) for us in UNITS for u in us)
     for n, m in (("CW8", 8), ("CW4", 4)):
         if m // 4 in sizes:
-            fill(ap(n), 768.0)
-            fill(ap(n, 5 * m, 6 * m), 816.0)
+            fill(ap(n, 2 * m, 3 * m), 768.0)
             lin(ap(n, 0, m), ap("IOT", 0, m), 768.0, col(PM48))
-            for k in (1, 3):
-                lin(ap(n, k * m, k * m + m), ap("IOT", 0, m), 0.0, col(PM48))
+            lin(ap(n, m, 2 * m), ap("IOT", 0, m), 0.0, col(PM48))
+            lin(ap(n + "L", 0, 2 * m), ap(n, m, 3 * m), 1.0)
+            fill(ap(n + "L", 2 * m, 3 * m), 816.0)
     if 1 in sizes:
         asel(ap("I3H"), ap("ONE", 0, 192), [[0, 3], [-1, 64]], A.is_equal, 0.0, 0, 1)
     fill(ap("ONF"), 1.0)
     fill(ap("O4K"), 4096.0)
     ts(ap("TH4", 0, 8, 1, 0, 1), ap("thi", 0, 8, 1, 0, 1), 4096.0, A.mult)
     for k in range(3):
-        lin(ap("TW", 4 * k, 4 * k + 4), ap("IOT", 0, 4), 16.0, col(PM))
+        lin(ap("KP", 4 * k, 4 * k + 4), ap("IOT", 0, 4), 16.0, col(PM))
         lin(ap("TF", 64 * k, 64 * k + 64), ap("IOT", 0, 64), 1.0 / 128)
-    lin(ap("DUM", 0, 8), ap("TW", 0, 8), 1.0, 4096.0)
-    lin(ap("D12", 0, 8), ap("TW", 0, 8), 1.0, 8192.0)
-    for n in ("DUM", "D12"):
-        lin(ap(n, 8, 12), ap("TW", 8, 12), 1.0, 1024.0)
+    lin(ap("DUM", 0, 8), ap("KP", 0, 8), 1.0, 4096.0)
+    lin(ap("DUM", 8, 12), ap("KP", 8, 12), 1.0, 1024.0)
+    lin(ap("TW"), ap("KP"), 8192.0)
     fill(ap("X0", W, W + 64), 0.0)
     fill(ap("X1", W, W + 64), 0.0)
     fill(ap("FW", 1024, 1088), 0.0)
@@ -439,13 +440,14 @@ def tail(s, p, n, nv, ui, lo):
     z0 = 256 * (ui % 2)
     cp(sl("ZA", z0 + 15, z0 + 15 + 128 * w, 16), sl("KC6", k0, k0 + 8 * w))
     cw, i3 = ("CW8", "I3") if n == 128 else ("CW4", "I3H")
-    mm([(ap("pW", 0, 3 * m), ap("I32"), ap(cw, 0, 3 * m))] + spread(ap("pW", 0, 3 * m), "ZA", z0, i3, n, 3))
+    mmp([(ap("pW", 0, 3 * m), ap("I32"), ap(cw, 0, 3 * m))], True, False)
+    mmp(spread(ap("pW", 0, 3 * m), "ZA", z0, i3, n, 3), False, True)
     ow = 24 * p
     cp(ap("OW", ow, ow + 3 * m), ap("pW", 0, 3 * m))
     if lo is not None:
         c = lo // 16
         for k in (0, 1):
-            act(ap("V12", 4 * k, 4 * k + 4), ap("pW", 2 * m + c, 2 * m + c + 4), F.Sign, bias=815.0, scale=-1.0)
+            act(ap("V12", 4 * k, 4 * k + 4), ap("pW", 2 * m + c, 2 * m + c + 4), F.Relu, bias=-814.0)
     last = s == RO - 1
     act(ap("ZN%d" % s, t0, t0 + n), ind(ap("B", 48 * t0, 48 * (t0 + n)), ap("OW", ow, ow + m)), F.Abs,
         bias=(0.0 if last else col(C15)), scale=col(ZSC))
@@ -453,8 +455,10 @@ def tail(s, p, n, nv, ui, lo):
     tt(ap("MN", a, c_), ind(ap("OH"), ap("OW", ow + m, ow + 3 * m)), ap("NM", a, c_), A.mult)
     if not last or lo is not None:
         mm([(ap("pQ", 0, n), ap("GB"), ap("MN", a, b)), (ap("pQ", 0, n), ap("GB"), ap("MN", b, c_))])
-        tt(ap("QN%d" % s, t0, t0 + n), ap("pQ", 0, n), ap("MO", 0, n), A.subtract)
+        if not last:
+            tt(ap("QN%d" % s, t0, t0 + n), ap("pQ", 0, n), ap("MO", 0, n), A.subtract)
         if lo is not None:
+            tt(ap("LM", 0, 64), ap("pQ", lo, lo + 64), ap("M0"), A.subtract)
             act(ap("WB"), ap("pQ", lo, lo + 64), F.Identity)
     if last:
         o = ap("pQ", 256, 256 + n, 1, 0, 8)
@@ -472,10 +476,10 @@ def learn(s, p, n, ui, lo):
     ts(sl("K64", 0, 8), sl("KI", k0, k0 + 8), 64, A.bitwise_and)
     tt(sl("ZJ", 15, 143, 16), sl("KC6", k0 + 16, k0 + 24), sl("K64", 0, 8), A.add)
     cw, i3 = ("CW8", "I3") if n == 128 else ("CW4", "I3H")
-    mm([(ap("pW", 64, 64 + 3 * m), ap("I32"), ap(cw, 3 * m, 6 * m))] + spread(ap("pW", 64, 64 + 2 * m), "ZA", 256 * (ui % 2) + 128, i3, n, 2)
+    mm([(ap("pW", 64, 64 + 3 * m), ap("I3", 0, 128), ap(cw + "L"))] + spread(ap("pW", 64, 64 + 2 * m), "ZA", 256 * (ui % 2) + 128, i3, n, 2)
        + spread(ap("pW", 64 + 2 * m, 64 + 3 * m), "ZJ", 0, i3, n, 1))
     cp(ap("OL", 0, 3 * m), ap("pW", 64, 64 + 3 * m))
-    ts(ap("V12", 8, 12), ap("pW", 64 + 2 * m + c, 64 + 2 * m + c + 4), 880.0, A.is_ge)
+    ts(ap("V12", 8, 12), ap("pW", 64 + 2 * m + c, 64 + 2 * m + c + 4), 880.0, A.is_lt)
     a, b = 2 * t0 + lo, 2 * t0 + n + lo
     if n == 64:
         tt(ap("ML"), ind(ap("OH"), ap("OL", 0, 8)), ap("NM", a, a + 128), A.mult)
@@ -483,28 +487,21 @@ def learn(s, p, n, ui, lo):
         tt(ap("ML", 0, 64), ind(ap("OH"), ap("OL", c, c + 4)), ap("NM", a, a + 64), A.mult)
         tt(ap("ML", 64, 128), ind(ap("OH"), ap("OL", m + c, m + c + 4)), ap("NM", b, b + 64), A.mult)
     mm([(ap("pQ", 128, 192), ap("GB"), ap("ML", 0, 64)), (ap("pQ", 128, 192), ap("GB"), ap("ML", 64, 128))])
-    tt(ap("LM"), ap("pQ", 128, 192), ap("MO", 0, 64), A.subtract)
-    scan(ap("SC2", 0, 64), ap("MK", 0, 64), ap("QN%d" % s, t0 + lo, t0 + lo + 64), 0.0, A.add, A.max)
-    scan(ap("SC2", 64, 128), ap("MK", 0, 64), ap("LM"), 0.0, A.add, A.max)
-    tt(ap("E12", 8, 12), ap("I3I", 12 * p + c, 12 * p + c + 4), ap("D12", 8, 12), A.subtract)
-    for x, y in SPLIT:
-        if x < 8:
-            z = min(y, 8)
-            tt(ap("E12", x, z), ap("SC2", 16 * x + 15, 16 * z, 16), ap("D12", x, z), A.subtract)
-        tt(ap("E13", x, y), ap("E12", x, y), ap("V12", x, y), A.mult)
-        tt(ap("VP", x, y), ap("E13", x, y), ap("DUM", x, y), A.add)
-        cp(ap("OV", x, y), ap("VP", x, y))
-        lin(ap("NB", x, y), ap("VP", x, y), -128.0)
-        tt(ap("U", 16 * x, 16 * y), ind(ap("IOT"), ap("OV", x, y)), ap("TF", 16 * x, 16 * y), A.add)
-        for k in range(x, y):
-            act(ap("DD", 64 * k, 64 * k + 64), ap("U", 64 * (k // 4), 64 * (k // 4) + 64), F.Abs, bias=ap("NB", k, k + 1), scale=128.0)
-    for x, y in SPLIT2:
-        scan(ap("DS", 64 * x, 64 * y), ap("M64", 64 * x, 64 * y), ap("DD", 64 * x, 64 * y), 0.0, A.add, A.min)
-    for x, y in SPLIT3:
-        tt(ap("KP", x, y), ap("DS", 64 * x + 63, 64 * y, 64), ap("TW", x, y), A.is_equal)
-        tt(ap("E14", x, y), ap("E13", x, y), ap("KP", x, y), A.mult)
-        tt(ap("VQ", x, y), ap("E14", x, y), ap("DUM", x, y), A.add)
-        cp(ap("OK%d" % s, x, y), ap("VQ", x, y))
+    tt(ap("LM", 64, 128), ap("pQ", 128, 192), ap("M0"), A.subtract)
+    scan(ap("SC2"), ap("MK", 0, 128), ap("LM"), 0.0, A.add, A.max)
+    tt(ap("DN"), ap("V12"), ap("DUM"), A.mult)
+    tt(ap("VP", 8, 12), ap("I3I", 12 * p + c, 12 * p + c + 4), ap("DN", 8, 12), A.max)
+    tt(ap("VP", 0, 8), ap("SC2", 15, 128, 16), ap("DN", 0, 8), A.max)
+    cp(ap("OV"), ap("VP"))
+    lin(ap("NB"), ap("VP"), -float(2 ** 20))
+    tt(ap("VT"), ap("VP"), ap("TW"), A.add)
+    tt(ap("U"), ind(ap("IOT"), ap("OV")), ap("TF"), A.add)
+    for k in range(12):
+        act(ap("DD", 64 * k, 64 * k + 64), ap("U", 64 * (k // 4), 64 * (k // 4) + 64), F.Abs, bias=ap("NB", k, k + 1), scale=float(2 ** 20))
+    scan(ap("DS"), ap("M64"), ap("DD"), 0.0, A.add, A.min)
+    tt(ap("KP"), ap("VT"), ap("DS", 63, 768, 64), A.subtract)
+    tt(ap("VQ"), ap("KP"), ap("DUM"), A.min)
+    cp(ap("OK%d" % s), ap("VQ"))
     X = ap("X%d" % (s % 2))
     tt(ap("T1"), ind(X, ap("OV", 0, 4)), ap("Z%d" % s, t0 + lo, t0 + lo + 64), A.add)
     ts(ap("T2"), ap("T1"), col(VS), A.mult, col(VB), A.add)
@@ -602,10 +599,12 @@ def depend():
 
 
 def prices(m):
-    cost = [c[0] + (c[1] + c[2] * m[1] + c[3] * m[2]) * m[0] + c[4] * m[3] for c in [o["c"] for o in OPS]]
-    pred = [[(j, OPS[j]["lat"] * m[5] + (0.0 if "R" in (o["eng"], OPS[j]["eng"]) or o["eng"] + OPS[j]["eng"] == "PP" else m[4]))
+    cost = [o["c"][0] + (o["c"][1] + o["c"][2] * m[1] + o["c"][3] * m[2]) * m[0] + o["c"][4] * m[3]
+            + (m[6] if o["eng"] in "VS" else 0.0) for o in OPS]
+    lat = [o["lat"] * (m[7] if o["eng"] == "R" else m[5]) for o in OPS]
+    pred = [[(j, lat[j] + (0.0 if "R" in (o["eng"], OPS[j]["eng"]) or o["eng"] + OPS[j]["eng"] == "PP" else m[4]))
              for j in o["dep"]] for o in OPS]
-    return cost, pred, [o["lat"] * m[5] for o in OPS]
+    return cost, pred, lat
 
 
 def place(seq, cost, pred, rel):

@@ -4,20 +4,33 @@ from concourse.mybir import AluOpType, ActivationFunctionType
 A = AluOpType
 F = ActivationFunctionType
 NR, W, RO = 4, 4096, 3
-UNITS = [[(0, 1), (2,), (3,)], [(1, 0), (2,), (3,)], [(2,), (0, 1), (3,)]]
-VSH = [[128, 0, 32], [128, 0, 32], [0, 128, 0]]
-ZG = [False, False, False]
-GCH = 32
-GS = 32
+UNITS = [[((0, 1), "SSVV"), ((2, 3), "SSSM")],
+         [((1, 0), "SSVV"), ((2, 3), "SSSM")],
+         [((2,), "SV"), ((0, 1), "SSSM"), ((3,), "SV")]]
+LISTS = [[(0, 12)], [(0, 12)], [(8, 12), (0, 8)]]
+GV = 32
+GS = 64
+NZ = 64
+ZV = 688
+IOS = 0
+TS = 0
+QS = 1
+GC = 1
+SL = 64
+ROUND = 1.5 * 2 ** 23
+ND = 3
 BIG = float(2 ** 26)
+HUGE = float(2 ** 31)
+MAGIC = 1.5 * 2 ** 29
 
 SCRATCH = {}
 SEMAPHORES = ["cV", "cS", "cP", "cG", "ls"]
 OPS = []
-SEEDS = (1, 9, 7000)
-GUESS = [(0.9, 1.56, 3.8, 0.46, 130.0, 0.9, 10.0, 1.6), (0.83, 1.3, 3.0, 0.42, 200.0, 0.7, 0.0, 1.2),
-         (0.83, 1.4, 3.0, 0.42, 80.0, 1.0, 30.0, 1.2), (1.2, 1.9, 5.0, 0.6, 150.0, 1.1, 20.0, 1.8),
-         (0.83, 1.56, 3.8, 0.42, 80.0, 0.8, 0.0, 2.0)]
+BANK = {}
+SEEDS = (3, 12, 50, 75000)
+GUESS = [(0.9, 1.56, 3.8, 0.46, 100.0, 20.0, 1500.0, 250.0, 2500.0), (0.83, 1.3, 3.0, 0.42, 200.0, 0.0, 2000.0, 200.0, 4000.0),
+         (1.0, 1.56, 3.8, 0.5, 60.0, 40.0, 1200.0, 350.0, 2000.0), (1.2, 1.9, 5.0, 0.6, 150.0, 20.0, 2000.0, 200.0, 4500.0),
+         (1.1, 1.3, 3.0, 0.55, 100.0, 10.0, 1500.0, 300.0, 3000.0)]
 
 
 def buf(name, cols, dtype, where="sbuf"):
@@ -31,37 +44,45 @@ for _n, _c, _d in [
         ("Z0", 256, "bfloat16"), ("Z1", 256, "bfloat16"), ("Z2", 256, "bfloat16"),
         ("Q0", 256, "float32"), ("Q1", 256, "float32"), ("Q2", 256, "float32"),
         ("ZN0", 256, "bfloat16"), ("ZN1", 256, "bfloat16"), ("ZN2", 256, "bfloat16"),
-        ("QN0", 256, "float32"), ("QN1", 256, "float32"), ("QN2", 256, "float32"), ("YQ", 256, "float32"),
-        ("B", 256 * 48, "bfloat16"), ("RS", 4096, "bfloat16"), ("RC", 4096, "bfloat16"), ("RL", 4096, "bfloat16"),
-        ("ZR", 4096, "bfloat16"), ("IOT", 4160, "float32"),
-        ("UI", 16, "int32"), ("I3I", 48, "int32"), ("O3", 48, "uint16"), ("N1", 512, "int32"), ("PP", 256, "float32"),
-        ("AP1", 256, "float32"), ("NM", 512, "int32"), ("ON", 512, "uint16"), ("SC", 4 * 384, "float32"),
-        ("KM", 4 * 8, "float32"), ("KI", 4 * 24, "int32"), ("KC6", 4 * 24, "int32"), ("K64", 8, "int32"),
-        ("ZA", 528, "bfloat16"), ("ZJ", 144, "bfloat16"), ("NW", 4 * 8, "bfloat16"),
-        ("OW", 4 * 24, "uint16"), ("OL", 24, "uint16"), ("MN", 512, "float32"), ("ML", 128, "float32"),
-        ("LM", 128, "float32"), ("WB", 64, "float32"), ("SC2", 128, "float32"), ("DN", 12, "float32"),
-        ("V12", 12, "float32"), ("VT", 12, "float32"), ("VP", 12, "float32"), ("OV", 12, "uint16"), ("NB", 12, "float32"),
-        ("U", 192, "float32"), ("DD", 768, "bfloat16"), ("DS", 768, "bfloat16"), ("KP", 12, "float32"),
-        ("M0", 64, "float32"), ("VQ", 12, "float32"), ("OK0", 12, "uint16"), ("OK1", 12, "uint16"), ("OK2", 12, "uint16"),
-        ("T1", 64, "float32"), ("T2", 64, "int32"), ("T3", 64, "int32"), ("XW0", 64, "bfloat16"), ("XW1", 64, "bfloat16"),
+        ("QN0", 256, "float32"), ("QN1", 256, "float32"), ("YQ", 256, "float32"),
+        ("B", 256 * 48, "bfloat16"), ("RS", 4096, "bfloat16"), ("RC", 4096, "bfloat16"), ("LS", 4096, "bfloat16"),
+        ("LC", 4096, "bfloat16"), ("ZR", 4096, "bfloat16"), ("IOT", 4160, "float32"), ("IO", 112, "float32"),
+        ("UI", 48, "int32"), ("I3I", 144, "int32"), ("O3", 144, "uint16"), ("N1", 512, "int32"), ("PP", 256, "float32"),
+        ("AP1", 256, "float32"), ("NM", 1024, "int32"), ("ON", 1024, "uint16"), ("SC", 4 * 288, "float32"), ("SL", 408, "float32"),
+        ("KI", 24, "int32"), ("KC6", 24, "int32"), ("K64", 8, "int32"), ("NW", 8 * 8, "bfloat16"),
+        ("OW", 144, "uint16"), ("OL", 12, "uint16"), ("MN", 512, "float32"), ("ML", 128, "float32"),
+        ("WB", 64, "float32"), ("SC2", 192, "float32"), ("VT", 12, "float32"), ("VP", 12, "float32"), ("OV", 12, "uint16"),
+        ("U", 192, "float32"), ("DD", 780, "bfloat16"), ("DS", 780, "bfloat16"), ("KP", 12, "float32"),
+        ("VQ", 12, "float32"), ("OK0", 12, "uint16"), ("OK1", 12, "uint16"), ("OK2", 12, "uint16"),
+        ("T1", 64, "float32"), ("T2", 64, "int32"), ("XW0", 64, "bfloat16"), ("XW1", 64, "bfloat16"),
         ("XW2", 64, "bfloat16"), ("XL0", 64, "bfloat16"), ("XL1", 64, "bfloat16"), ("XL2", 64, "bfloat16"),
-        ("F1", 64, "float32"), ("F2", 64, "float32"), ("LIM", 24, "float32"), ("TH4", 8, "float32"),
-        ("ONE", 384, "bfloat16"), ("ONF", 128, "float32"), ("O4K", 128, "bfloat16"), ("I3", 384, "bfloat16"),
-        ("I3H", 192, "bfloat16"), ("NI", 128, "bfloat16"), ("I32", 128, "float32"), ("PI", 3, "int32"), ("CF", 16, "float32"),
-        ("I48", 768, "bfloat16"), ("OH", 928, "bfloat16"), ("G8", 8, "float32"), ("WS", 24, "bfloat16"), ("WR", 8, "bfloat16"),
+        ("F1", 64, "float32"), ("F2", 64, "float32"), ("TH4", 8, "float32"),
+        ("ONE", 384, "bfloat16"), ("ONF", 128, "float32"), ("I3", 384, "bfloat16"),
+        ("I3H", 384, "bfloat16"), ("PI", 4, "int32"), ("CF", 16, "float32"),
+        ("I48", 768, "bfloat16"), ("OH", 928, "bfloat16"), ("G8", 8, "float32"), ("WR", 24, "bfloat16"),
         ("IG", 128, "float32"), ("GB", 128, "float32"), ("G8T", 128, "float32"), ("IM", 128, "float32"), ("MO", 128, "float32"),
-        ("CW8", 24, "float32"), ("CW4", 12, "float32"), ("TW", 12, "float32"), ("DUM", 12, "float32"),
-        ("CW8L", 24, "bfloat16"), ("CW4L", 12, "bfloat16"),
-        ("TF", 192, "float32"), ("HZ", 144, "bfloat16"), ("KC32", 256, "bfloat16"),
-        ("KC48", 384, "bfloat16"), ("MK", 1024, "bfloat16"), ("M16", 384, "bfloat16"), ("M32", 256, "bfloat16"),
-        ("M64", 768, "bfloat16"), ("ZT", 512, "bfloat16"), ("EX", 2048, "bfloat16"), ("ZS", 1024, "bfloat16")]:
+        ("M0", 128, "bfloat16"), ("CT", 40, "bfloat16"), ("CR", 8, "bfloat16"), ("TW", 12, "float32"), ("DUM", 12, "float32"),
+        ("TF", 192, "float32"), ("KC36", 288, "bfloat16"), ("KC51", 408, "bfloat16"),
+        ("M36", 288, "bfloat16"), ("M51", 408, "bfloat16"), ("M65", 780, "bfloat16"), ("T3", 64, "float32"),
+        ("ZT", 512, "bfloat16"), ("I16", 512, "bfloat16"), ("EX", 512, "bfloat16")]:
     buf(_n, _c, _d)
-for _n in ["pH", "pK0", "pK1", "pW", "pQ", "pD0", "pD1", "pD2"]:
+for _n in ["pH", "pK0", "pK1", "pL", "pQ", "pD0", "pD1", "pD2"]:
     buf(_n, 512, "float32", "psum")
+PART = {}
+for _n, _c in [("HZ", 144), ("WS", 32), ("MK", 16 * SL), ("ZS", 16 * NZ), ("ZA", 3 * 144), ("ZL", 272), ("ZJ", 144), ("NL", 288)]:
+    PART[_n] = (sum(c for a, c in PART.values()), _c)
+buf("ZZ", sum(c for a, c in PART.values()), "bfloat16")
+
+
+def spec(name):
+    return SCRATCH[name.split("#")[0] + "0"] if "#" in name else SCRATCH[name]
 
 
 def ap(name, a=0, b=None, step=1, p0=0, p1=128):
-    return (name, a, SCRATCH[name][1][1] if b is None else b, step, p0, p1)
+    if name in PART:
+        o, c = PART[name]
+        return ("ZZ", o + a, o + (c if b is None else b), step, p0, p1)
+    return (name, a, spec(name)[1][1] if b is None else b, step, p0, p1)
 
 
 def ind(win, off):
@@ -73,7 +94,7 @@ def cnt(x):
 
 
 def wid(x):
-    return 2 if SCRATCH[x[0]][2] in ("bfloat16", "uint16") else 4
+    return 2 if spec(x[0])[2] in ("bfloat16", "uint16") else 4
 
 
 def real(T, x):
@@ -81,12 +102,13 @@ def real(T, x):
         return x
     if x[0] == "IND":
         return real(T, x[1]).indirect(real(T, x[2]))
+    t = T[BANK.get(x[0], x[0])]
     if x[3] == 1:
-        return T[x[0]][x[4]:x[5], x[1]:x[2]]
-    return T[x[0]][x[4]:x[5], x[1]:x[2]:x[3]]
+        return t[x[4]:x[5], x[1]:x[2]]
+    return t[x[4]:x[5], x[1]:x[2]:x[3]]
 
 
-def add(eng, cost, outs, ins, fn, sem=None, val=0, after=(), lat=0.0):
+def add(eng, cost, outs, ins, fn, sem=None, val=0, after=(), lat=None, grp=None):
     rd, wr = [], []
     for x in ins:
         if isinstance(x, tuple):
@@ -97,7 +119,8 @@ def add(eng, cost, outs, ins, fn, sem=None, val=0, after=(), lat=0.0):
             rd.append(x[2])
         else:
             wr.append(x)
-    OPS.append({"eng": eng, "c": cost, "rd": rd, "wr": wr, "fn": fn, "sem": sem, "val": val, "after": list(after), "lat": lat})
+    OPS.append({"eng": eng, "c": cost, "rd": rd, "wr": wr, "fn": fn, "sem": sem, "val": val, "after": list(after), "lat": lat,
+                "grp": grp, "stop": grp is None})
     return len(OPS) - 1
 
 
@@ -111,7 +134,7 @@ def vcost(out, ins, two=False):
 
 
 def tt(out, a, b, op):
-    two = a[0] != "IND" and SCRATCH[a[0]][0] == "sbuf" and SCRATCH[b[0]][0] == "sbuf"
+    two = a[0] != "IND" and spec(a[0])[0] == "sbuf" and spec(b[0])[0] == "sbuf"
     c = vcost(out, [a, b], two) if (two or a[0] == "IND" or out[0] == "IND") else (10, max(64, cnt(out)), 0, 0, 0)
     return add("V", c, [out], [a, b], lambda g, T, r: [g.vector.tensor_tensor(real(T, out), real(T, a), real(T, b), op)])
 
@@ -148,23 +171,23 @@ def lin(out, a, scale, bias=0.0):
 
 
 def fill(out, v):
-    return lin(out, ap("ONE", 0, cnt(out)), v)
+    return lin(out, ap("ONE", 0, cnt(out), 1, out[4], out[5]), v)
 
 
-def mm(lst):
-    return mmp(lst, True, True)
-
-
-def mmp(lst, first, last):
+def mm(lst, first=True, grp=None, after=(), close=()):
     c = sum(max(min(64, cnt(l)), cnt(rh)) * (4 if wid(l) == 4 else 1) for o, l, rh in lst)
-    ins = [x for o, l, rh in lst for x in (l, rh)]
-    return add("P", (30, 0, 0, 0, c), [lst[0][0]], ins, lambda g, T, r: [
-        g.tensor.matmul(real(T, o), real(T, l), real(T, rh), first and i == 0, last and i == len(lst) - 1)
-        for i, (o, l, rh) in enumerate(lst)])
+    ins = [x for o, l, rh in lst + list(close) for x in (l, rh)]
+    me = len(OPS)
+    def fn(g, T, r):
+        stop = OPS[me]["stop"]
+        full = lst + list(close) if stop else lst
+        return [g.tensor.matmul(real(T, o), real(T, l), real(T, rh), first and i == 0, stop and i == len(full) - 1)
+                for i, (o, l, rh) in enumerate(full)]
+    return add("P", (30, 0, 0, 0, c), sorted(set(o for o, l, rh in lst)), ins, fn, grp=grp, after=after)
 
 
 def iota(out, pat, base=0, cm=0):
-    fl = SCRATCH[out[0]][2] != "int32"
+    fl = spec(out[0])[2] != "int32"
     def fn(g, T, r):
         if fl:
             return [g.iota(real(T, out), pat, base, cm, allow_small_or_imprecise_dtypes=True)]
@@ -177,15 +200,21 @@ def asel(out, a, pat, op, fill, base, cm):
                lambda g, T, r: [g.affine_select(real(T, out), real(T, a), pat, op, fill, base, cm)])
 
 
-def dma(q, outs, ins, fn, nbytes, after=()):
+def gfill(out, v):
+    return asel(out, ap("ONE", 0, cnt(out), 1, out[4], out[5]), [[0, cnt(out)]], A.is_gt, v, 0, 0)
+
+
+def dma(outs, ins, fn, nbytes, behind=None):
     sem = "d%d" % len(SEMAPHORES)
     SEMAPHORES.append(sem)
-    qq = (lambda g: g.sync) if q == "Y" else (lambda g: g.scalar)
     def f2(g, T, r):
         o, i = fn(T)
-        qq(g).dma_start(o, i).then_inc(T.sem[sem], 16)
+        g.sync.dma_start(o, i).then_inc(T.sem[sem], 16)
         return []
-    return add(q, (60, 0, 0, 0, 0), outs, ins, f2, sem=sem, val=16, after=after, lat=2000 + nbytes / 180.0)
+    i = add("Y", (60, 0, 0, 0, 0), outs, ins, f2, after=[] if behind is None else [behind])
+    j = add("E", (0, 0, 0, 0, 0), [], [], None, after=[i] if behind is None else [i, behind + 1], lat=nbytes)
+    add("D", (0, 0, 0, 0, 0), outs, ins, None, sem=sem, val=16, after=[j])
+    return i
 
 
 def send(src, dst, hop):
@@ -199,172 +228,155 @@ def send(src, dst, hop):
         r["ls"] += len(r["topo"].engines(r["core"], to))
         return []
     i = add("G", (600, 0, 0, 0, 0), [], [src], fn)
-    return add("R", (0, 0, 0, 0, 0), [dst], [], None, sem=sem, val=("eng", hop), after=[i], lat=2500)
+    return add("R", (0, 0, 0, 0, 0), [dst], [], None, sem=sem, val=hop, after=[i])
 
 
 def col(i, p0=0, p1=128):
     return ap("CF", i, i + 1, 1, p0, p1)
 
 
-PM3, PM31, PM66, PM, PG, C15, ZSC, VS, VB, VMIN, IS15, WCOL, PM48, HWF, PF, NWC = range(16)
+PF, PM, PG, P32, PM3, C15, ZSC, VS, VB, VMIN, IS15, WCOL, HWF, NI15 = range(14)
 
 
 def setup():
-    dma("Y", [ap("zin")], [], lambda T: (T.zin[:], T.z0[:]), 65536)
-    dma("Y", [ap("hwi")], [], lambda T: (T.hwi[:], T.hw[:]), 512)
-    dma("S", [ap("awi")], [], lambda T: (T.awi[:], T.aw[:]), 262144)
-    dma("S", [ap("swi")], [], lambda T: (T.swi[:], T.sw[:]), 262144)
-    dma("Y", [ap("fwi")], [], lambda T: (T.fwi[:], T.fw[:]), 524288)
-    dma("S", [ap("qi")], [], lambda T: (T.qi[0:8, :], T.q0[:]), 8192)
-    dma("S", [ap("thi")], [], lambda T: (T.thi[0:1, :], T.th[:]), 32)
-    x0 = dma("Y", [ap("X0", 0, W)], [], lambda T: (T.X0[:, 0:W], T.lx[:]), 1.5 * 2 ** 20)
-    dma("Y", [ap("X1", 0, W)], [], lambda T: (T.X1[:, 0:W], T.lx[:]), 2 ** 20, after=[x0])
+    loads = [(ap("zin"), lambda T: (T.zin[:], T.z0[:]), 65536), (ap("hwi"), lambda T: (T.hwi[:], T.hw[:]), 8192),
+             (ap("awi"), lambda T: (T.awi[:], T.aw[:]), 262144), (ap("swi"), lambda T: (T.swi[:], T.sw[:]), 262144),
+             (ap("qi"), lambda T: (T.qi[0:8, :], T.q0[:]), 8192), (ap("thi"), lambda T: (T.thi[0:1, :], T.th[:]), 32),
+             (ap("X0", W), lambda T: (T.X0[:, W:W + 64], T.lx[:, 0:64]), 16384),
+             (ap("X0", 0, W), lambda T: (T.X0[:, 0:W], T.lx[:]), 2 ** 20), (ap("fwi"), lambda T: (T.fwi[:], T.fw[:]), 524288),
+             (ap("X1", W), lambda T: (T.X1[:, W:W + 64], T.lx[:, 0:64]), 16384),
+             (ap("X1", 0, W), lambda T: (T.X1[:, 0:W], T.lx[:]), 2 ** 20)]
+    prev = None
+    for x, fn, nb in loads:
+        prev = dma([x], [], fn, nb, prev)
     iota(ap("PI", 0, 1), [[0, 1]], 0, 1)
-    iota(ap("IOT", 0, 128), [[1, 128]])
+    iota(ap("IO"), [[1, 112]])
+    dma([ap("FW", 1024)], [ap("IO", 0, 64)], lambda T: (T.FW[:, 1024:1088], T.IO[:, 0:64]), 32768, prev)
     ms(ap("ONE"), 1.0)
+    ms(ap("ZZ", 0, ZV), 0.0)
+    for a in range(ZV, cnt(ap("ZZ")), 384):
+        fill(ap("ZZ", a, min(a + 384, cnt(ap("ZZ")))), 0.0)
     ts(ap("PI", 1, 2), ap("PI", 0, 1), 15, A.bitwise_and)
     ts(ap("PI", 2, 3), ap("PI", 0, 1), 4, A.logical_shift_right)
-    cp(col(PM), ap("PI", 1, 2))
-    cp(col(PG), ap("PI", 2, 3))
-    cp(col(PF), ap("PI", 0, 1))
+    ts(ap("PI", 3, 4), ap("PI", 0, 1), 31, A.bitwise_and)
+    cp(ap("CF", PF, P32 + 1), ap("PI"))
     ts(col(IS15), col(PM), 15.0, A.is_equal)
     lin(col(C15), col(IS15), 15.0)
-    ts(ap("G8"), ap("IOT", 0, 8), col(PG), A.is_equal)
-    ms(ap("HZ"), 0.0)
+    ts(ap("G8"), ap("IO", 0, 8), col(PG), A.is_equal)
     cp(col(HWF), ap("hwi"))
-    ts(ap("HZ", 15, 143, 16), ap("G8"), col(HWF), A.mult)
-    first = [h for u in UNITS[0] for h in u]
-    for a, q, k, b in runs(first, 0, [0, 1, 2, 3]):
-        ts(ap("Z0", 64 * a, 64 * (a + k)), ap("zin", 64 * q, 64 * (q + k)), col(C15), A.add)
-    cp(ap("FW", 0, 1024), ap("fwi"))
+    lin(ap("HZ", 15, 143, 16), ap("G8"), col(HWF))
+    first = [h for u, md in UNITS[0] for h in u]
+    for a, q, k, b in runs(first, 0, [0, 1, 2, 3], False):
+        lin(ap("Z0", 64 * a, 64 * (a + k)), ap("zin", 64 * q, 64 * (q + k)), 1.0, col(C15))
+    if GC:
+        for a in (0, 512):
+            asel(ap("FW", a, a + 512), ap("fwi", a, a + 512), [[0, 512]], A.is_ge, 0.0, 0, 0)
+    else:
+        cp(ap("FW", 0, 1024), ap("fwi"))
     ts(ap("SP"), ap("swi"), 2048.0, A.subtract)
     ts(ap("RT0"), ap("awi"), 3232.0, A.mult, 65536.0, A.add)
     ts(ap("RT"), ap("RT0"), 131071, A.bitwise_and)
     iota(ap("IG"), [[1, 8], [0, 16]])
     iota(ap("IM"), [[0, 8], [1, 16]])
     asel(ap("I3"), ap("ONE"), [[0, 3], [-1, 128]], A.is_equal, 0.0, 0, 1)
-    lin(ap("NI"), ap("I3", 0, 128), -1.0)
-    for i in range(16):
-        lin(ap("EX", i, 2048, 16), ap("I3", 0, 128), 1.0)
+    iota(ap("I16"), [[1, 32], [0, 16]])
+    ts(ap("EX"), ap("I16"), col(P32), A.is_equal)
     ts(ap("G8T", 0, 128, 1, 0, 8), ap("IG", 0, 128, 1, 0, 8), col(PF, 0, 8), A.is_equal)
-    ts(ap("GB"), ap("IM"), col(PM), A.not_equal, 8192.0, A.mult)
-    lin(ap("MO"), ap("GB"), 1.0, -4096.0)
-    lin(ap("M0"), ap("GB", 0, 64), 1.0)
+    ts(ap("M0"), ap("IM"), col(PM), A.not_equal, -8192.0, A.mult)
+    lin(ap("MO"), ap("M0"), 1.0, 4096.0)
     cp(ap("qf", 0, 256, 1, 0, 8), ap("qi", 0, 256, 1, 0, 8))
     mm([(ap("pQ", 0, 256), ap("G8T", 0, 128, 1, 0, 8), ap("qf", 0, 256, 1, 0, 8))])
     for a, q, k, b in runs(first, 0, [0, 1, 2, 3]):
-        tt(ap("Q0", 64 * a, 64 * (a + k)), ap("pQ", 64 * q, 64 * (q + k)), ap("MO", 0, 64 * k), A.subtract)
+        tt(ap("Q0", 64 * a, 64 * (a + k)), ap("pQ", 64 * q, 64 * (q + k)), ap("MO", 0, 64 * k), A.add)
     ts(ap("GB"), ap("IG"), col(PG), A.is_equal)
-    for i, m, a in [(PM3, 3.0, 0.0), (PM31, 3.0, 1.0), (PM66, 3.0, 66.0), (PM48, 48.0, 0.0)]:
-        lin(col(i), col(PM), m, a)
-    for i, m, a in [(ZSC, -1.0, 1.0), (VS, 1.0, 1.0), (VB, -26.0, 0.0), (VMIN, -240.0, 255.0), (WCOL, 61440.0, 4096.0),
-                    (NWC, -61440.0, -4096.0)]:
+    lin(col(PM3), col(PM), 3.0)
+    for i, m, a in [(ZSC, -1.0, 1.0), (VMIN, -240.0, 255.0), (WCOL, 61440.0, 4096.0)] + (
+            [(VS, 0.5005, 0.4995), (VB, -13.0, ROUND), (NI15, -1.0, 0.0)] if TS else [(VS, 0.5, 0.5), (VB, -12.75, -0.25)]):
         lin(col(i), col(IS15), m, a)
-    fill(ap("WS", 1, 24, 3), 0.0)
     lin(ap("WS", 0, 24, 3), ap("G8"), col(WCOL))
-    lin(ap("WS", 2, 24, 3), ap("G8"), col(NWC))
-    lin(ap("WR"), ap("G8"), 8192.0)
-    nz = max([0] + [v for s in range(RO) for v in VSH[s] if v <= 64 and not ZG[s]])
-    ms(ap("MK"), 0.0)
-    for n, w in (("ZS", 16 * nz), ("ZA", 528), ("M16", 384), ("M32", 256), ("M64", 768)):
-        if w:
-            dma("Y", [ap(n, 0, w)], [ap("MK", 0, w)], lambda T, n=n, w=w: (T[n][:, 0:w], T.MK[:, 0:w]), 256 * w)
-    fill(ap("MK", 0, 16 * GCH, 16), -32768.0)
-    for n, st in (("M16", 16), ("M32", 32)):
-        fill(ap(n, 0, None, st), BIG)
-    fill(ap("M64", 0, None, 64), float(2 ** 40))
-    iota(ap("KC48", 0, None, 1, 0, 1), [[0, 8], [65, 3], [3, 16]])
-    iota(ap("KC32", 0, None, 1, 0, 1), [[0, 8], [65, 2], [3, 16]])
+    lin(ap("WS", 2, 24, 3), ap("WS", 0, 24, 3), -1.0)
+    lin(ap("WR"), ap("WS", 0, 24), -2.0)
+    gfill(ap("MK", 0, None, 16), -32768.0)
+    asel(ap("M36"), ap("ZA", 0, 288), [[0, 8], [1, 36]], A.not_equal, BIG, 0, 0)
+    gfill(ap("M36", 34, None, 36), MAGIC)
+    gfill(ap("M36", 35, None, 36), -MAGIC)
+    asel(ap("M51"), ap("ZA", 0, 408), [[0, 24], [1, 17]], A.not_equal, BIG, 0, 0)
+    iota(ap("KC36", 0, None, 1, 0, 1), [[0, 8], [65, 2], [3, 18]], -23)
+    iota(ap("KC51", 0, None, 1, 0, 1), [[0, 8], [65, 3], [3, 17]], 1)
+    for n, a, st in (("KC36", 17, 18), ("KC36", 34, 36), ("KC51", 33, 51), ("KC51", 50, 51)):
+        gfill(ap(n, a, None, st, 0, 1), HUGE)
     iota(ap("I48"), [[0, 16], [1, 48]])
     ts(ap("OH", 0, 768), ap("I48"), col(PM3), A.is_equal)
-    ts(ap("OH", 47, 768, 48), ap("IOT", 0, 16), col(PM), A.is_equal)
-    ts(ap("OH", 768, 816), ap("IOT", 0, 48), col(PM31), A.is_equal)
-    ts(ap("OH", 816, 928), ap("IOT", 0, 112), col(PM66), A.not_equal)
-    lin(ap("I32"), ap("I3", 0, 128), 1.0)
-    fill(ap("ZJ"), 0.0)
-    sizes = set(len(u) for us in UNITS for u in us)
-    for n, m in (("CW8", 8), ("CW4", 4)):
-        if m // 4 in sizes:
-            fill(ap(n, 2 * m, 3 * m), 768.0)
-            lin(ap(n, 0, m), ap("IOT", 0, m), 768.0, col(PM48))
-            lin(ap(n, m, 2 * m), ap("IOT", 0, m), 0.0, col(PM48))
-            lin(ap(n + "L", 0, 2 * m), ap(n, m, 3 * m), 1.0)
-            fill(ap(n + "L", 2 * m, 3 * m), 816.0)
-    if 1 in sizes:
-        asel(ap("I3H"), ap("ONE", 0, 192), [[0, 3], [-1, 64]], A.is_equal, 0.0, 0, 1)
-    fill(ap("ONF"), 1.0)
-    fill(ap("O4K"), 4096.0)
-    ts(ap("TH4", 0, 8, 1, 0, 1), ap("thi", 0, 8, 1, 0, 1), 4096.0, A.mult)
-    for k in range(3):
-        lin(ap("KP", 4 * k, 4 * k + 4), ap("IOT", 0, 4), 16.0, col(PM))
-        lin(ap("TF", 64 * k, 64 * k + 64), ap("IOT", 0, 64), 1.0 / 128)
+    ts(ap("OH", 47, 768, 48), ap("IO", 0, 16), col(PM), A.is_equal)
+    ts(ap("OH", 768, 816), ap("IO", 0, 48), 1.0, A.subtract, col(PM3), A.is_equal)
+    ts(ap("OH", 816, 928), ap("IO"), 66.0, A.subtract, col(PM3), A.not_equal)
+    ts(ap("CT", 0, 16), ap("ONE", 0, 16), col(PM3), A.mult, 16.0, A.mult)
+    for k, v in ((2, 768.0), (3, 816.0), (4, 60.0 * 2048)):
+        gfill(ap("CT", 8 * k, 8 * k + 8), v)
+    iota(ap("CR", 0, 8, 1, 0, 1), [[768, 8]])
+    for a, k, v in ((0, 3, 1.0), (192, 1, -2048.0), (256, 2, 2.0)):
+        asel(ap("I3H", a, a + 64 * k), ap("ZA", 0, 64 * k), [[0, k], [-1, 64]], A.not_equal, v, 0, 1)
+    iota(ap("ONF", 0, 128, 1, 0, 1), [[0, 128]], 1)
+    ts(ap("TH4", 0, 8, 1, 0, 1), ap("thi", 0, 8, 1, 0, 1), 4096.0, A.mult, 129.0, A.subtract)
+    iota(ap("VT"), [[0, 3], [16, 4]])
+    lin(ap("KP"), ap("VT"), 1.0, col(PM))
+    iota(ap("TF"), [[0, 3], [1, 64]], 1)
     lin(ap("DUM", 0, 8), ap("KP", 0, 8), 1.0, 4096.0)
     lin(ap("DUM", 8, 12), ap("KP", 8, 12), 1.0, 1024.0)
-    lin(ap("TW"), ap("KP"), 8192.0)
-    fill(ap("X0", W, W + 64), 0.0)
-    fill(ap("X1", W, W + 64), 0.0)
-    fill(ap("FW", 1024, 1088), 0.0)
-    for k in range(4):
-        iota(ap("IOT", 128 + 1008 * k, 1136 + 1008 * k), [[1, 1008]], 128 + 1008 * k)
+    lin(ap("TW"), ap("KP"), 8192.0, 8192.0)
+    iota(ap("M65"), [[0, 780]], 1)
+    gfill(ap("M65", 0, None, 65), float(2 ** 40))
+    gfill(ap("M65", 64, None, 65), float(2 ** 20))
+    gfill(ap("DD", 64, None, 65), HUGE)
+    for k in range(8):
+        if k < 8 - IOS:
+            iota(ap("IOT", 520 * k, 520 * k + 520), [[128, 520]], 128 * 520 * k)
+        else:
+            lin(ap("IOT", 520 * k, 520 * k + 520), ap("IOT", 0, 520), 1.0, 128.0 * 520 * k)
 
 
-def limit(s):
-    lst = [(ap("pW", 256, 264), ap("ONF", 0, 128, 1, 0, 1), ap("TH4", 0, 8, 1, 0, 1))]
-    if s > 0:
-        p = 0
-        for u in UNITS[s - 1]:
-            n = 64 * len(u)
-            lst.append((ap("pW", 256, 264), ap("O4K", 0, 128, 1, 0, n), ap("NW", 8 * p, 8 * p + 8, 1, 0, n)))
-            p += len(u)
-    mm(lst)
-    ts(ap("LIM", 8 * s, 8 * s + 8), ap("pW", 256, 264), 4090.0 * 4096, A.min, 81.0, A.subtract)
-
-
-def front(s, p, n, nv):
-    t0, m = 64 * p, n // 16
+def front(s, p, n, units):
+    t0, m, hc = 64 * p, n // 16, 16 * s + 4 * p
     Z, Q = "Z%d" % s, "Q%d" % s
-    mm([(ap("pH", 0, m), ap("HZ", 15 - r, 143 - r), ap(Z, t0 + r, t0 + n, 16)) for r in range(16)])
-    ui = ap("UI", 4 * p, 4 * p + m)
-    cp(ui, ap("pH", 0, m))
-    o = 12 * p
+    mm([(ap("pH", hc, hc + m), ap("HZ", 15 - r, 143 - r), ap(Z, t0 + r, t0 + n, 16)) for r in range(16)])
+    ui = ap("UI", hc, hc + m)
+    cp(ui, ap("pH", hc, hc + m))
+    o = 3 * hc
     ts(ap("I3I", o, o + m), ui, 2, A.logical_shift_right, 1023, A.bitwise_and)
     ts(ap("I3I", o + m, o + 2 * m), ui, 511, A.bitwise_and)
     ts(ap("I3I", o + 2 * m, o + 3 * m), ui, 3, A.logical_shift_right, 511, A.bitwise_and)
     cp(ap("O3", o, o + 3 * m), ap("I3I", o, o + 3 * m))
     ok, os_, oa = [ap("O3", o + k * m, o + k * m + m) for k in range(3)]
-    a, b, c = 2 * t0, 2 * t0 + n, 2 * t0 + 2 * n
-    tt(ap("N1", a, b), ind(ap("FW" if s else "fwi", 0, 1024), ok), ap(Q, t0, t0 + n), A.max)
-    ts(ap("NM", a, b), ap("N1", a, b), 4095, A.bitwise_and)
-    cp(ap("ON", a, b), ap("NM", a, b))
     ts(ap("PP", t0, t0 + n), ind(ap("awi"), oa), 32.0, A.add)
     tt(ap("AP1", t0, t0 + n), ind(ap("SP"), os_), ap("PP", t0, t0 + n), A.mult)
-    tt(ap("N1", b, c), ind(ap("RT"), oa), ap("AP1", t0, t0 + n), A.add)
-    ts(ap("NM", b, c), ap("N1", b, c), 5, A.arith_shift_right, 4095, A.bitwise_and)
-    cp(ap("ON", b, c), ap("NM", b, c))
-    zt = ap("pH", 128, 256, 1, 0, n)
-    mm([(zt, ap(Z, t0, t0 + n), ap("NI"))])
-    act(ap("ZT", 2 * t0, 2 * t0 + 128, 1, 0, n), zt, F.Identity)
-    v0, v1 = t0 + n - nv, t0 + n
-    if nv and ZG[s]:
-        for i in range(16):
-            asel(ap("ZR", 16 * v0 + i, 16 * v1, 16), ap(Z, v0, v1), [[0, nv]], A.is_ge, 0.0, 0, 0)
-    elif nv > 64:
-        for i in range(16):
-            cp(ap("ZR", 16 * v0 + i, 16 * v1, 16), ap(Z, v0, v1))
-    elif nv:
-        cp(ap("ZS", 0, 16 * nv, 16), ap(Z, v0, v1))
-        for a in range(0, nv, 32):
-            scan(ap("ZR", 16 * (v0 + a), 16 * (v0 + a + 32)), ap("MK", 0, 512), ap("ZS", 16 * a, 16 * a + 512), 0.0, A.add, A.max)
+    tt(ap("N1", 256 + t0, 256 + t0 + n), ind(ap("RT"), oa), ap("AP1", t0, t0 + n), A.add)
+    tt(ap("N1", t0, t0 + n), ind(ap("FW" if s else "fwi", 0, 1024), ok), ap(Q, t0, t0 + n), A.max)
+    for q, k in units:
+        u0, a = 64 * q, 512 * (s % 2) + 128 * q
+        ts(ap("NM", a + k, a + 2 * k), ap("N1", 256 + u0, 256 + u0 + k), 5, A.arith_shift_right, 4095, A.bitwise_and)
+        cp(ap("ON", a + k, a + 2 * k), ap("NM", a + k, a + 2 * k))
+        ts(ap("NM", a, a + k), ap("N1", u0, u0 + k), 4095, A.bitwise_and)
+        cp(ap("ON", a, a + k), ap("NM", a, a + k))
 
 
-DB = [0]
+TURN = [0, 0]
 
 
-def bulk(s, p, n, nv):
-    t0 = 64 * p
+def spans(md, letters, most):
+    out = []
+    for k, c in enumerate(md):
+        if c in letters:
+            if out and out[-1][1] == 32 * k and out[-1][1] - out[-1][0] < most:
+                out[-1] = (out[-1][0], 32 * k + 32)
+            else:
+                out.append((32 * k, 32 * k + 32))
+    return out
+
+
+def bulk(s, p, md):
+    t0, n = 64 * p, 32 * len(md)
     X = ap("X%d" % (s % 2))
-    ns = n - nv
-    so, co = 2 * t0, 2 * t0 + n
+    on = 512 * (s % 2) + 2 * t0
     Z = "Z%d" % s
 
     def lane(k, a, b):
@@ -373,156 +385,192 @@ def bulk(s, p, n, nv):
     def flat(name, a, b):
         return ap(name, 16 * (t0 + a), 16 * (t0 + b))
 
-    def viapsum(raw, k, func, a, b):
-        for x in range(a, b, 32):
-            y = min(b, x + 32)
-            d = ap("pD%d" % (DB[0] % 3), 0, 16 * (y - x))
-            DB[0] += 1
-            mm([(d, ap("ZT", 2 * t0, 2 * t0 + 128, 1, 0, n), ap("EX", 16 * x, 16 * y, 1, 0, n)), (d, ap("I3", 0, 128), flat(raw, x, y))])
-            act(lane(k, x, y), d, func)
+    def bank():
+        TURN[0] += 1
+        return "pD#%d" % TURN[0]
 
-    for a in range(0, ns, GS):
-        b = min(ns, a + GS)
-        act(flat("RC", a, b), ind(X, ap("ON", co + a, co + b)), F.Identity)
-        viapsum("RC", 1, F.Abs, a, b)
-    for a in range(0, ns, GCH):
-        b = min(ns, a + GCH)
-        scan(lane(2, a, b), ap("MK", 0, 16 * (b - a)), flat("RC", a, b), 0.0, A.add, A.max)
-    if ns:
-        top = ap("B", 48 * t0 + 47, 48 * (t0 + ns), 48)
-        tt(top, top, ap(Z, t0, t0 + ns), A.subtract)
-    for a in range(0, n, GS):
-        b = min(n, a + GS)
-        act(flat("RS", a, b), ind(X, ap("ON", so + a, so + b)), F.Identity)
-        viapsum("RS", 0, F.Abs, a, b)
-    for a in range(ns, n, GCH):
-        b = min(n, a + GCH)
-        tt(lane(1, a, b), ind(X, ap("ON", co + a, co + b)), flat("ZR", a, b), A.subtract)
-        ts(flat("RL", a, b), lane(1, a, b), 0.0, A.max)
-        scan(lane(2, a, b), ap("MK", 0, 16 * (b - a)), lane(1, a, b), 0.0, A.add, A.max)
+    def greatest(src, a, b):
+        for x in range(a, b, SL):
+            y = min(b, x + SL)
+            scan(lane(2, x, y), ap("MK", 0, 16 * (y - x)), src(x, y), 0.0, A.add, A.max)
+
+    if md.strip("V"):
+        zt = ap(bank(), 0, 128, 1, 0, n)
+        mm([(zt, ap(Z, t0, t0 + n), ap("I3", 0, 128))])
+        lin(ap("ZT", 2 * t0, 2 * t0 + 128, 1, 0, n), zt, -1.0)
+    for a, b in spans(md, "VMN", NZ):
+        z0 = TURN[1] if TURN[1] + 16 * (b - a) <= 16 * NZ else 0
+        TURN[1] = z0 + 16 * (b - a)
+        cp(ap("ZS", z0, TURN[1], 16), ap(Z, t0 + a, t0 + b))
+        for x in range(a, b, SL):
+            y = min(b, x + SL)
+            scan(flat("ZR", x, y), ap("MK", 0, 16 * (y - x)), ap("ZS", z0 + 16 * (x - a), z0 + 16 * (y - a)), 0.0, A.add, A.max)
+    for k, raw, low, mine in ((1, "RC", "LC", "SN"), (0, "RS", "LS", "SM")):
+        o = on + k * n
+        for a, b in spans(md, mine, GS):
+            act(flat(raw, a, b), ind(X, ap("ON", o + a, o + b)), F.Identity)
+            for x in range(a, b, 32):
+                d = ap(bank())
+                mm([(d, ap("ZT", 2 * t0, 2 * t0 + 128, 1, x, x + 32), ap("EX", 0, 512, 1, x, x + 32)),
+                    (d, ap("I3", 0, 128), flat(raw, x, x + 32))])
+                act(lane(k, x, x + 32), d, F.Abs)
+            if k:
+                greatest(lambda x, y: flat("RC", x, y), a, b)
+        if k:
+            for a, b in spans(md, mine, 128):
+                top = ap("B", 48 * (t0 + a) + 47, 48 * (t0 + b), 48)
+                tt(top, top, ap(Z, t0 + a, t0 + b), A.subtract)
+        for a, b in spans(md, "VMN".replace(mine[1], ""), GV):
+            tt(lane(k, a, b), ind(X, ap("ON", o + a, o + b)), flat("ZR", a, b), A.subtract)
+            ts(flat(low, a, b), lane(k, a, b), 0.0, A.min)
+            if k:
+                greatest(lambda x, y: lane(1, x, y), a, b)
 
 
-def spread(out, zname, z0, rhs, n, w):
-    return [(out, ap(zname, z0 + 15 - r, z0 + 143 - r, 1, 0, n), ap(rhs, r, w * n, 16, 0, n)) for r in range(16)]
+def spread(out, zname, z0, rhs, c0, cols, n):
+    return [(out, ap(zname, z0 + 15 - r, z0 + 143 - r, 1, 0, n), ap(rhs, c0 + r, c0 + cols, 16, 0, n)) for r in range(16)]
 
 
-def tail(s, p, n, nv, ui, lo):
-    t0, m, ns = 64 * p, n // 16, n - nv
-    K = "pK%d" % (ui % 2)
-    L = 32 if lo is None else 48
+KEYS = []
+
+
+def tail(s, p, md):
+    n = 32 * len(md)
+    t0, m = 64 * p, n // 16
+    K = "pK#%d" % len(KEYS)
+    BANK[K] = "pK%d" % (len(KEYS) % 2)
+    L, H = (36, 18) if p else (51, 17)
     def sl(name, a, b, st=1):
         return ap(name, a, b, st, 0, n)
-    bl = lambda k, i, a=0, b=n: ap("B", 48 * (t0 + a) + 3 * i + k, 48 * (t0 + b), 48)
-    mmp([(sl(K, 0, 8 * L), ap("ONE", 0, n, 1, 0, 1), ap("KC%d" % L, 0, None, 1, 0, 1))], True, False)
-    if ns:
-        mmp([(ap(K, 16 + i, 8 * L, L, 0, ns), bl(1, i, 0, ns), ap("WS", 0, 24, 3)) for i in range(16)], False, False)
-    if nv:
-        mmp([(ap(K, 16 + i, 8 * L, L, ns, n), bl(1, i, ns, n), ap("WS", 2, 24, 3)) for i in range(16)]
-            + [(ap(K, 16 + i, 8 * L, L, ns, n), ap("RL", 16 * (t0 + ns) + i, 16 * (t0 + n), 16), ap("WR")) for i in range(16)], False, False)
-    if lo is None:
-        mmp([(sl(K, i, 256, 32), bl(0, i), ap("WS", 0, 24, 3)) for i in range(16)], False, True)
+    mm([(sl(K, 0, 8 * L), ap("ONE", 0, n, 1, 0, 1), ap("KC%d" % L, 0, None, 1, 0, 1))], True, K, KEYS[-2:-1])
+    lst = [(sl(K, 16, 8 * L, L), ap("ONF", 0, n, 1, 0, 1), ap("TH4", 0, 8, 1, 0, 1))]
+    if s > 0:
+        q = 0
+        for u, x in UNITS[s - 1]:
+            c, k = 32 * ((s - 1) % 2) + 8 * q, 64 * len(u)
+            c2 = 144 * ((s - 1) % 2)
+            lst.append((sl(K, 16, 8 * L, L), ap("ONE", 0, n, 1, 0, k),
+                        ap("NW", c, c + 8, 1, 0, k) if q else ap("NL", c2 + 15, c2 + 143, 16, 0, k)))
+            q += len(u)
+    mm(lst, False, K)
+    for k, low, other in ((1, "LC", "VM"), (0, "LS", "VN")):
+        st, ws = (L, 3) if k or p else (H, 1)
+        d = mm([(sl(K, H * k + i, 8 * L, st), ap("B", 48 * t0 + 3 * i + k, 48 * (t0 + n), 48), ap("WS", 0, 24, ws))
+                for i in range(16)], False, K)
+        for a, b in spans(md, other, 128):
+            for x, y in ([(a, 64), (64, b)] if a == 32 and b > 64 else [(a, b)]):
+                mm([(ap(K, H * k + i, 8 * L, st, x, y), ap(low, 16 * (t0 + x) + i, 16 * (t0 + y), 16), ap("WR", 0, 24, ws))
+                    for i in range(16)], False, K, [d],
+                   [(sl(K, 0, 8), ap("ONE", 0, n, 1, 0, 1), ap("WS", 24, 32, 1, 0, 1))] if y - x < n else [])
+    if p:
+        c0, za, z0 = 288 * p, "ZA", 144 * (p - 1)
+        KEYS.append(scan(sl("SC", c0, c0 + 288), sl("M36", 0, 288), sl(K, 0, 288), 0.0, A.add, A.min))
+        tt(sl("ZA", z0 + 15, z0 + 143, 16), sl("SC", c0 + 33, c0 + 288, 36), sl("SC", c0 + 35, c0 + 288, 36), A.subtract)
     else:
-        mmp([(sl(K, i, 384, 16), bl(0, i), ap("WS")) for i in range(16)], False, True)
-    c0 = 384 * p
-    scan(sl("SC", c0, c0 + 8 * L), sl("M32" if lo is None else "M16", 0, 8 * L), sl(K, 0, 8 * L), 0.0, A.add, A.min)
-    k0 = 24 * p
-    lim = sl("LIM", 8 * s, 8 * s + 8)
-    if lo is None:
-        tt(sl("KI", k0, k0 + 8), sl("SC", c0 + 31, c0 + 256, 32), lim, A.min)
-    else:
-        ks, kc, kn = [sl("SC", c0 + 15 + 16 * k, c0 + 384, 48) for k in range(3)]
-        tt(sl("KM", 8 * p, 8 * p + 8), ks, kc, A.min)
-        tt(sl("KI", k0, k0 + 8), sl("KM", 8 * p, 8 * p + 8), lim, A.min)
-        tt(sl("KI", k0 + 8, k0 + 16), ks, kc, A.max)
-        cp(sl("KI", k0 + 16, k0 + 24), kn)
-    w = 1 if lo is None else 2
-    ts(sl("KC6", k0, k0 + 16 * w - 8), sl("KI", k0, k0 + 16 * w - 8), 63, A.bitwise_and)
-    z0 = 256 * (ui % 2)
-    cp(sl("ZA", z0 + 15, z0 + 15 + 128 * w, 16), sl("KC6", k0, k0 + 8 * w))
-    cw, i3 = ("CW8", "I3") if n == 128 else ("CW4", "I3H")
-    mmp([(ap("pW", 0, 3 * m), ap("I32"), ap(cw, 0, 3 * m))], True, False)
-    mmp(spread(ap("pW", 0, 3 * m), "ZA", z0, i3, n, 3), False, True)
-    ow = 24 * p
-    cp(ap("OW", ow, ow + 3 * m), ap("pW", 0, 3 * m))
-    if lo is not None:
-        c = lo // 16
-        for k in (0, 1):
-            act(ap("V12", 4 * k, 4 * k + 4), ap("pW", 2 * m + c, 2 * m + c + 4), F.Relu, bias=-814.0)
+        za, z0 = "ZL", 0
+        KEYS.append(scan(sl("SL", 0, 408), sl("M51", 0, 408), sl(K, 0, 408), 0.0, A.add, A.min))
+        tt(sl("KI", 0, 8), sl("SL", 16, 408, 51), sl("SL", 33, 408, 51), A.min)
+        tt(sl("KI", 8, 16), sl("SL", 15, 408, 51), sl("SL", 33, 408, 51), A.max)
+        cp(sl("KI", 16, 24), sl("SL", 50, 408, 51))
+        ts(sl("KC6", 0, 24), sl("KI", 0, 24), 63, A.bitwise_and)
+        cp(sl("ZL", 15, 271, 16), sl("KC6", 0, 16))
+    shift = 23.0 if p else -1.0
+    i3, cs = ("I3", 1) if n == 128 else ("I3H", 2)
+    ow = 48 * s + 12 * p
+    pw = 64 + ow
+    mm([(ap("pH", pw, pw + 3 * m), ap("I3", 0, 128), ap("CT", 0, 24, cs)),
+        (ap("pH", pw, pw + m), ap("ONE", 0, 128, 1, 0, 1), ap("CR", 0, m, 1, 0, 1))]
+       + spread(ap("pH", pw, pw + 3 * m), za, z0, i3, 0, 3 * n, n))
+    ts(ap("OW", ow, ow + 3 * m), ap("pH", pw, pw + 3 * m), shift, A.add)
     last = s == RO - 1
     act(ap("ZN%d" % s, t0, t0 + n), ind(ap("B", 48 * t0, 48 * (t0 + n)), ap("OW", ow, ow + m)), F.Abs,
         bias=(0.0 if last else col(C15)), scale=col(ZSC))
     a, b, c_ = 2 * t0, 2 * t0 + n, 2 * t0 + 2 * n
-    tt(ap("MN", a, c_), ind(ap("OH"), ap("OW", ow + m, ow + 3 * m)), ap("NM", a, c_), A.mult)
-    if not last or lo is not None:
-        mm([(ap("pQ", 0, n), ap("GB"), ap("MN", a, b)), (ap("pQ", 0, n), ap("GB"), ap("MN", b, c_))])
-        if not last:
-            tt(ap("QN%d" % s, t0, t0 + n), ap("pQ", 0, n), ap("MO", 0, n), A.subtract)
-        if lo is not None:
-            tt(ap("LM", 0, 64), ap("pQ", lo, lo + 64), ap("M0"), A.subtract)
-            act(ap("WB"), ap("pQ", lo, lo + 64), F.Identity)
+    nm = 512 * (s % 2)
+    tt(ap("MN", a, c_), ind(ap("OH"), ap("OW", ow + m, ow + 3 * m)), ap("NM", nm + a, nm + c_), A.mult)
+    if not last or not p:
+        k = 64 if last else n
+        pq = ap("pQ", t0, t0 + k)
+        lst = [(pq, ap("GB"), ap("MN", a, a + k)), (pq, ap("GB"), ap("MN", b, b + k))]
+        if p and QS:
+            mm([(pq, ap("I3", 0, 128), ap("M0", 0, n))] + lst)
+            lin(ap("QN%d" % s, t0, t0 + n), pq, 1.0, 4096.0)
+        else:
+            mm(lst)
+            if not last:
+                tt(ap("QN%d" % s, t0, t0 + n), pq, ap("MO", 0, n), A.add)
+        if not p:
+            act(ap("WB"), ap("pQ", 0, 64), F.Identity)
     if last:
-        o = ap("pQ", 256, 256 + n, 1, 0, 8)
+        o = ap("pQ", 320, 320 + n, 1, 0, 8)
         mm([(o, ap("G8"), ap("MN", a, b)), (o, ap("G8"), ap("MN", b, c_))])
         act(ap("YQ", t0, t0 + n, 1, 0, 8), o, F.Identity)
-    else:
-        act(sl("NW", 8 * p, 8 * p + 8), sl("ZA", z0 + 15, z0 + 143, 16), F.Relu, bias=-46.0)
+    c, c2 = 32 * (s % 2) + 8 * p, 144 * (s % 2)
+    if not last or not p:
+        act(sl("NW", c, c + 8) if p else sl("NL", c2 + 15, c2 + 143, 16), sl(za, z0 + 15, z0 + 143, 16), F.Relu,
+            bias=4096.0 * (shift - 46.0), scale=4096.0)
 
 
-def learn(s, p, n, ui, lo):
-    t0, m, c = 64 * p, n // 16, lo // 16
+def learn(s, n):
     def sl(name, a, b, st=1):
-        return ap(name, a, b, st, 0, n)
-    c0, k0 = 384 * p, 24 * p
-    ts(sl("K64", 0, 8), sl("KI", k0, k0 + 8), 64, A.bitwise_and)
-    tt(sl("ZJ", 15, 143, 16), sl("KC6", k0 + 16, k0 + 24), sl("K64", 0, 8), A.add)
-    cw, i3 = ("CW8", "I3") if n == 128 else ("CW4", "I3H")
-    mm([(ap("pW", 64, 64 + 3 * m), ap("I3", 0, 128), ap(cw + "L"))] + spread(ap("pW", 64, 64 + 2 * m), "ZA", 256 * (ui % 2) + 128, i3, n, 2)
-       + spread(ap("pW", 64 + 2 * m, 64 + 3 * m), "ZJ", 0, i3, n, 1))
-    cp(ap("OL", 0, 3 * m), ap("pW", 64, 64 + 3 * m))
-    ts(ap("V12", 8, 12), ap("pW", 64 + 2 * m + c, 64 + 2 * m + c + 4), 880.0, A.is_lt)
-    a, b = 2 * t0 + lo, 2 * t0 + n + lo
+        return ap(name, a, b, st, 0, 64)
+    ts(sl("K64", 0, 8), sl("KI", 0, 8), 64, A.bitwise_and)
+    tt(sl("ZJ", 15, 143, 16), sl("KC6", 16, 24), sl("K64", 0, 8), A.add)
+    ol = [mm([(ap("pL", c, c + 8), ap("I3", 0, 128), ap("CT", 8 + 2 * c, 24 + 2 * c, 2))]
+             + spread(ap("pL", c, c + 8), z, z0, "I3H", 16 * c, 128, 64)) for c, z, z0 in ((0, "ZL", 128), (8, "ZJ", 0))]
+    ts(ap("OL", 0, 8), ap("pL", 0, 8), -1.0, A.add)
+    ts(ap("OL", 8, 12), ap("pL", 8, 12), -1.0, A.add)
+    tt(ap("SC2", 143, 192, 16), ap("pL", 12, 16), ap("I3I", 48 * s, 48 * s + 4), A.max)
+    a = 512 * (s % 2)
     if n == 64:
         tt(ap("ML"), ind(ap("OH"), ap("OL", 0, 8)), ap("NM", a, a + 128), A.mult)
     else:
-        tt(ap("ML", 0, 64), ind(ap("OH"), ap("OL", c, c + 4)), ap("NM", a, a + 64), A.mult)
-        tt(ap("ML", 64, 128), ind(ap("OH"), ap("OL", m + c, m + c + 4)), ap("NM", b, b + 64), A.mult)
-    mm([(ap("pQ", 128, 192), ap("GB"), ap("ML", 0, 64)), (ap("pQ", 128, 192), ap("GB"), ap("ML", 64, 128))])
-    tt(ap("LM", 64, 128), ap("pQ", 128, 192), ap("M0"), A.subtract)
-    scan(ap("SC2"), ap("MK", 0, 128), ap("LM"), 0.0, A.add, A.max)
-    tt(ap("DN"), ap("V12"), ap("DUM"), A.mult)
-    tt(ap("VP", 8, 12), ap("I3I", 12 * p + c, 12 * p + c + 4), ap("DN", 8, 12), A.max)
-    tt(ap("VP", 0, 8), ap("SC2", 15, 128, 16), ap("DN", 0, 8), A.max)
-    cp(ap("OV"), ap("VP"))
-    lin(ap("NB"), ap("VP"), -float(2 ** 20))
-    tt(ap("VT"), ap("VP"), ap("TW"), A.add)
-    tt(ap("U"), ind(ap("IOT"), ap("OV")), ap("TF"), A.add)
-    for k in range(12):
-        act(ap("DD", 64 * k, 64 * k + 64), ap("U", 64 * (k // 4), 64 * (k // 4) + 64), F.Abs, bias=ap("NB", k, k + 1), scale=float(2 ** 20))
-    scan(ap("DS"), ap("M64"), ap("DD"), 0.0, A.add, A.min)
-    tt(ap("KP"), ap("VT"), ap("DS", 63, 768, 64), A.subtract)
-    tt(ap("VQ"), ap("KP"), ap("DUM"), A.min)
-    cp(ap("OK%d" % s), ap("VQ"))
+        tt(ap("ML", 0, 64), ind(ap("OH"), ap("OL", 0, 4)), ap("NM", a, a + 64), A.mult)
+        tt(ap("ML", 64, 128), ind(ap("OH"), ap("OL", 4, 8)), ap("NM", a + n, a + n + 64), A.mult)
+    g, c2 = "L%d" % s, 144 * (s % 2)
+    mm([(ap("pL", 128, 256), ap("I3", 0, 128), ap("M0"))], True, g, ol)
+    mm([(ap("pL", 128 + r, 256, 16), ap("NL", c2 + 15 - r, c2 + 143 - r, 1, 0, 64), ap("I3H", 256 + r, 384, 16, 0, 64))
+        for r in range(16)], False, g)
+    mm([(ap("pL", 192, 256), ap("GB"), ap("MN", 0, 64)), (ap("pL", 192, 256), ap("GB"), ap("MN", n, n + 64))], False, g)
+    mm([(ap("pL", 128, 192), ap("GB"), ap("ML", 0, 64)), (ap("pL", 128, 192), ap("GB"), ap("ML", 64, 128))], False, g)
+    scan(ap("SC2", 0, 128), ap("MK", 0, 128), ap("pL", 128, 256), 0.0, A.add, A.max)
+    for a, b in LISTS[s]:
+        tt(ap("VP", a, b), ap("SC2", 16 * a + 15, 16 * b, 16), ap("DUM", a, b), A.min)
+        cp(ap("OV", a, b), ap("VP", a, b))
+        tt(ap("VT", a, b), ap("VP", a, b), ap("TW", a, b), A.add)
+        tt(ap("U", 16 * a, 16 * b), ind(ap("IOT"), ap("OV", a, b)), ap("TF", 16 * a, 16 * b), A.add)
+        for k in range(a, b):
+            act(ap("DD", 65 * k, 65 * k + 64), ap("U", 64 * (k // 4), 64 * (k // 4) + 64), F.Abs, bias=ap("VP", k, k + 1),
+                scale=-1.0 / 128)
+        scan(ap("DS", 65 * a, 65 * b), ap("M65", 65 * a, 65 * b), ap("DD", 65 * a, 65 * b), 1.0, A.mult, A.min)
+        tt(ap("KP", a, b), ap("VT", a, b), ap("DS", 65 * a + 64, 65 * b, 65), A.subtract)
+        tt(ap("VQ", a, b), ap("KP", a, b), ap("DUM", a, b), A.min)
+        cp(ap("OK%d" % s, a, b), ap("VQ", a, b))
     X = ap("X%d" % (s % 2))
-    tt(ap("T1"), ind(X, ap("OV", 0, 4)), ap("Z%d" % s, t0 + lo, t0 + lo + 64), A.add)
-    ts(ap("T2"), ap("T1"), col(VS), A.mult, col(VB), A.add)
-    ts(ap("T3"), ap("T2"), 1, A.arith_shift_right)
-    ts(ap("XW%d" % s), ap("T3"), col(VMIN), A.min)
-    ts(ap("XL%d" % s), ind(X, ap("OV", 4, 8)), col(IS15), A.subtract, 0.0, A.max)
+    tt(ap("T1"), ind(X, ap("OV", 4, 8)), ap("Z%d" % s, 0, 64), A.add)
+    if TS:
+        lin(ap("T3"), ap("T1"), col(VS), col(VB))
+        ts(ap("XW%d" % s), ap("T3"), ROUND, A.subtract, col(VMIN), A.min)
+        act(ap("XL%d" % s), ind(X, ap("OV", 0, 4)), F.Relu, bias=col(NI15))
+    else:
+        ts(ap("T2"), ap("T1"), col(VS), A.mult, col(VB), A.add)
+        ts(ap("XW%d" % s), ap("T2"), col(VMIN), A.min)
+        ts(ap("XL%d" % s), ind(X, ap("OV", 0, 4)), col(IS15), A.subtract, 0.0, A.max)
     tt(ap("F1"), ind(ap("FW"), ap("OV", 8, 12)), ap("WB"), A.subtract)
-    tt(ap("F2"), ind(ap("OH"), ap("OL", 2 * m + c, 2 * m + c + 4)), ap("F1"), A.mult)
+    tt(ap("F2"), ind(ap("OH"), ap("OL", 8, 12)), ap("F1"), A.mult)
     tt(ind(ap("FW"), ap("OK%d" % s, 8, 12)), ap("F2"), ap("WB"), A.add)
 
 
 def update(s, x):
-    cp(ind(ap("X%d" % x), ap("OK%d" % s, 4, 8)), ap("XL%d" % s))
-    cp(ind(ap("X%d" % x), ap("OK%d" % s, 0, 4)), ap("XW%d" % s))
+    cp(ind(ap("X%d" % x), ap("OK%d" % s, 0, 4)), ap("XL%d" % s))
+    cp(ind(ap("X%d" % x), ap("OK%d" % s, 4, 8)), ap("XW%d" % s))
 
 
-def runs(u, p, nxt):
+def runs(u, p, nxt, blocks=True):
     out = []
     for k, h in enumerate(u):
         q = nxt.index(h)
-        if out and out[-1][3] == h // 2 and out[-1][1] + out[-1][2] == q:
+        if out and (out[-1][3] == h // 2 or not blocks) and out[-1][1] + out[-1][2] == q:
             out[-1] = (out[-1][0], out[-1][1], out[-1][2] + 1, out[-1][3])
         else:
             out.append((p + k, q, 1, h // 2))
@@ -531,37 +579,33 @@ def runs(u, p, nxt):
 
 def program():
     setup()
-    ui = 0
     for s in range(RO):
-        limit(s)
-        p = 0
-        for u, nv in zip(UNITS[s], VSH[s]):
-            front(s, p, 64 * len(u), nv)
-            p += len(u)
-        p = 0
+        places = [sum(len(u) for u, md in UNITS[s][:k]) for k in range(len(UNITS[s]))]
+        sizes = [64 * len(u) for u, md in UNITS[s]]
+        if s == 0:
+            front(s, 0, 256, list(zip(places, sizes)))
+        else:
+            for p, n in zip(places, sizes):
+                front(s, p, n, [(p, n)])
         last = s == RO - 1
-        nxt = [0, 1, 2, 3] if last else [h for u in UNITS[s + 1] for h in u]
-        for u, nv in zip(UNITS[s], VSH[s]):
-            n = 64 * len(u)
-            lo = 64 * u.index(s) if s in u else None
-            bulk(s, p, n, nv)
-            tail(s, p, n, nv, ui, lo)
-            for (a, q, k, b) in runs(u, p, nxt):
+        nxt = [0, 1, 2, 3] if last else [h for u, md in UNITS[s + 1] for h in u]
+        for (u, md), p, n in zip(UNITS[s], places, sizes):
+            bulk(s, p, md)
+            tail(s, p, md)
+            for (a, q, k, b) in runs(u, p, nxt, not last):
                 sa, sb, da, db = 64 * a, 64 * (a + k), 64 * q, 64 * (q + k)
                 if last:
-                    dma("Y", [], [ap("ZN2", sa, sb)], lambda T, sa=sa, sb=sb, da=da, db=db: (T.yz[:, da:db], T.ZN2[:, sa:sb]), 32768)
-                    dma("Y", [], [ap("YQ", sa, sb)], lambda T, sa=sa, sb=sb, da=da, db=db: (T.yq[:, da:db], T.YQ[0:8, sa:sb]), 4096)
+                    dma([], [ap("ZN2", sa, sb)], lambda T, sa=sa, sb=sb, da=da, db=db: (T.yz[:, da:db], T.ZN2[:, sa:sb]), 65536)
+                    dma([], [ap("YQ", sa, sb)], lambda T, sa=sa, sb=sb, da=da, db=db: (T.yq[:, da:db], T.YQ[0:8, sa:sb]), 4096)
                 else:
                     send(ap("ZN%d" % s, sa, sb), ap("Z%d" % (s + 1), da, db), 1 + b + s)
                     send(ap("QN%d" % s, sa, sb), ap("Q%d" % (s + 1), da, db), 1 + b + s)
-            if lo is not None:
-                learn(s, p, n, ui, lo)
+            if p == 0:
+                learn(s, n)
                 update(s, (s + 1) % 2)
                 if last:
-                    dma("Y", [], [ap("X1")], lambda T: (T.yx[:], T.X1[:, 0:W]), 2 ** 20)
-                    dma("Y", [], [ap("FW")], lambda T: (T.yf[:], T.FW[:, 0:1024]), 2 ** 19)
-            p += len(u)
-            ui += 1
+                    i = dma([], [ap("FW")], lambda T: (T.yf[:], T.FW[:, 0:1024]), 2 ** 19)
+                    dma([], [ap("X1")], lambda T: (T.yx[:], T.X1[:, 0:W]), 2 ** 20, i)
         if not last:
             update(s, s % 2)
 
@@ -576,127 +620,280 @@ def meet(a, b):
 
 
 def depend():
-    hist = {}
+    hist, head = {}, {}
     for i, o in enumerate(OPS):
         d = set(o["after"])
-        for x, w in [(x, False) for x in o["rd"]] + [(x, True) for x in o["wr"]]:
-            ps = SCRATCH[x[0]][0] == "psum"
-            for (j, y, wj) in hist.get(x[0], []):
-                if j == i:
-                    continue
-                if ps:
-                    if OPS[j]["eng"] != o["eng"] or o["eng"] == "P":
-                        d.add(j)
-                elif (w or wj) and meet(x, y):
+        g = o["grp"]
+        if g is not None and head.setdefault(g, i) != i:
+            d.add(head[g])
+        use = [(x, False) for x in o["rd"]] + [(x, True) for x in o["wr"]]
+        for x, w in use:
+            for j, y, wj in hist.get(x[0], []):
+                if (w or wj) and (g is None or OPS[j]["grp"] != g) and meet(x, y):
                     d.add(j)
-        for x, w in [(x, False) for x in o["rd"]] + [(x, True) for x in o["wr"]]:
+        for x, w in use:
             hist.setdefault(x[0], []).append((i, x, w))
+        o["true"] = d
+        names = set(x[0] for x, w in use)
+        o["shared"] = sorted(names & set(["pH", "pL", "pQ"]))
+        o["diff"] = ([x for x in names if x[:3] == "pD#"] + [None])[0]
+
+
+def reduce_deps(order, extra):
+    reach = [0] * len(OPS)
+    for i in order:
+        dep = OPS[i]["true"] | extra.get(i, set())
         cover = 0
-        for j in d:
-            cover |= OPS[j]["reach"]
-        o["dep"] = sorted(j for j in d if not cover >> j & 1)
-        o["reach"] = 0 if o["eng"] == "R" else cover | sum(1 << j for j in d if not cover >> j & 1)
+        for j in dep:
+            cover |= reach[j]
+        OPS[i]["dep"] = sorted(j for j in dep if not cover >> j & 1)
+        reach[i] = 0 if OPS[i]["eng"] == "R" else cover | sum(1 << j for j in OPS[i]["dep"])
 
 
 def prices(m):
     cost = [o["c"][0] + (o["c"][1] + o["c"][2] * m[1] + o["c"][3] * m[2]) * m[0] + o["c"][4] * m[3]
-            + (m[6] if o["eng"] in "VS" else 0.0) for o in OPS]
-    lat = [o["lat"] * (m[7] if o["eng"] == "R" else m[5]) for o in OPS]
-    pred = [[(j, lat[j] + (0.0 if "R" in (o["eng"], OPS[j]["eng"]) or o["eng"] + OPS[j]["eng"] == "PP" else m[4]))
+            + (m[5] if o["eng"] in "VS" else 0.0) for o in OPS]
+    cost = [o["lat"] / m[7] if o["eng"] == "E" else c for o, c in zip(OPS, cost)]
+    lat = [m[8] if o["eng"] == "R" else (m[6] if o["eng"] == "D" else 0.0) for o in OPS]
+    pred = [[(j, lat[j] + (0.0 if o["eng"] in "RDE" or o["eng"] + OPS[j]["eng"] in ("PP", "YY") else m[4]))
              for j in o["dep"]] for o in OPS]
-    return cost, pred, lat
+    return cost, pred, lat, m[4]
 
 
-def place(seq, cost, pred, rel):
+def slot(iv, t, c):
+    k = len(iv)
+    while k > 0 and iv[k - 1][1] > t:
+        k -= 1
+    while k < len(iv) and iv[k][0] < t + c:
+        t = max(t, iv[k][1])
+        k += 1
+    iv.insert(k, (t, t + c))
+    return t
+
+
+def place(seq, cost, pred, rel, wait=None):
     t0 = [0.0] * len(OPS)
-    gaps = {}
-    for i in seq:
+    gaps = {"V": [], "S": [], "P": [], "G": [], "Y": []}
+    free = [(0.0, b, None) for b in range(ND)]
+    held, edge = {}, {}
+    done = [False] * len(OPS)
+    late = []
+    todo = list(seq)[::-1]
+    while todo:
+        i = todo.pop()
+        u = DIFF[i] if wait is not None else None
         t = rel[i]
+        ok = not (u and ENG[i] == "P" and not free)
         for j, d in pred[i]:
+            if not done[j]:
+                ok = False
+                break
             x = t0[j] + cost[j] + d
             if x > t:
                 t = x
-        e = OPS[i]["eng"]
-        if e != "R":
-            iv = gaps.setdefault(e, [])
-            k = len(iv)
-            while k > 0 and iv[k - 1][1] > t:
-                k -= 1
-            c = cost[i]
-            while k < len(iv) and iv[k][0] < t + c:
-                t = max(t, iv[k][1])
-                k += 1
-            iv.insert(k, (t, t + c))
+        if not ok:
+            late.append(i)
+            continue
+        if u and ENG[i] == "P":
+            f = min(free)
+            free.remove(f)
+            held[u] = f[1]
+            edge[i] = f[2]
+            t = max(t, f[0])
+        if ENG[i] in gaps:
+            t = slot(gaps[ENG[i]], t, cost[i])
         t0[i] = t
+        done[i] = True
+        if u and ENG[i] != "P":
+            free.append((t + cost[i] + wait, held[u], i))
+            todo.extend(late[::-1])
+            late = []
     return t0
 
 
-def replay(order, cost, pred, lat):
-    t0 = [0.0] * len(OPS)
-    free = {}
+def rotate(order):
+    free = [(b, None) for b in range(ND)]
+    held, edge = {}, {}
     for i in order:
-        e = OPS[i]["eng"]
-        t = free.get(e, 0.0)
+        u = DIFF[i]
+        if u:
+            if ENG[i] != "P":
+                free.append((held[u], i))
+            elif not free:
+                return None, None
+            else:
+                held[u], edge[i] = free.pop(0)
+    return held, edge
+
+
+def replay(order, edge, cost, pred, lat, wait, a=0, old=None, last=None):
+    fin = list(old[1]) if old else [0.0] * len(OPS)
+    why = list(old[2]) if old else [None] * len(OPS)
+    last = list(last or [None] * 16)
+    for i in order[a:]:
+        t, w = 0.0, None
+        for q, d in AFTER[i]:
+            j = last[q]
+            if j is not None and fin[j] + d * wait > t:
+                t, w = fin[j] + d * wait, j
         for j, d in pred[i]:
-            x = t0[j] + cost[j] + d
-            if x > t:
-                t = x
-        t0[i] = t
-        if e != "R":
-            free[e] = t + cost[i]
-    return max(t0[i] + cost[i] + lat[i] for i in order), t0
+            if fin[j] + d > t:
+                t, w = fin[j] + d, j
+        j = edge.get(i)
+        if j is not None and fin[j] + wait > t:
+            t, w = fin[j] + wait, j
+        t += cost[i]
+        fin[i] = t
+        why[i] = w
+        for q in MARK[i]:
+            last[q] = i
+    end, top = max((fin[i] + lat[i], i) for i in SINK)
+    return end, fin, why, top
 
 
-def schedule(seed, rounds, tries=0):
+ENG, DIFF, AFTER, MARK, SINK = [], [], [], [], []
+
+
+def schedule(seed, rounds, tries, moves):
     n = len(OPS)
+    ENG[:] = [o["eng"] for o in OPS]
+    DIFF[:] = [o["diff"] for o in OPS]
+    slots = dict((x, k) for k, x in enumerate(list("VSPGY") + [b + e for b in ("pH", "pL", "pQ") for e in "VSP"]))
+    MARK[:] = [[slots[x] for x in [o["eng"]] + [b + o["eng"] for b in o["shared"]] if x in slots] for o in OPS]
+    AFTER[:] = [([(slots[o["eng"]], 0)] if o["eng"] in slots else [])
+                + [(slots[b + e], 1) for b in o["shared"] for e in "VSP" if e != o["eng"]] for o in OPS]
+    reduce_deps(range(n), {})
+    anc = [0] * n
+    for i in range(n):
+        for j in OPS[i]["true"]:
+            anc[i] |= anc[j] | 1 << j
+    rnd = np.random.RandomState(seed)
     pr = [prices(m) for m in GUESS]
-    cost, pred, lat = pr[0]
+    cost, pred, lat, wait = pr[0]
     succ = [[] for _ in OPS]
     for i in range(n):
         for j, d in pred[i]:
             succ[j].append((i, d))
-    rnd = np.random.RandomState(seed)
     zero = [0.0] * n
-    best, base = None, None
-    t0 = place(range(n), cost, pred, zero)
-    for k in range(rounds):
-        c2 = [c * (1 + 0.25 * x) for c, x in zip(cost, rnd.rand(n))] if k % 3 == 2 else cost
-        back = place(sorted(range(n), key=lambda i: (-(t0[i] + cost[i]), -i)), c2, succ, lat)
-        t0 = place(sorted(range(n), key=lambda i: (-(back[i] + c2[i]), i)), cost, pred, zero)
-        order = sorted(range(n), key=lambda i: (t0[i], i))
-        ends = [replay(order, *p)[0] for p in pr]
-        base = base or ends
-        score = sum(a / b for a, b in zip(ends, base))
-        if best is None or score < best[0]:
-            best = (score, order, ends, t0)
-        elif k % 3 == 1:
-            t0 = best[3]
-    t0 = replay(best[1], *pr[0])[1]
-    for k in range(tries):
-        a, w, sg = rnd.rand() * best[2][0], [3e3, 8e3, 20e3][rnd.randint(3)], [300.0, 1000.0, 3000.0][rnd.randint(3)]
-        key = [t + z if a < t < a + w else t for t, z in zip(t0, (rnd.randn(n) * sg).tolist())]
+    base = [sum(p[0]) / 3.0 for p in pr]
+
+    SINK[:] = [i for i in range(n) if not succ[i]]
+
+    def judge(order, a=0, old=None):
+        held, edge = rotate(order)
+        if edge is None:
+            return (1e9, order, None)
+        last = [None] * 16
+        for i in order[:a]:
+            for q in MARK[i]:
+                last[q] = i
+        res = [replay(order, edge, *p, a, old and old[k], last) for k, p in enumerate(pr)]
+        return (sum((r[0] + SMOOTH * sum(r[1]) / n) / b for r, b in zip(res, base)) / len(pr), order, res)
+
+    def settle(key, m):
+        key = list(key)
         for i in range(n):
             for j, d in pred[i]:
                 if key[j] >= key[i]:
                     key[i] = key[j] + 1e-3
-        m = pr[rnd.randint(len(pr))] if rnd.rand() < 0.3 else pr[0]
-        t1 = place(sorted(range(n), key=lambda i: (key[i], i)), m[0], m[1], zero)
-        order = sorted(range(n), key=lambda i: (t1[i], i))
-        ends = [replay(order, *p)[0] for p in pr]
-        score = sum(a / b for a, b in zip(ends, base))
-        if score < best[0]:
-            best = (score, order, ends)
-            t0 = replay(order, *pr[0])[1]
-    return best[1], best[2]
+        t1 = place(sorted(range(n), key=lambda i: key[i]), m[0], m[1], zero, m[3])
+        return judge(sorted(range(n), key=lambda i: (t1[i], i)))
+
+    best = cur = settle(range(n), pr[0])
+    for k in range(rounds):
+        c2 = [c * (1 + 0.25 * x) for c, x in zip(cost, rnd.rand(n))] if k % 3 == 2 else cost
+        back = place(sorted(range(n), key=lambda i: (-cur[2][0][1][i], -i)), c2, succ, lat)
+        new = settle([-(back[i] + c2[i]) for i in range(n)], pr[0])
+        cur = new if new[2] else best
+        if cur[0] < best[0]:
+            best = cur
+        elif k % 3 == 1:
+            cur = best
+    for k in range(tries):
+        a, w, sg = rnd.rand() * best[2][0][0], [3e3, 8e3, 20e3][rnd.randint(3)], [300.0, 1000.0, 3000.0][rnd.randint(3)]
+        key = [t - c + z if a < t < a + w else t - c for t, c, z in zip(best[2][0][1], cost, (rnd.randn(n) * sg).tolist())]
+        new = settle(key, pr[rnd.randint(len(pr))] if rnd.rand() < 0.3 else pr[0])
+        if new[0] < best[0]:
+            best = new
+    cur = best
+    for k in range(moves):
+        order = cur[1]
+        end, fin, why, i = cur[2][rnd.randint(len(pr))]
+        if rnd.rand() < FILL:
+            a = rnd.randint(n)
+            j = order[a]
+            if why[j] is None or not anc[j] >> why[j] & 1 or ENG[j] not in "VSP":
+                continue
+            later = [x for x in order[a + 1:a + 60] if ENG[x] == ENG[j] and not anc[x] >> j & 1][:8]
+            if not later:
+                continue
+            i = later[rnd.randint(len(later))]
+            b = order.index(i) + 1
+            seg = order[a:b]
+            new = [x for x in seg if anc[i] >> x & 1] + [i] + [x for x in seg[:-1] if not anc[i] >> x & 1]
+            new = judge(order[:a] + new + order[b:], a, cur[2])
+            if new[0] < cur[0] - HEAT * (1 - k / moves) * np.log(rnd.rand() + 1e-12):
+                cur = new
+                if cur[0] < best[0]:
+                    best = cur
+            continue
+        if rnd.rand() < 0.3:
+            i = order[rnd.randint(n)]
+        pairs = []
+        while why[i] is not None:
+            if not anc[i] >> why[i] & 1:
+                pairs.append((why[i], i))
+            i = why[i]
+        if not pairs:
+            continue
+        j, i = pairs[rnd.randint(len(pairs))]
+        a, b = order.index(j), order.index(i) + 1
+        far = int(rnd.rand() ** 3 * 40)
+        if rnd.rand() < 0.5:
+            a = max(0, a - far)
+            seg = order[a:b]
+            new = [x for x in seg if anc[i] >> x & 1] + [i] + [x for x in seg[:-1] if not anc[i] >> x & 1]
+        else:
+            b = min(n, b + far)
+            seg = order[a:b]
+            new = [x for x in seg[1:] if not anc[x] >> j & 1] + [j] + [x for x in seg if anc[x] >> j & 1]
+        new = judge(order[:a] + new + order[b:], a, cur[2])
+        if new[0] < cur[0] - HEAT * (1 - k / moves) * np.log(rnd.rand() + 1e-12):
+            cur = new
+            if cur[0] < best[0]:
+                best = cur
+    return best
+
+
+SMOOTH = 0.3
+HEAT = 0.0004
+FILL = 0.5
 
 
 def build():
     del OPS[:]
     del SEMAPHORES[5:]
-    DB[0] = 0
+    del KEYS[:]
+    TURN[:] = [0, 0]
     program()
     depend()
-    return schedule(*SEEDS)
+    score, order, res = schedule(*SEEDS)
+    ends = [r[0] for r in res]
+    held, edge = rotate(order)
+    extra = dict((i, set([j])) for i, j in edge.items() if j is not None)
+    for u, b in held.items():
+        BANK[u] = "pD%d" % b
+    hist, last = {}, {}
+    for i in order:
+        for b in OPS[i]["shared"]:
+            extra.setdefault(i, set()).update(j for j in hist.get(b, []) if ENG[j] != ENG[i])
+            hist.setdefault(b, []).append(i)
+        if OPS[i]["grp"] is not None:
+            last[OPS[i]["grp"]] = i
+    for i in last.values():
+        OPS[i]["stop"] = True
+    reduce_deps(order, extra)
+    return order, ends
 
 
 ORDER, EST = build()
@@ -715,8 +912,10 @@ def rank_program(g, core, T, topo):
         o = OPS[i]
         e = o["eng"]
         if e == "R":
-            src = T.cores[(rank - o["val"][1]) % NR]
-            done[i] = (o["sem"], len(topo.engines(src, core)))
+            done[i] = (o["sem"], len(topo.engines(T.cores[(rank - o["val"]) % NR], core)))
+            continue
+        if e in "DE":
+            done[i] = (o["sem"], o["val"]) if e == "D" else None
             continue
         need = {}
         for j in o["dep"]:
@@ -728,15 +927,11 @@ def rank_program(g, core, T, topo):
                 queue[e].wait_ge(T.sem[sem], v)
                 seen[(e, sem)] = v
         ins = o["fn"](g, T, r)
-        if o["sem"] is not None:
-            done[i] = (o["sem"], o["val"])
-        elif ins:
-            for x in ins:
-                x.then_inc(T.sem["c" + e], 1)
+        for x in ins:
+            x.then_inc(T.sem["c" + e], 1)
+        if ins:
             count["c" + e] += len(ins)
-            done[i] = ("c" + e, count["c" + e])
-        else:
-            done[i] = None
+        done[i] = ("c" + e, count["c" + e]) if ins else None
     final = dict(count)
     final["ls"] = r["ls"]
     for i in ORDER:

@@ -4,21 +4,33 @@ from concourse.mybir import AluOpType, ActivationFunctionType
 A = AluOpType
 F = ActivationFunctionType
 NR, W, RO = 4, 4096, 3
-UNITS = [[((0, 1), "SSVV"), ((2, 3), "SSSM")],
-         [((1, 0), "SSVV"), ((2, 3), "SSSM")],
-         [((2,), "SV"), ((0, 1), "SSSM"), ((3,), "SV")]]
+UNITS = [[((0, 1), "SSVV"), ((2, 3), "SSMV")],
+         [((1, 0), "SSVV"), ((2, 3), "SSMV")],
+         [((2,), "VV"), ((1, 0), "SSSM"), ((3,), "SM")]]
+PLACE = [[0, 1, 2, 3], [1, 0, 2, 3], [2, 3, 1, 0]]
+MODE = {"S": "SS", "V": "VV", "M": "SV", "N": "VS", "H": "HH", "J": "SH", "K": "HV", "L": "VH"}
 LISTS = [[(0, 12)], [(0, 12)], [(8, 12), (0, 8)]]
 GV = 32
 GS = 64
-NZ = 64
+NZ = 0
 ZV = 688
-IOS = 0
-TS = 0
-QS = 1
+IOS = 4
+TS = 1
+US = 1
+DS_ = "lwk"
+OLS = 1
+ZG = 0
+F0 = 1
+SP3 = 0
+PL = 1
+DW = 32
+ZP = [(0, 0), (0, 2), (1, 0), (1, 2), (2, 0), (2, 1), (2, 2), (2, 3), (1, 1), (1, 3)]
+PS = ZP[2:]
+QS = 3
 GC = 1
 SL = 64
 ROUND = 1.5 * 2 ** 23
-ND = 3
+ND = 4
 BIG = float(2 ** 26)
 HUGE = float(2 ** 31)
 MAGIC = 1.5 * 2 ** 29
@@ -27,10 +39,13 @@ SCRATCH = {}
 SEMAPHORES = ["cV", "cS", "cP", "cG", "ls"]
 OPS = []
 BANK = {}
-SEEDS = (3, 12, 50, 75000)
-GUESS = [(0.9, 1.56, 3.8, 0.46, 100.0, 20.0, 1500.0, 250.0, 2500.0), (0.83, 1.3, 3.0, 0.42, 200.0, 0.0, 2000.0, 200.0, 4000.0),
-         (1.0, 1.56, 3.8, 0.5, 60.0, 40.0, 1200.0, 350.0, 2000.0), (1.2, 1.9, 5.0, 0.6, 150.0, 20.0, 2000.0, 200.0, 4500.0),
-         (1.1, 1.3, 3.0, 0.55, 100.0, 10.0, 1500.0, 300.0, 3000.0)]
+SEEDS = (4, 150, 1500, 48000)
+GUESS = [(0.9, 1.56, 3.8, 0.46, 100.0, 20.0, 1500.0, 300.0, 2500.0, 1000.0),
+         (0.83, 1.3, 3.0, 0.42, 180.0, 0.0, 1200.0, 500.0, 2000.0, 1000.0),
+         (0.85, 1.3, 3.0, 0.43, 150.0, 0.0, 2000.0, 220.0, 4500.0, 2000.0),
+         (1.0, 1.56, 3.8, 0.5, 60.0, 40.0, 1000.0, 600.0, 2000.0, 500.0),
+         (1.2, 1.9, 5.0, 0.6, 130.0, 20.0, 1800.0, 250.0, 4500.0, 2000.0),
+         (1.15, 1.3, 3.0, 0.58, 80.0, 10.0, 1300.0, 400.0, 3000.0, 1500.0)]
 
 
 def buf(name, cols, dtype, where="sbuf"):
@@ -39,14 +54,14 @@ def buf(name, cols, dtype, where="sbuf"):
 
 for _n, _c, _d in [
         ("X0", 4160, "bfloat16"), ("X1", 4160, "bfloat16"), ("fwi", 1024, "int32"), ("FW", 1088, "float32"),
-        ("swi", 512, "int32"), ("SP", 512, "float32"), ("awi", 512, "int32"), ("RT0", 512, "int32"), ("RT", 512, "int32"),
+        ("swi", 512, "int32"), ("SP", 512, "float32"), ("AWF", 512, "float32"), ("awi", 512, "int32"), ("RT0", 512, "int32"), ("RT", 512, "int32"),
         ("zin", 256, "bfloat16"), ("hwi", 1, "int32"), ("thi", 8, "int32"), ("qi", 256, "int32"), ("qf", 256, "float32"),
         ("Z0", 256, "bfloat16"), ("Z1", 256, "bfloat16"), ("Z2", 256, "bfloat16"),
         ("Q0", 256, "float32"), ("Q1", 256, "float32"), ("Q2", 256, "float32"),
         ("ZN0", 256, "bfloat16"), ("ZN1", 256, "bfloat16"), ("ZN2", 256, "bfloat16"),
         ("QN0", 256, "float32"), ("QN1", 256, "float32"), ("YQ", 256, "float32"),
         ("B", 256 * 48, "bfloat16"), ("RS", 4096, "bfloat16"), ("RC", 4096, "bfloat16"), ("LS", 4096, "bfloat16"),
-        ("LC", 4096, "bfloat16"), ("ZR", 4096, "bfloat16"), ("IOT", 4160, "float32"), ("IO", 112, "float32"),
+        ("LC", 4096, "bfloat16"), ("ZR", 4096, "bfloat16"), ("IOT", 1088, "float32"), ("IO", 112, "float32"),
         ("UI", 48, "int32"), ("I3I", 144, "int32"), ("O3", 144, "uint16"), ("N1", 512, "int32"), ("PP", 256, "float32"),
         ("AP1", 256, "float32"), ("NM", 1024, "int32"), ("ON", 1024, "uint16"), ("SC", 4 * 288, "float32"), ("SL", 408, "float32"),
         ("KI", 24, "int32"), ("KC6", 24, "int32"), ("K64", 8, "int32"), ("NW", 8 * 8, "bfloat16"),
@@ -57,17 +72,20 @@ for _n, _c, _d in [
         ("T1", 64, "float32"), ("T2", 64, "int32"), ("XW0", 64, "bfloat16"), ("XW1", 64, "bfloat16"),
         ("XW2", 64, "bfloat16"), ("XL0", 64, "bfloat16"), ("XL1", 64, "bfloat16"), ("XL2", 64, "bfloat16"),
         ("F1", 64, "float32"), ("F2", 64, "float32"), ("TH4", 8, "float32"),
-        ("ONE", 384, "bfloat16"), ("ONF", 128, "float32"), ("I3", 384, "bfloat16"),
-        ("I3H", 384, "bfloat16"), ("PI", 4, "int32"), ("CF", 16, "float32"),
+        ("ONE", 384, "bfloat16"), ("ONF", 128, "float32"), ("I3", 128, "bfloat16"), ("I2", 128, "bfloat16"),
+        ("LN", 144, "bfloat16"), ("STM", 144, "bfloat16"), ("RB8", 48, "bfloat16"), ("RB4", 32, "bfloat16"),
+        ("LB", 848, "bfloat16"), ("WRB8", 384, "bfloat16"), ("WRB4", 256, "bfloat16"), ("PI", 4, "int32"), ("CF", 16, "float32"),
         ("I48", 768, "bfloat16"), ("OH", 928, "bfloat16"), ("G8", 8, "float32"), ("WR", 24, "bfloat16"),
         ("IG", 128, "float32"), ("GB", 128, "float32"), ("G8T", 128, "float32"), ("IM", 128, "float32"), ("MO", 128, "float32"),
         ("M0", 128, "bfloat16"), ("CT", 40, "bfloat16"), ("CR", 8, "bfloat16"), ("TW", 12, "float32"), ("DUM", 12, "float32"),
         ("TF", 192, "float32"), ("KC36", 288, "bfloat16"), ("KC51", 408, "bfloat16"),
-        ("M36", 288, "bfloat16"), ("M51", 408, "bfloat16"), ("M65", 780, "bfloat16"), ("T3", 64, "float32"),
+        ("M36", 288, "bfloat16"), ("M51", 408, "bfloat16"), ("M64", 768, "bfloat16"), ("T3", 64, "float32"), ("NB", 12, "float32"),
         ("ZT", 512, "bfloat16"), ("I16", 512, "bfloat16"), ("EX", 512, "bfloat16")]:
     buf(_n, _c, _d)
-for _n in ["pH", "pK0", "pK1", "pL", "pQ", "pD0", "pD1", "pD2"]:
+for _n in ["pH", "pK0", "pK1", "pQ"] + ([] if PL else ["pL"]):
     buf(_n, 512, "float32", "psum")
+for _n in range(ND):
+    buf("pD%d" % _n, 16 * DW, "float32", "psum")
 PART = {}
 for _n, _c in [("HZ", 144), ("WS", 32), ("MK", 16 * SL), ("ZS", 16 * NZ), ("ZA", 3 * 144), ("ZL", 272), ("ZJ", 144), ("NL", 288)]:
     PART[_n] = (sum(c for a, c in PART.values()), _c)
@@ -79,6 +97,8 @@ def spec(name):
 
 
 def ap(name, a=0, b=None, step=1, p0=0, p1=128):
+    if name == "pL" and PL:
+        return ("pH", 192 + a, 192 + b, step, p0, p1)
     if name in PART:
         o, c = PART[name]
         return ("ZZ", o + a, o + (c if b is None else b), step, p0, p1)
@@ -174,14 +194,15 @@ def fill(out, v):
     return lin(out, ap("ONE", 0, cnt(out), 1, out[4], out[5]), v)
 
 
-def mm(lst, first=True, grp=None, after=(), close=()):
+def mm(lst, first=True, grp=None, after=(), close=(), each=999):
     c = sum(max(min(64, cnt(l)), cnt(rh)) * (4 if wid(l) == 4 else 1) for o, l, rh in lst)
     ins = [x for o, l, rh in lst + list(close) for x in (l, rh)]
     me = len(OPS)
     def fn(g, T, r):
         stop = OPS[me]["stop"]
         full = lst + list(close) if stop else lst
-        return [g.tensor.matmul(real(T, o), real(T, l), real(T, rh), first and i == 0, stop and i == len(full) - 1)
+        return [g.tensor.matmul(real(T, o), real(T, l), real(T, rh), first and i % each == 0,
+                                stop and (i == len(full) - 1 or (i + 1) % each == 0))
                 for i, (o, l, rh) in enumerate(full)]
     return add("P", (30, 0, 0, 0, c), sorted(set(o for o, l, rh in lst)), ins, fn, grp=grp, after=after)
 
@@ -202,6 +223,10 @@ def asel(out, a, pat, op, fill, base, cm):
 
 def gfill(out, v):
     return asel(out, ap("ONE", 0, cnt(out), 1, out[4], out[5]), [[0, cnt(out)]], A.is_gt, v, 0, 0)
+
+
+def gcopy(out, a):
+    return asel(out, a, [[0, cnt(out)]], A.is_ge, 0.0, 0, 0)
 
 
 def dma(outs, ins, fn, nbytes, behind=None):
@@ -265,7 +290,7 @@ def setup():
     ts(ap("G8"), ap("IO", 0, 8), col(PG), A.is_equal)
     cp(col(HWF), ap("hwi"))
     lin(ap("HZ", 15, 143, 16), ap("G8"), col(HWF))
-    first = [h for u, md in UNITS[0] for h in u]
+    first = PLACE[0]
     for a, q, k, b in runs(first, 0, [0, 1, 2, 3], False):
         lin(ap("Z0", 64 * a, 64 * (a + k)), ap("zin", 64 * q, 64 * (q + k)), 1.0, col(C15))
     if GC:
@@ -273,18 +298,20 @@ def setup():
             asel(ap("FW", a, a + 512), ap("fwi", a, a + 512), [[0, 512]], A.is_ge, 0.0, 0, 0)
     else:
         cp(ap("FW", 0, 1024), ap("fwi"))
+    if PS:
+        gcopy(ap("AWF"), ap("awi"))
     ts(ap("SP"), ap("swi"), 2048.0, A.subtract)
     ts(ap("RT0"), ap("awi"), 3232.0, A.mult, 65536.0, A.add)
     ts(ap("RT"), ap("RT0"), 131071, A.bitwise_and)
     iota(ap("IG"), [[1, 8], [0, 16]])
     iota(ap("IM"), [[0, 8], [1, 16]])
-    asel(ap("I3"), ap("ONE"), [[0, 3], [-1, 128]], A.is_equal, 0.0, 0, 1)
+    asel(ap("I3"), ap("ONE", 0, 128), [[-1, 128]], A.is_equal, 0.0, 0, 1)
     iota(ap("I16"), [[1, 32], [0, 16]])
     ts(ap("EX"), ap("I16"), col(P32), A.is_equal)
     ts(ap("G8T", 0, 128, 1, 0, 8), ap("IG", 0, 128, 1, 0, 8), col(PF, 0, 8), A.is_equal)
-    ts(ap("M0"), ap("IM"), col(PM), A.not_equal, -8192.0, A.mult)
+    ts(ap("M0"), ap("IM"), col(PM), A.not_equal, -16384.0, A.mult)
     lin(ap("MO"), ap("M0"), 1.0, 4096.0)
-    cp(ap("qf", 0, 256, 1, 0, 8), ap("qi", 0, 256, 1, 0, 8))
+    asel(ap("qf", 0, 256, 1, 0, 8), ap("qi", 0, 256, 1, 0, 8), [[0, 256]], A.is_ge, 0.0, 0, 0)
     mm([(ap("pQ", 0, 256), ap("G8T", 0, 128, 1, 0, 8), ap("qf", 0, 256, 1, 0, 8))])
     for a, q, k, b in runs(first, 0, [0, 1, 2, 3]):
         tt(ap("Q0", 64 * a, 64 * (a + k)), ap("pQ", 64 * q, 64 * (q + k)), ap("MO", 0, 64 * k), A.add)
@@ -314,25 +341,32 @@ def setup():
     for k, v in ((2, 768.0), (3, 816.0), (4, 60.0 * 2048)):
         gfill(ap("CT", 8 * k, 8 * k + 8), v)
     iota(ap("CR", 0, 8, 1, 0, 1), [[768, 8]])
-    for a, k, v in ((0, 3, 1.0), (192, 1, -2048.0), (256, 2, 2.0)):
-        asel(ap("I3H", a, a + 64 * k), ap("ZA", 0, 64 * k), [[0, k], [-1, 64]], A.not_equal, v, 0, 1)
+    asel(ap("I2"), ap("ZA", 0, 128), [[0, 2], [-1, 64]], A.not_equal, 2.0, 0, 1)
+    if SP3:
+        iota(ap("LN"), [[0, 9], [1, 16]])
+        gfill(ap("LN", 0, None, 16), 16.0)
+        ts(ap("STM"), ap("LN"), col(PM), A.is_le)
+    else:
+        asel(ap("WRB8"), ap("ONE"), [[0, 3], [-1, 128]], A.is_equal, 0.0, 0, 1)
+        for a, k, v in ((0, 3, 1.0), (192, 1, -2048.0)):
+            asel(ap("WRB4", a, a + 64 * k), ap("ZA", 0, 64 * k), [[0, k], [-1, 64]], A.not_equal, v, 0, 1)
+    for n, m, k in (("RB8", 8, 3), ("RB4", 4, 4)) if SP3 else ():
+        iota(ap(n, m * k), [[0, k], [1, m]])
+        ts(ap(n, 0, m * k), ap(n, m * k), col(PG), A.is_equal)
+        if m == 4:
+            lin(ap(n, 12, 16), ap(n, 12, 16), -2048.0)
+        lin(ap(n, m * k), ap(n, 0, m * k), -1.0)
     iota(ap("ONF", 0, 128, 1, 0, 1), [[0, 128]], 1)
     ts(ap("TH4", 0, 8, 1, 0, 1), ap("thi", 0, 8, 1, 0, 1), 4096.0, A.mult, 129.0, A.subtract)
     iota(ap("VT"), [[0, 3], [16, 4]])
     lin(ap("KP"), ap("VT"), 1.0, col(PM))
-    iota(ap("TF"), [[0, 3], [1, 64]], 1)
     lin(ap("DUM", 0, 8), ap("KP", 0, 8), 1.0, 4096.0)
     lin(ap("DUM", 8, 12), ap("KP", 8, 12), 1.0, 1024.0)
-    lin(ap("TW"), ap("KP"), 8192.0, 8192.0)
-    iota(ap("M65"), [[0, 780]], 1)
-    gfill(ap("M65", 0, None, 65), float(2 ** 40))
-    gfill(ap("M65", 64, None, 65), float(2 ** 20))
-    gfill(ap("DD", 64, None, 65), HUGE)
-    for k in range(8):
-        if k < 8 - IOS:
-            iota(ap("IOT", 520 * k, 520 * k + 520), [[128, 520]], 128 * 520 * k)
-        else:
-            lin(ap("IOT", 520 * k, 520 * k + 520), ap("IOT", 0, 520), 1.0, 128.0 * 520 * k)
+    lin(ap("TW"), ap("KP"), 8192.0, -63.0 * 8192)
+    iota(ap("M64"), [[0, 768]], -8192)
+    gfill(ap("M64", 0, None, 64), HUGE)
+    for k in range(2):
+        iota(ap("IOT", 544 * k, 544 * k + 544), [[1, 544]], 544 * k)
 
 
 def front(s, p, n, units):
@@ -347,7 +381,10 @@ def front(s, p, n, units):
     ts(ap("I3I", o + 2 * m, o + 3 * m), ui, 3, A.logical_shift_right, 511, A.bitwise_and)
     cp(ap("O3", o, o + 3 * m), ap("I3I", o, o + 3 * m))
     ok, os_, oa = [ap("O3", o + k * m, o + k * m + m) for k in range(3)]
-    ts(ap("PP", t0, t0 + n), ind(ap("awi"), oa), 32.0, A.add)
+    if (s, p) in PS:
+        lin(ap("PP", t0, t0 + n), ind(ap("AWF"), oa), 1.0, 32.0)
+    else:
+        ts(ap("PP", t0, t0 + n), ind(ap("awi"), oa), 32.0, A.add)
     tt(ap("AP1", t0, t0 + n), ind(ap("SP"), os_), ap("PP", t0, t0 + n), A.mult)
     tt(ap("N1", 256 + t0, 256 + t0 + n), ind(ap("RT"), oa), ap("AP1", t0, t0 + n), A.add)
     tt(ap("N1", t0, t0 + n), ind(ap("FW" if s else "fwi", 0, 1024), ok), ap(Q, t0, t0 + n), A.max)
@@ -394,41 +431,70 @@ def bulk(s, p, md):
             y = min(b, x + SL)
             scan(lane(2, x, y), ap("MK", 0, 16 * (y - x)), src(x, y), 0.0, A.add, A.max)
 
-    if md.strip("V"):
+    if (s, p) in ZP or any("S" in MODE[c] for c in md):
         zt = ap(bank(), 0, 128, 1, 0, n)
-        mm([(zt, ap(Z, t0, t0 + n), ap("I3", 0, 128))])
+        mm([(zt, ap(Z, t0, t0 + n), ap("I3"))])
         lin(ap("ZT", 2 * t0, 2 * t0 + 128, 1, 0, n), zt, -1.0)
-    for a, b in spans(md, "VMN", NZ):
+    for a, b in spans(md, [c for c in MODE if c != "S"], DW) if (s, p) in ZP else ():
+        bk = bank()
+        mm([(ap(bk, 16 * (x - a), 16 * (x - a) + 512), ap("ZT", 2 * t0, 2 * t0 + 128, 1, x, x + 32), ap("EX", 0, 512, 1, x, x + 32))
+            for x in range(a, b, 32)], each=1)
+        lin(flat("ZR", a, b), ap(bk, 0, 16 * (b - a)), -1.0)
+    for a, b in spans(md, [c for c in MODE if c != "S"], NZ) if (s, p) not in ZP else ():
         z0 = TURN[1] if TURN[1] + 16 * (b - a) <= 16 * NZ else 0
         TURN[1] = z0 + 16 * (b - a)
-        cp(ap("ZS", z0, TURN[1], 16), ap(Z, t0 + a, t0 + b))
+        (gcopy if s and ZG else cp)(ap("ZS", z0, TURN[1], 16), ap(Z, t0 + a, t0 + b))
         for x in range(a, b, SL):
             y = min(b, x + SL)
             scan(flat("ZR", x, y), ap("MK", 0, 16 * (y - x)), ap("ZS", z0 + 16 * (x - a), z0 + 16 * (y - a)), 0.0, A.add, A.max)
-    for k, raw, low, mine in ((1, "RC", "LC", "SN"), (0, "RS", "LS", "SM")):
-        o = on + k * n
+    for k, raw, low in ((1, "RC", "LC"), (0, "RS", "LS")):
+        o, mine = on + k * n, by(k, "S")
+        for a, b in spans(md, by(k, "H"), GV):
+            tt(flat(low, a, b), ind(X, ap("ON", o + a, o + b)), flat("ZR", a, b), A.subtract)
+            act(lane(k, a, b), flat(low, a, b), F.Abs)
+            if k:
+                greatest(lambda x, y: flat("LC", x, y), a, b)
         for a, b in spans(md, mine, GS):
             act(flat(raw, a, b), ind(X, ap("ON", o + a, o + b)), F.Identity)
-            for x in range(a, b, 32):
-                d = ap(bank())
-                mm([(d, ap("ZT", 2 * t0, 2 * t0 + 128, 1, x, x + 32), ap("EX", 0, 512, 1, x, x + 32)),
-                    (d, ap("I3", 0, 128), flat(raw, x, x + 32))])
-                act(lane(k, x, x + 32), d, F.Abs)
+            for x0 in range(a, b, DW):
+                y0, bk = min(b, x0 + DW), bank()
+                lst = []
+                for x in range(x0, y0, 32):
+                    d = ap(bk, 16 * (x - x0), 16 * (x - x0) + 512)
+                    lst += [(d, ap("ZT", 2 * t0, 2 * t0 + 128, 1, x, x + 32), ap("EX", 0, 512, 1, x, x + 32)),
+                            (d, ap("I3"), flat(raw, x, x + 32))]
+                mm(lst, each=2)
+                act(lane(k, x0, y0), ap(bk, 0, 16 * (y0 - x0)), F.Abs)
             if k:
                 greatest(lambda x, y: flat("RC", x, y), a, b)
         if k:
             for a, b in spans(md, mine, 128):
                 top = ap("B", 48 * (t0 + a) + 47, 48 * (t0 + b), 48)
                 tt(top, top, ap(Z, t0 + a, t0 + b), A.subtract)
-        for a, b in spans(md, "VMN".replace(mine[1], ""), GV):
-            tt(lane(k, a, b), ind(X, ap("ON", o + a, o + b)), flat("ZR", a, b), A.subtract)
+        for a, b in spans(md, by(k, "V"), GV):
+            for x in range(a, b, GV):
+                y = min(b, x + GV)
+                tt(lane(k, x, y), ind(X, ap("ON", o + x, o + y)), flat("ZR", x, y), A.subtract)
             ts(flat(low, a, b), lane(k, a, b), 0.0, A.min)
             if k:
                 greatest(lambda x, y: lane(1, x, y), a, b)
 
 
+def by(k, who):
+    return [c for c in MODE if MODE[c][k] == who]
+
+
 def spread(out, zname, z0, rhs, c0, cols, n):
-    return [(out, ap(zname, z0 + 15 - r, z0 + 143 - r, 1, 0, n), ap(rhs, c0 + r, c0 + cols, 16, 0, n)) for r in range(16)]
+    z = ap(zname, z0, z0 + 129, 1, 0, n)
+    if not SP3:
+        return [(out, ("ZZ", z[1] - r, z[1] - r + 128, 1, 0, n), ap("W" + rhs, 16 * c0 + r, 16 * (c0 + cols), 16, 0, n))
+                for r in range(16)]
+    y = z[1] - PART["ZA"][0]
+    scan(ap("LB", y, y + 129, 1, 0, n), ap("STM", 0, 129, 1, 0, n), z, 0.0, A.mult, A.add)
+    w = cnt(ap(rhs)) // 2
+    pos, neg = ap(rhs, c0, c0 + cols, 1, 0, n), ap(rhs, w + c0, w + c0 + cols, 1, 0, n)
+    return [(out, ap(zname, z0 + 1, z0 + 129, 1, 0, n), pos), (out, ap("LB", y, y + 128, 1, 0, n), pos),
+            (out, ap("LB", y + 1, y + 129, 1, 0, n), neg)]
 
 
 KEYS = []
@@ -445,16 +511,16 @@ def tail(s, p, md):
     mm([(sl(K, 0, 8 * L), ap("ONE", 0, n, 1, 0, 1), ap("KC%d" % L, 0, None, 1, 0, 1))], True, K, KEYS[-2:-1])
     lst = [(sl(K, 16, 8 * L, L), ap("ONF", 0, n, 1, 0, 1), ap("TH4", 0, 8, 1, 0, 1))]
     if s > 0:
-        q = 0
         for u, x in UNITS[s - 1]:
+            q = PLACE[s - 1].index(u[0])
             c, k = 32 * ((s - 1) % 2) + 8 * q, 64 * len(u)
             c2 = 144 * ((s - 1) % 2)
             lst.append((sl(K, 16, 8 * L, L), ap("ONE", 0, n, 1, 0, k),
-                        ap("NW", c, c + 8, 1, 0, k) if q else ap("NL", c2 + 15, c2 + 143, 16, 0, k)))
-            q += len(u)
+                        ap("NW", c, c + 8, 1, 0, k) if q else ap("NL", c2, c2 + 128, 16, 0, k)))
     mm(lst, False, K)
-    for k, low, other in ((1, "LC", "VM"), (0, "LS", "VN")):
+    for k, low in ((1, "LC"), (0, "LS")):
         st, ws = (L, 3) if k or p else (H, 1)
+        other = by(k, "V")
         d = mm([(sl(K, H * k + i, 8 * L, st), ap("B", 48 * t0 + 3 * i + k, 48 * (t0 + n), 48), ap("WS", 0, 24, ws))
                 for i in range(16)], False, K)
         for a, b in spans(md, other, 128):
@@ -465,7 +531,7 @@ def tail(s, p, md):
     if p:
         c0, za, z0 = 288 * p, "ZA", 144 * (p - 1)
         KEYS.append(scan(sl("SC", c0, c0 + 288), sl("M36", 0, 288), sl(K, 0, 288), 0.0, A.add, A.min))
-        tt(sl("ZA", z0 + 15, z0 + 143, 16), sl("SC", c0 + 33, c0 + 288, 36), sl("SC", c0 + 35, c0 + 288, 36), A.subtract)
+        tt(sl("ZA", z0, z0 + 128, 16), sl("SC", c0 + 33, c0 + 288, 36), sl("SC", c0 + 35, c0 + 288, 36), A.subtract)
     else:
         za, z0 = "ZL", 0
         KEYS.append(scan(sl("SL", 0, 408), sl("M51", 0, 408), sl(K, 0, 408), 0.0, A.add, A.min))
@@ -473,14 +539,13 @@ def tail(s, p, md):
         tt(sl("KI", 8, 16), sl("SL", 15, 408, 51), sl("SL", 33, 408, 51), A.max)
         cp(sl("KI", 16, 24), sl("SL", 50, 408, 51))
         ts(sl("KC6", 0, 24), sl("KI", 0, 24), 63, A.bitwise_and)
-        cp(sl("ZL", 15, 271, 16), sl("KC6", 0, 16))
+        cp(sl("ZL", 0, 256, 16), sl("KC6", 0, 16))
     shift = 23.0 if p else -1.0
-    i3, cs = ("I3", 1) if n == 128 else ("I3H", 2)
     ow = 48 * s + 12 * p
-    pw = 64 + ow
-    mm([(ap("pH", pw, pw + 3 * m), ap("I3", 0, 128), ap("CT", 0, 24, cs)),
+    pw = 48 + ow
+    mm([(ap("pH", pw, pw + 3 * m), ap("I3"), ap("CT", 0, 24, 8 // m)),
         (ap("pH", pw, pw + m), ap("ONE", 0, 128, 1, 0, 1), ap("CR", 0, m, 1, 0, 1))]
-       + spread(ap("pH", pw, pw + 3 * m), za, z0, i3, 0, 3 * n, n))
+       + spread(ap("pH", pw, pw + 3 * m), za, z0, "RB%d" % m, 0, 3 * m, n))
     ts(ap("OW", ow, ow + 3 * m), ap("pH", pw, pw + 3 * m), shift, A.add)
     last = s == RO - 1
     act(ap("ZN%d" % s, t0, t0 + n), ind(ap("B", 48 * t0, 48 * (t0 + n)), ap("OW", ow, ow + m)), F.Abs,
@@ -488,26 +553,22 @@ def tail(s, p, md):
     a, b, c_ = 2 * t0, 2 * t0 + n, 2 * t0 + 2 * n
     nm = 512 * (s % 2)
     tt(ap("MN", a, c_), ind(ap("OH"), ap("OW", ow + m, ow + 3 * m)), ap("NM", nm + a, nm + c_), A.mult)
-    if not last or not p:
-        k = 64 if last else n
-        pq = ap("pQ", t0, t0 + k)
-        lst = [(pq, ap("GB"), ap("MN", a, a + k)), (pq, ap("GB"), ap("MN", b, b + k))]
-        if p and QS:
-            mm([(pq, ap("I3", 0, 128), ap("M0", 0, n))] + lst)
+    if not last:
+        pq = ap("pQ", t0, t0 + n)
+        lst = [(pq, ap("GB"), ap("MN", a, b)), (pq, ap("GB"), ap("MN", b, c_))]
+        if (QS >> (1 if p else 0)) & 1:
+            mm([(pq, ap("I3"), ap("M0", 0, n))] + lst)
             lin(ap("QN%d" % s, t0, t0 + n), pq, 1.0, 4096.0)
         else:
             mm(lst)
-            if not last:
-                tt(ap("QN%d" % s, t0, t0 + n), pq, ap("MO", 0, n), A.add)
-        if not p:
-            act(ap("WB"), ap("pQ", 0, 64), F.Identity)
-    if last:
+            tt(ap("QN%d" % s, t0, t0 + n), pq, ap("MO", 0, n), A.add)
+    else:
         o = ap("pQ", 320, 320 + n, 1, 0, 8)
         mm([(o, ap("G8"), ap("MN", a, b)), (o, ap("G8"), ap("MN", b, c_))])
         act(ap("YQ", t0, t0 + n, 1, 0, 8), o, F.Identity)
     c, c2 = 32 * (s % 2) + 8 * p, 144 * (s % 2)
     if not last or not p:
-        act(sl("NW", c, c + 8) if p else sl("NL", c2 + 15, c2 + 143, 16), sl(za, z0 + 15, z0 + 143, 16), F.Relu,
+        act(sl("NW", c, c + 8) if p else sl("NL", c2, c2 + 128, 16), sl(za, z0, z0 + 128, 16), F.Relu,
             bias=4096.0 * (shift - 46.0), scale=4096.0)
 
 
@@ -515,11 +576,11 @@ def learn(s, n):
     def sl(name, a, b, st=1):
         return ap(name, a, b, st, 0, 64)
     ts(sl("K64", 0, 8), sl("KI", 0, 8), 64, A.bitwise_and)
-    tt(sl("ZJ", 15, 143, 16), sl("KC6", 16, 24), sl("K64", 0, 8), A.add)
-    ol = [mm([(ap("pL", c, c + 8), ap("I3", 0, 128), ap("CT", 8 + 2 * c, 24 + 2 * c, 2))]
-             + spread(ap("pL", c, c + 8), z, z0, "I3H", 16 * c, 128, 64)) for c, z, z0 in ((0, "ZL", 128), (8, "ZJ", 0))]
-    ts(ap("OL", 0, 8), ap("pL", 0, 8), -1.0, A.add)
-    ts(ap("OL", 8, 12), ap("pL", 8, 12), -1.0, A.add)
+    tt(sl("ZJ", 0, 128, 16), sl("KC6", 16, 24), sl("K64", 0, 8), A.add)
+    ol = [mm([(ap("pL", c, c + 8), ap("I3"), ap("CT", 8 + 2 * c, 24 + 2 * c, 2))]
+             + spread(ap("pL", c, c + 8), z, z0, "RB4", c, 8, 64)) for c, z, z0 in ((0, "ZL", 128), (8, "ZJ", 0))]
+    for a, b in ([(0, 8), (8, 12)] if OLS else [(0, 12)]):
+        ts(ap("OL", a, b), ap("pL", a, b), -1.0, A.add)
     tt(ap("SC2", 143, 192, 16), ap("pL", 12, 16), ap("I3I", 48 * s, 48 * s + 4), A.max)
     a = 512 * (s % 2)
     if n == 64:
@@ -528,22 +589,30 @@ def learn(s, n):
         tt(ap("ML", 0, 64), ind(ap("OH"), ap("OL", 0, 4)), ap("NM", a, a + 64), A.mult)
         tt(ap("ML", 64, 128), ind(ap("OH"), ap("OL", 4, 8)), ap("NM", a + n, a + n + 64), A.mult)
     g, c2 = "L%d" % s, 144 * (s % 2)
-    mm([(ap("pL", 128, 256), ap("I3", 0, 128), ap("M0"))], True, g, ol)
-    mm([(ap("pL", 128 + r, 256, 16), ap("NL", c2 + 15 - r, c2 + 143 - r, 1, 0, 64), ap("I3H", 256 + r, 384, 16, 0, 64))
-        for r in range(16)], False, g)
-    mm([(ap("pL", 192, 256), ap("GB"), ap("MN", 0, 64)), (ap("pL", 192, 256), ap("GB"), ap("MN", n, n + 64))], False, g)
-    mm([(ap("pL", 128, 192), ap("GB"), ap("ML", 0, 64)), (ap("pL", 128, 192), ap("GB"), ap("ML", 64, 128))], False, g)
+    scan(sl("LN", 0, 128), sl("MK", 0, 128), sl("NL", c2, c2 + 128), 0.0, A.add, A.max)
+    for c, own, plain, src, x2, u in ((192, 192, 256, "MN", n, 64), (64, 128, 64, "ML", 64, 0)):
+        mm([(ap("pL", c, c + 128), sl("LN", 0, 128), sl("I2", 0, 128)), (ap("pL", own, own + 64), ap("I3"), ap("M0", 0, 64))]
+           + [(ap("pL", y, y + 64), ap("GB"), ap(src, x, x + 64)) for y in (own, plain) for x in (0, x2)])
+        act(ap("U", u, u + 64), ap("pL", plain, plain + 64), F.Identity)
     scan(ap("SC2", 0, 128), ap("MK", 0, 128), ap("pL", 128, 256), 0.0, A.add, A.max)
+    if "l" in DS_ or "w" in DS_:
+        lin(ap("NB", 0, 8), ap("SC2", 15, 128, 16), -float(2 ** 20))
     for a, b in LISTS[s]:
         tt(ap("VP", a, b), ap("SC2", 16 * a + 15, 16 * b, 16), ap("DUM", a, b), A.min)
         cp(ap("OV", a, b), ap("VP", a, b))
         tt(ap("VT", a, b), ap("VP", a, b), ap("TW", a, b), A.add)
-        tt(ap("U", 16 * a, 16 * b), ind(ap("IOT"), ap("OV", a, b)), ap("TF", 16 * a, 16 * b), A.add)
+        if b == 12:
+            (cp if US else lambda o, x: act(o, x, F.Identity))(ap("U", 128, 192), ind(ap("IOT"), ap("OV", 8, 12)))
+            if "k" in DS_:
+                lin(ap("NB", 8, 12), ap("VP", 8, 12), -float(2 ** 20))
         for k in range(a, b):
-            act(ap("DD", 65 * k, 65 * k + 64), ap("U", 64 * (k // 4), 64 * (k // 4) + 64), F.Abs, bias=ap("VP", k, k + 1),
-                scale=-1.0 / 128)
-        scan(ap("DS", 65 * a, 65 * b), ap("M65", 65 * a, 65 * b), ap("DD", 65 * a, 65 * b), 1.0, A.mult, A.min)
-        tt(ap("KP", a, b), ap("VT", a, b), ap("DS", 65 * a + 64, 65 * b, 65), A.subtract)
+            d, u = ap("DD", 64 * k, 64 * k + 64), ap("U", 64 * (k // 4), 64 * (k // 4) + 64)
+            if "lwk"[k // 4] in DS_:
+                act(d, u, F.Abs, bias=ap("NB", k, k + 1), scale=float(2 ** 20))
+            else:
+                ts(d, u, ap("VP", k, k + 1) if k >= 8 else ap("SC2", 16 * k + 15, 16 * k + 16), A.not_equal, float(2 ** 20), A.mult)
+        scan(ap("DS", 64 * a, 64 * b), ap("M64", 64 * a, 64 * b), ap("DD", 64 * a, 64 * b), 0.0, A.add, A.min)
+        tt(ap("KP", a, b), ap("VT", a, b), ap("DS", 64 * a + 63, 64 * b, 64), A.subtract)
         tt(ap("VQ", a, b), ap("KP", a, b), ap("DUM", a, b), A.min)
         cp(ap("OK%d" % s, a, b), ap("VQ", a, b))
     X = ap("X%d" % (s % 2))
@@ -556,9 +625,9 @@ def learn(s, n):
         ts(ap("T2"), ap("T1"), col(VS), A.mult, col(VB), A.add)
         ts(ap("XW%d" % s), ap("T2"), col(VMIN), A.min)
         ts(ap("XL%d" % s), ind(X, ap("OV", 0, 4)), col(IS15), A.subtract, 0.0, A.max)
-    tt(ap("F1"), ind(ap("FW"), ap("OV", 8, 12)), ap("WB"), A.subtract)
+    tt(ap("F1"), ind(ap("FW"), ap("OV", 8, 12)), ap("U", 64, 128), A.subtract)
     tt(ap("F2"), ind(ap("OH"), ap("OL", 8, 12)), ap("F1"), A.mult)
-    tt(ind(ap("FW"), ap("OK%d" % s, 8, 12)), ap("F2"), ap("WB"), A.add)
+    tt(ind(ap("FW"), ap("OK%d" % s, 8, 12)), ap("F2"), ap("U", 64, 128), A.add)
 
 
 def update(s, x):
@@ -580,15 +649,13 @@ def runs(u, p, nxt, blocks=True):
 def program():
     setup()
     for s in range(RO):
-        places = [sum(len(u) for u, md in UNITS[s][:k]) for k in range(len(UNITS[s]))]
+        places = [PLACE[s].index(u[0]) for u, md in UNITS[s]]
         sizes = [64 * len(u) for u, md in UNITS[s]]
-        if s == 0:
-            front(s, 0, 256, list(zip(places, sizes)))
-        else:
-            for p, n in zip(places, sizes):
-                front(s, p, n, [(p, n)])
+        w = 4 if s == 0 and F0 else 2
+        for p in range(0, 4, w):
+            front(s, p, 64 * w, [(q, n) for q, n in zip(places, sizes) if p <= q < p + w])
         last = s == RO - 1
-        nxt = [0, 1, 2, 3] if last else [h for u, md in UNITS[s + 1] for h in u]
+        nxt = [0, 1, 2, 3] if last else PLACE[s + 1]
         for (u, md), p, n in zip(UNITS[s], places, sizes):
             bulk(s, p, md)
             tail(s, p, md)
@@ -654,6 +721,7 @@ def prices(m):
     cost = [o["c"][0] + (o["c"][1] + o["c"][2] * m[1] + o["c"][3] * m[2]) * m[0] + o["c"][4] * m[3]
             + (m[5] if o["eng"] in "VS" else 0.0) for o in OPS]
     cost = [o["lat"] / m[7] if o["eng"] == "E" else c for o, c in zip(OPS, cost)]
+    cost[[o["eng"] for o in OPS].index("R") - 1] += m[9]
     lat = [m[8] if o["eng"] == "R" else (m[6] if o["eng"] == "D" else 0.0) for o in OPS]
     pred = [[(j, lat[j] + (0.0 if o["eng"] in "RDE" or o["eng"] + OPS[j]["eng"] in ("PP", "YY") else m[4]))
              for j in o["dep"]] for o in OPS]
@@ -866,7 +934,7 @@ def schedule(seed, rounds, tries, moves):
 
 
 SMOOTH = 0.3
-HEAT = 0.0004
+HEAT = 0.0002
 FILL = 0.5
 
 

@@ -4,48 +4,54 @@ from concourse.mybir import AluOpType, ActivationFunctionType
 A = AluOpType
 F = ActivationFunctionType
 NR, W, RO = 4, 4096, 3
-UNITS = [[((0, 1), "SSVV"), ((2, 3), "SSMV")],
-         [((1, 0), "SSVV"), ((2, 3), "SSMV")],
-         [((2,), "VV"), ((1, 0), "SSSM"), ((3,), "SM")]]
-PLACE = [[0, 1, 2, 3], [1, 0, 2, 3], [2, 3, 1, 0]]
+UNITS = [[((0,), "SV"), ((1,), "SV"), ((2, 3), "SSSV")],
+         [((1, 0), "SSSV"), ((2,), "SV"), ((3,), "SS")],
+         [((2, 1), "SSSV"), ((0, 3), "SSSV")]]
+PLACE = [[0, 1, 2, 3], [1, 0, 2, 3], [2, 1, 0, 3]]
+FRONTS = [[(0, 4)], [(0, 1), (1, 1), (2, 2)], [(0, 1), (1, 2), (3, 1)]]
 MODE = {"S": "SS", "V": "VV", "M": "SV", "N": "VS", "H": "HH", "J": "SH", "K": "HV", "L": "VH"}
 LISTS = [[(0, 12)], [(0, 12)], [(8, 12), (0, 8)]]
 GV = 32
 GS = 64
-NZ = 0
-ZV = 688
-IOS = 4
-TS = 1
+NZ = 64
 US = 1
-DS_ = "lwk"
+DS_ = ["lw", "w", ""]
 OLS = 1
-ZG = 0
-F0 = 1
-SP3 = 0
+SP3 = 1
 PL = 1
-DW = 32
-ZP = [(0, 0), (0, 2), (1, 0), (1, 2), (2, 0), (2, 1), (2, 2), (2, 3), (1, 1), (1, 3)]
-PS = ZP[2:]
-QS = 3
-GC = 1
-SL = 64
+DW = 64
+ZP = [(0, 0), (0, 1), (0, 2)]
+ZG = []
+XC = 1
+XS = 0
+LOADS = "zHasxqfty"
+ZV = "ZA"
+XF = 0
+NV = 0
+SL = 32
 ROUND = 1.5 * 2 ** 23
-ND = 4
+ND = 2
 BIG = float(2 ** 26)
 HUGE = float(2 ** 31)
 MAGIC = 1.5 * 2 ** 29
 
+UNITS = [[((0, 1), "SSVV"), ((2, 3), "SSMV")], [((1, 0), "SSVV"), ((2, 3), "SSMV")], [((2,), "VV"), ((1, 0), "SSSM"), ((3,), "SM")]]
+GV, US, OLS, XS = 32, 1, 1, 0
+PLACE = [[0, 1, 2, 3], [1, 0, 2, 3], [2, 3, 1, 0]]
+FRONTS = [[(0, 4)], [(0, 2), (2, 2)], [(0, 2), (2, 2)]]
+ZP = [(s, p) for s in range(3) for p in range(4)]
+NZ, DS_, SP3, DW, ND, XC, SL = 0, ["lw"] * 3, 0, 32, 4, 0, 64
 SCRATCH = {}
 SEMAPHORES = ["cV", "cS", "cP", "cG", "ls"]
 OPS = []
 BANK = {}
-SEEDS = (4, 150, 1500, 48000)
-GUESS = [(0.9, 1.56, 3.8, 0.46, 100.0, 20.0, 1500.0, 300.0, 2500.0, 1000.0),
-         (0.83, 1.3, 3.0, 0.42, 180.0, 0.0, 1200.0, 500.0, 2000.0, 1000.0),
-         (0.85, 1.3, 3.0, 0.43, 150.0, 0.0, 2000.0, 220.0, 4500.0, 2000.0),
-         (1.0, 1.56, 3.8, 0.5, 60.0, 40.0, 1000.0, 600.0, 2000.0, 500.0),
-         (1.2, 1.9, 5.0, 0.6, 130.0, 20.0, 1800.0, 250.0, 4500.0, 2000.0),
-         (1.15, 1.3, 3.0, 0.58, 80.0, 10.0, 1300.0, 400.0, 3000.0, 1500.0)]
+SEEDS = (1, 10, 30)
+STAGES = [(120000, 0.001, 0.0004), (120000, 0.0004, 0.0)]
+GUESS = [(0.87, 1.33, 2.5, 0.32, 210.0, -4.0, 600.0, 550.0, 2400.0, 1000.0, -20.0, 225.0, 410.0, 320.0),
+         (0.93, 1.06, 2.5, 0.40, 130.0, 18.0, 900.0, 700.0, 2000.0, 900.0, 10.0, 170.0, 400.0, 650.0),
+         (0.83, 1.56, 3.8, 0.38, 150.0, 5.0, 1200.0, 400.0, 2500.0, 1200.0, 0.0, 150.0, 300.0, 500.0),
+         (1.13, 2.08, 3.0, 0.48, 245.0, 0.0, 600.0, 410.0, 1900.0, 800.0, -18.0, 250.0, 560.0, 800.0),
+         (1.07, 1.8, 4.5, 0.52, 180.0, 10.0, 850.0, 300.0, 4400.0, 800.0, 0.0, 200.0, 470.0, 500.0)]
 
 
 def buf(name, cols, dtype, where="sbuf"):
@@ -54,8 +60,8 @@ def buf(name, cols, dtype, where="sbuf"):
 
 for _n, _c, _d in [
         ("X0", 4160, "bfloat16"), ("X1", 4160, "bfloat16"), ("fwi", 1024, "int32"), ("FW", 1088, "float32"),
-        ("swi", 512, "int32"), ("SP", 512, "float32"), ("AWF", 512, "float32"), ("awi", 512, "int32"), ("RT0", 512, "int32"), ("RT", 512, "int32"),
-        ("zin", 256, "bfloat16"), ("hwi", 1, "int32"), ("thi", 8, "int32"), ("qi", 256, "int32"), ("qf", 256, "float32"),
+        ("swi", 512, "int32"), ("SP", 512, "float32"), ("PW", 512, "float32"), ("awi", 512, "int32"), ("RT", 512, "float32"),
+        ("hwi", 1, "int32"), ("thi", 8, "int32"), ("qi", 256, "int32"), ("qf", 256, "float32"),
         ("Z0", 256, "bfloat16"), ("Z1", 256, "bfloat16"), ("Z2", 256, "bfloat16"),
         ("Q0", 256, "float32"), ("Q1", 256, "float32"), ("Q2", 256, "float32"),
         ("ZN0", 256, "bfloat16"), ("ZN1", 256, "bfloat16"), ("ZN2", 256, "bfloat16"),
@@ -64,30 +70,30 @@ for _n, _c, _d in [
         ("LC", 4096, "bfloat16"), ("ZR", 4096, "bfloat16"), ("IOT", 1088, "float32"), ("IO", 112, "float32"),
         ("UI", 48, "int32"), ("I3I", 144, "int32"), ("O3", 144, "uint16"), ("N1", 512, "int32"), ("PP", 256, "float32"),
         ("AP1", 256, "float32"), ("NM", 1024, "int32"), ("ON", 1024, "uint16"), ("SC", 4 * 288, "float32"), ("SL", 408, "float32"),
-        ("KI", 24, "int32"), ("KC6", 24, "int32"), ("K64", 8, "int32"), ("NW", 8 * 8, "bfloat16"),
+        ("KI", 26, "int32"), ("KC6", 26, "int32"), ("CW", 8, "float32"), ("NW", 8 * 8, "bfloat16"),
         ("OW", 144, "uint16"), ("OL", 12, "uint16"), ("MN", 512, "float32"), ("ML", 128, "float32"),
-        ("WB", 64, "float32"), ("SC2", 192, "float32"), ("VT", 12, "float32"), ("VP", 12, "float32"), ("OV", 12, "uint16"),
+        ("KO", 4, "float32"), ("SC2", 192, "float32"), ("VT", 12, "float32"), ("VP", 12, "float32"), ("OV", 12, "uint16"),
         ("U", 192, "float32"), ("DD", 780, "bfloat16"), ("DS", 780, "bfloat16"), ("KP", 12, "float32"),
         ("VQ", 12, "float32"), ("OK0", 12, "uint16"), ("OK1", 12, "uint16"), ("OK2", 12, "uint16"),
-        ("T1", 64, "float32"), ("T2", 64, "int32"), ("XW0", 64, "bfloat16"), ("XW1", 64, "bfloat16"),
+        ("T1", 64, "float32"), ("DG", 128, "bfloat16"), ("XW0", 64, "bfloat16"), ("XW1", 64, "bfloat16"),
         ("XW2", 64, "bfloat16"), ("XL0", 64, "bfloat16"), ("XL1", 64, "bfloat16"), ("XL2", 64, "bfloat16"),
         ("F1", 64, "float32"), ("F2", 64, "float32"), ("TH4", 8, "float32"),
-        ("ONE", 384, "bfloat16"), ("ONF", 128, "float32"), ("I3", 128, "bfloat16"), ("I2", 128, "bfloat16"),
+        ("ONE", 384, "bfloat16"), ("ONF", 128, "float32"), ("I3", 128, "bfloat16"),
         ("LN", 144, "bfloat16"), ("STM", 144, "bfloat16"), ("RB8", 48, "bfloat16"), ("RB4", 32, "bfloat16"),
-        ("LB", 848, "bfloat16"), ("WRB8", 384, "bfloat16"), ("WRB4", 256, "bfloat16"), ("PI", 4, "int32"), ("CF", 16, "float32"),
-        ("I48", 768, "bfloat16"), ("OH", 928, "bfloat16"), ("G8", 8, "float32"), ("WR", 24, "bfloat16"),
-        ("IG", 128, "float32"), ("GB", 128, "float32"), ("G8T", 128, "float32"), ("IM", 128, "float32"), ("MO", 128, "float32"),
-        ("M0", 128, "bfloat16"), ("CT", 40, "bfloat16"), ("CR", 8, "bfloat16"), ("TW", 12, "float32"), ("DUM", 12, "float32"),
-        ("TF", 192, "float32"), ("KC36", 288, "bfloat16"), ("KC51", 408, "bfloat16"),
-        ("M36", 288, "bfloat16"), ("M51", 408, "bfloat16"), ("M64", 768, "bfloat16"), ("T3", 64, "float32"), ("NB", 12, "float32"),
-        ("ZT", 512, "bfloat16"), ("I16", 512, "bfloat16"), ("EX", 512, "bfloat16")]:
+        ("LB", 864, "bfloat16"), ("WRB8", 384, "bfloat16"), ("WRB4", 256, "bfloat16"), ("PI", 4, "int32"), ("CF", 20, "float32"),
+        ("OH", 880, "bfloat16"), ("G8", 8, "float32"), ("WR", 24, "bfloat16"),
+        ("IG", 128, "float32"), ("GB", 128, "float32"), ("G8T", 128, "float32"), ("IM", 128, "float32"),
+        ("M0", 128, "bfloat16"), ("CT", 40, "bfloat16"), ("CR", 8, "bfloat16"), ("DUS", 12, "float32"), ("DUM", 12, "float32"),
+        ("KC36", 288, "bfloat16"), ("KC51", 408, "bfloat16"),
+        ("M36", 288, "bfloat16"), ("M51", 408, "bfloat16"), ("M65", 780, "bfloat16"), ("T3", 64, "float32"), ("NB", 12, "float32"),
+        ("ZT", 512, "bfloat16"), ("Z4", 1024, "bfloat16"), ("I16", 512, "bfloat16"), ("EX", 512, "bfloat16")]:
     buf(_n, _c, _d)
 for _n in ["pH", "pK0", "pK1", "pQ"] + ([] if PL else ["pL"]):
     buf(_n, 512, "float32", "psum")
 for _n in range(ND):
     buf("pD%d" % _n, 16 * DW, "float32", "psum")
 PART = {}
-for _n, _c in [("HZ", 144), ("WS", 32), ("MK", 16 * SL), ("ZS", 16 * NZ), ("ZA", 3 * 144), ("ZL", 272), ("ZJ", 144), ("NL", 288)]:
+for _n, _c in [("HZ", 144), ("WS", 32), ("DH", 144), ("MK", 16 * SL), ("ZA", 3 * 144), ("ZL", 3 * 144), ("NL", 288), ("ZS", 16 * NZ)]:
     PART[_n] = (sum(c for a, c in PART.values()), _c)
 buf("ZZ", sum(c for a, c in PART.values()), "bfloat16")
 
@@ -229,14 +235,15 @@ def gcopy(out, a):
     return asel(out, a, [[0, cnt(out)]], A.is_ge, 0.0, 0, 0)
 
 
-def dma(outs, ins, fn, nbytes, behind=None):
+def dma(outs, ins, fn, nbytes, behind=None, after=(), queue="Y"):
     sem = "d%d" % len(SEMAPHORES)
     SEMAPHORES.append(sem)
     def f2(g, T, r):
         o, i = fn(T)
-        g.sync.dma_start(o, i).then_inc(T.sem[sem], 16)
+        (g.sync if queue == "Y" else g.scalar).dma_start(o, i).then_inc(T.sem[sem], 16)
         return []
-    i = add("Y", (60, 0, 0, 0, 0), outs, ins, f2, after=[] if behind is None else [behind])
+    same = behind is not None and OPS[behind]["eng"] == queue
+    i = add(queue, (0, 0, 0, 0, 0), outs, ins, f2, after=list(after) + ([behind] if same else []), lat="dma")
     j = add("E", (0, 0, 0, 0, 0), [], [], None, after=[i] if behind is None else [i, behind + 1], lat=nbytes)
     add("D", (0, 0, 0, 0, 0), outs, ins, None, sem=sem, val=16, after=[j])
     return i
@@ -252,7 +259,7 @@ def send(src, dst, hop):
         g.remote_dma(real(T, dst), real(T, src), T.sem[sem], T.sem["ls"], pid, rid, m)
         r["ls"] += len(r["topo"].engines(r["core"], to))
         return []
-    i = add("G", (600, 0, 0, 0, 0), [], [src], fn)
+    i = add("G", (0, 0, 0, 0, 0), [], [src], fn, lat="send")
     return add("R", (0, 0, 0, 0, 0), [dst], [], None, sem=sem, val=hop, after=[i])
 
 
@@ -260,49 +267,42 @@ def col(i, p0=0, p1=128):
     return ap("CF", i, i + 1, 1, p0, p1)
 
 
-PF, PM, PG, P32, PM3, C15, ZSC, VS, VB, VMIN, IS15, WCOL, HWF, NI15 = range(14)
+PF, PM, PG, P32, PM3, OFF, ZSC, VS, VB, VMIN, IS15, WCOL, HWF, NI15, NOFF, SPB, SPC, VMAX = range(18)
 
 
 def setup():
-    loads = [(ap("zin"), lambda T: (T.zin[:], T.z0[:]), 65536), (ap("hwi"), lambda T: (T.hwi[:], T.hw[:]), 8192),
-             (ap("awi"), lambda T: (T.awi[:], T.aw[:]), 262144), (ap("swi"), lambda T: (T.swi[:], T.sw[:]), 262144),
-             (ap("qi"), lambda T: (T.qi[0:8, :], T.q0[:]), 8192), (ap("thi"), lambda T: (T.thi[0:1, :], T.th[:]), 32),
-             (ap("X0", W), lambda T: (T.X0[:, W:W + 64], T.lx[:, 0:64]), 16384),
-             (ap("X0", 0, W), lambda T: (T.X0[:, 0:W], T.lx[:]), 2 ** 20), (ap("fwi"), lambda T: (T.fwi[:], T.fw[:]), 524288),
-             (ap("X1", W), lambda T: (T.X1[:, W:W + 64], T.lx[:, 0:64]), 16384),
-             (ap("X1", 0, W), lambda T: (T.X1[:, 0:W], T.lx[:]), 2 ** 20)]
+    loads = {"z": (ap("Z0"), lambda T: (T.Z0[:], T.z0[:]), 65536), "h": (ap("hwi"), lambda T: (T.hwi[:], T.hw[:]), 8192),
+             "a": (ap("awi"), lambda T: (T.awi[:], T.aw[:]), 262144), "s": (ap("swi"), lambda T: (T.swi[:], T.sw[:]), 262144),
+             "q": (ap("qi"), lambda T: (T.qi[0:8, :], T.q0[:]), 8192), "t": (ap("thi"), lambda T: (T.thi[0:1, :], T.th[:]), 32),
+             "x": (ap("X0", 0, W), lambda T: (T.X0[:, 0:W], T.lx[:]), 2 ** 20), "f": (ap("fwi"), lambda T: (T.fwi[:], T.fw[:]), 524288),
+             "y": (ap("X1", 0, W), lambda T: (T.X1[:, 0:W], T.lx[:]), 2 ** 20)}
     prev = None
-    for x, fn, nb in loads:
-        prev = dma([x], [], fn, nb, prev)
+    for k in LOADS:
+        x, fn, nb = loads[k.lower()]
+        prev = dma([x], [], fn, nb, prev, queue="Y" if k.islower() else "S")
+    ms(ap("ONE"), 1.0)
+    zv = PART[ZV][0]
+    ms(ap("HZ"), 0.0)
+    ms(ap("ZZ", 144, zv), 0.0)
+    for a in range(zv, cnt(ap("ZZ")), 384):
+        fill(ap("ZZ", a, min(a + 384, cnt(ap("ZZ")))), 0.0)
     iota(ap("PI", 0, 1), [[0, 1]], 0, 1)
     iota(ap("IO"), [[1, 112]])
-    dma([ap("FW", 1024)], [ap("IO", 0, 64)], lambda T: (T.FW[:, 1024:1088], T.IO[:, 0:64]), 32768, prev)
-    ms(ap("ONE"), 1.0)
-    ms(ap("ZZ", 0, ZV), 0.0)
-    for a in range(ZV, cnt(ap("ZZ")), 384):
-        fill(ap("ZZ", a, min(a + 384, cnt(ap("ZZ")))), 0.0)
+    for x in (ap("X0", W), ap("X1", W), ap("FW", 1024)):
+        fill(x, 0.0)
     ts(ap("PI", 1, 2), ap("PI", 0, 1), 15, A.bitwise_and)
     ts(ap("PI", 2, 3), ap("PI", 0, 1), 4, A.logical_shift_right)
     ts(ap("PI", 3, 4), ap("PI", 0, 1), 31, A.bitwise_and)
     cp(ap("CF", PF, P32 + 1), ap("PI"))
     ts(col(IS15), col(PM), 15.0, A.is_equal)
-    lin(col(C15), col(IS15), 15.0)
     ts(ap("G8"), ap("IO", 0, 8), col(PG), A.is_equal)
     cp(col(HWF), ap("hwi"))
     lin(ap("HZ", 15, 143, 16), ap("G8"), col(HWF))
-    first = PLACE[0]
-    for a, q, k, b in runs(first, 0, [0, 1, 2, 3], False):
-        lin(ap("Z0", 64 * a, 64 * (a + k)), ap("zin", 64 * q, 64 * (q + k)), 1.0, col(C15))
-    if GC:
-        for a in (0, 512):
-            asel(ap("FW", a, a + 512), ap("fwi", a, a + 512), [[0, 512]], A.is_ge, 0.0, 0, 0)
-    else:
-        cp(ap("FW", 0, 1024), ap("fwi"))
-    if PS:
-        gcopy(ap("AWF"), ap("awi"))
+    for a in (0, 512):
+        gcopy(ap("FW", a, a + 512), ap("fwi", a, a + 512))
+    ts(ap("PW"), ap("awi"), 32.0, A.add)
     ts(ap("SP"), ap("swi"), 2048.0, A.subtract)
-    ts(ap("RT0"), ap("awi"), 3232.0, A.mult, 65536.0, A.add)
-    ts(ap("RT"), ap("RT0"), 131071, A.bitwise_and)
+    lin(ap("RT"), ap("PW"), 3232.0, -37888.0 - 51 * 2 ** 17)
     iota(ap("IG"), [[1, 8], [0, 16]])
     iota(ap("IM"), [[0, 8], [1, 16]])
     asel(ap("I3"), ap("ONE", 0, 128), [[-1, 128]], A.is_equal, 0.0, 0, 1)
@@ -310,38 +310,46 @@ def setup():
     ts(ap("EX"), ap("I16"), col(P32), A.is_equal)
     ts(ap("G8T", 0, 128, 1, 0, 8), ap("IG", 0, 128, 1, 0, 8), col(PF, 0, 8), A.is_equal)
     ts(ap("M0"), ap("IM"), col(PM), A.not_equal, -16384.0, A.mult)
-    lin(ap("MO"), ap("M0"), 1.0, 4096.0)
     asel(ap("qf", 0, 256, 1, 0, 8), ap("qi", 0, 256, 1, 0, 8), [[0, 256]], A.is_ge, 0.0, 0, 0)
-    mm([(ap("pQ", 0, 256), ap("G8T", 0, 128, 1, 0, 8), ap("qf", 0, 256, 1, 0, 8))])
-    for a, q, k, b in runs(first, 0, [0, 1, 2, 3]):
-        tt(ap("Q0", 64 * a, 64 * (a + k)), ap("pQ", 64 * q, 64 * (q + k)), ap("MO", 0, 64 * k), A.add)
+    mm([(ap("pQ", 0, 256), ap("G8T", 0, 128, 1, 0, 8), ap("qf", 0, 256, 1, 0, 8))]
+       + [(ap("pQ", a, a + 128), ap("I3"), ap("M0")) for a in (0, 128)])
+    lin(ap("Q0"), ap("pQ", 0, 256), 1.0, 4096.0)
     ts(ap("GB"), ap("IG"), col(PG), A.is_equal)
     lin(col(PM3), col(PM), 3.0)
-    for i, m, a in [(ZSC, -1.0, 1.0), (VMIN, -240.0, 255.0), (WCOL, 61440.0, 4096.0)] + (
-            [(VS, 0.5005, 0.4995), (VB, -13.0, ROUND), (NI15, -1.0, 0.0)] if TS else [(VS, 0.5, 0.5), (VB, -12.75, -0.25)]):
+    for i, m, a in [(ZSC, -1.0, 1.0), (VMIN, -240.0, 255.0), (WCOL, -69632.0, 4096.0), (VS, 0.5005, 0.4995), (VB, 2.0, ROUND),
+                    (NI15, -1.0, 0.0), (OFF, -16384.0, 16384.0), (NOFF, 16384.0, -16384.0), (SPB, 2 / 128, -65 / 128)] + [
+                    (VMAX, -240.0, ROUND + 255.0)] * XS:
         lin(col(i), col(IS15), m, a)
+    lin(col(SPC), col(PM), 1 / 128, col(SPB))
+    lin(ap("DH", 1, 129), ap("M0"), 1.0, 16384.0)
+    lin(ap("LN", 0, 128), ap("M0"), -2.0, -32768.0)
+    mm([(ap("pQ", 256, 384), ap("I3"), ap(x, 0, 128)) for x in ("LN", "DH")])
+    lin(ap("DG"), ap("pQ", 256, 384), 1.0)
     lin(ap("WS", 0, 24, 3), ap("G8"), col(WCOL))
     lin(ap("WS", 2, 24, 3), ap("WS", 0, 24, 3), -1.0)
     lin(ap("WR"), ap("WS", 0, 24), -2.0)
     gfill(ap("MK", 0, None, 16), -32768.0)
-    asel(ap("M36"), ap("ZA", 0, 288), [[0, 8], [1, 36]], A.not_equal, BIG, 0, 0)
+    ms(ap("M36"), 0.0)
+    gfill(ap("M36", 0, None, 36), BIG)
     gfill(ap("M36", 34, None, 36), MAGIC)
     gfill(ap("M36", 35, None, 36), -MAGIC)
-    asel(ap("M51"), ap("ZA", 0, 408), [[0, 24], [1, 17]], A.not_equal, BIG, 0, 0)
+    ms(ap("M51"), 0.0)
+    gfill(ap("M51", 0, None, 17), BIG)
     iota(ap("KC36", 0, None, 1, 0, 1), [[0, 8], [65, 2], [3, 18]], -23)
     iota(ap("KC51", 0, None, 1, 0, 1), [[0, 8], [65, 3], [3, 17]], 1)
     for n, a, st in (("KC36", 17, 18), ("KC36", 34, 36), ("KC51", 33, 51), ("KC51", 50, 51)):
         gfill(ap(n, a, None, st, 0, 1), HUGE)
-    iota(ap("I48"), [[0, 16], [1, 48]])
-    ts(ap("OH", 0, 768), ap("I48"), col(PM3), A.is_equal)
+    ts(ap("OH", 0, 48), ap("IO", 0, 48), col(PM3), A.is_equal)
+    for a in (48, 96, 192, 384):
+        lin(ap("OH", a, 2 * a), ap("OH", 0, a), 1.0)
     ts(ap("OH", 47, 768, 48), ap("IO", 0, 16), col(PM), A.is_equal)
     ts(ap("OH", 768, 816), ap("IO", 0, 48), 1.0, A.subtract, col(PM3), A.is_equal)
-    ts(ap("OH", 816, 928), ap("IO"), 66.0, A.subtract, col(PM3), A.not_equal)
+    ts(ap("OH", 816, 880), ap("IO", 0, 64), 2.0, A.subtract, col(PM3), A.not_equal)
     ts(ap("CT", 0, 16), ap("ONE", 0, 16), col(PM3), A.mult, 16.0, A.mult)
-    for k, v in ((2, 768.0), (3, 816.0), (4, 60.0 * 2048)):
+    for k, v in ((2, 768.0), (3, 816.0)):
         gfill(ap("CT", 8 * k, 8 * k + 8), v)
+    lin(ap("CT", 32, 40), ap("ONE", 0, 8), col(OFF), 2048.0)
     iota(ap("CR", 0, 8, 1, 0, 1), [[768, 8]])
-    asel(ap("I2"), ap("ZA", 0, 128), [[0, 2], [-1, 64]], A.not_equal, 2.0, 0, 1)
     if SP3:
         iota(ap("LN"), [[0, 9], [1, 16]])
         gfill(ap("LN", 0, None, 16), 16.0)
@@ -357,16 +365,22 @@ def setup():
             lin(ap(n, 12, 16), ap(n, 12, 16), -2048.0)
         lin(ap(n, m * k), ap(n, 0, m * k), -1.0)
     iota(ap("ONF", 0, 128, 1, 0, 1), [[0, 128]], 1)
-    ts(ap("TH4", 0, 8, 1, 0, 1), ap("thi", 0, 8, 1, 0, 1), 4096.0, A.mult, 129.0, A.subtract)
+    ts(ap("TH4", 0, 8, 1, 0, 1), ap("thi", 0, 8, 1, 0, 1), 4096.0, A.mult, 129.0 + 240 * 4096, A.subtract)
+    iota(ap("KI"), [[0, 26]])
     iota(ap("VT"), [[0, 3], [16, 4]])
-    lin(ap("KP"), ap("VT"), 1.0, col(PM))
-    lin(ap("DUM", 0, 8), ap("KP", 0, 8), 1.0, 4096.0)
-    lin(ap("DUM", 8, 12), ap("KP", 8, 12), 1.0, 1024.0)
-    lin(ap("TW"), ap("KP"), 8192.0, -63.0 * 8192)
-    iota(ap("M64"), [[0, 768]], -8192)
-    gfill(ap("M64", 0, None, 64), HUGE)
-    for k in range(2):
-        iota(ap("IOT", 544 * k, 544 * k + 544), [[1, 544]], 544 * k)
+    iota(ap("KP", 0, 8), [[0, 2], [16, 4]], 4096)
+    iota(ap("KP", 8, 12), [[16, 4]], 1024)
+    lin(ap("VQ"), ap("KP"), 1.0, col(PM))
+    lin(ap("DUM"), ap("VQ"), 1.0, col(OFF))
+    lin(ap("DUS"), ap("VQ"), 2.0 ** -20)
+    for a in (0, 390):
+        ms(ap("M65", a, a + 390), -1 / 128)
+    gfill(ap("M65", 0, None, 65), HUGE)
+    lin(ap("M65", 64, None, 65), ap("VT"), -1 / 128)
+    gfill(ap("DD", 64, None, 65), HUGE)
+    iota(ap("IOT", 0, 544), [[1, 544]])
+    for a in (0, 272):
+        ts(ap("IOT", 544 + a, 816 + a), ap("IOT", a, 272 + a), 544.0, A.add)
 
 
 def front(s, p, n, units):
@@ -381,29 +395,42 @@ def front(s, p, n, units):
     ts(ap("I3I", o + 2 * m, o + 3 * m), ui, 3, A.logical_shift_right, 511, A.bitwise_and)
     cp(ap("O3", o, o + 3 * m), ap("I3I", o, o + 3 * m))
     ok, os_, oa = [ap("O3", o + k * m, o + k * m + m) for k in range(3)]
-    if (s, p) in PS:
-        lin(ap("PP", t0, t0 + n), ind(ap("AWF"), oa), 1.0, 32.0)
-    else:
-        ts(ap("PP", t0, t0 + n), ind(ap("awi"), oa), 32.0, A.add)
+    if p == 0:
+        ts(ap("KO"), ap("I3I", o, o + 4), col(OFF), A.add)
+    lin(ap("PP", t0, t0 + n), ind(ap("PW"), oa), 1.0)
     tt(ap("AP1", t0, t0 + n), ind(ap("SP"), os_), ap("PP", t0, t0 + n), A.mult)
     tt(ap("N1", 256 + t0, 256 + t0 + n), ind(ap("RT"), oa), ap("AP1", t0, t0 + n), A.add)
     tt(ap("N1", t0, t0 + n), ind(ap("FW" if s else "fwi", 0, 1024), ok), ap(Q, t0, t0 + n), A.max)
     for q, k in units:
-        u0, a = 64 * q, 512 * (s % 2) + 128 * q
-        ts(ap("NM", a + k, a + 2 * k), ap("N1", 256 + u0, 256 + u0 + k), 5, A.arith_shift_right, 4095, A.bitwise_and)
-        cp(ap("ON", a + k, a + 2 * k), ap("NM", a + k, a + 2 * k))
-        ts(ap("NM", a, a + k), ap("N1", u0, u0 + k), 4095, A.bitwise_and)
-        cp(ap("ON", a, a + k), ap("NM", a, a + k))
+        x, y, a = max(t0, 64 * q), min(t0 + n, 64 * q + k), 512 * (s % 2) + 64 * q
+        if x < y:
+            ts(ap("NM", a + k + x, a + k + y), ap("N1", 256 + x, 256 + y), 5, A.arith_shift_right, 4095, A.bitwise_and)
+            cp(ap("ON", a + k + x, a + k + y), ap("NM", a + k + x, a + k + y))
+            ts(ap("NM", a + x, a + y), ap("N1", x, y), 4095, A.bitwise_and)
+            cp(ap("ON", a + x, a + y), ap("NM", a + x, a + y))
+    for a in range(t0, t0 + n, 128):
+        k = min(n, 128)
+        zt = ap(bank(), 0, 128, 1, 0, k)
+        mm([(zt, ap(Z, a, a + k), ap("I3"))])
+        lin(ap("ZT", 2 * a, 2 * a + 128, 1, 0, k), zt, -1.0)
+        for x in range(0, k, 32):
+            TURNED[a + x] = (a, x)
 
 
 TURN = [0, 0]
+TURNED = {}
+
+
+def bank():
+    TURN[0] += 1
+    return "pD#%d" % TURN[0]
 
 
 def spans(md, letters, most):
     out = []
     for k, c in enumerate(md):
         if c in letters:
-            if out and out[-1][1] == 32 * k and out[-1][1] - out[-1][0] < most:
+            if out and out[-1][1] == 32 * k and out[-1][1] - out[-1][0] < most and (32 * k % most or most > 64):
                 out[-1] = (out[-1][0], 32 * k + 32)
             else:
                 out.append((32 * k, 32 * k + 32))
@@ -422,28 +449,28 @@ def bulk(s, p, md):
     def flat(name, a, b):
         return ap(name, 16 * (t0 + a), 16 * (t0 + b))
 
-    def bank():
-        TURN[0] += 1
-        return "pD#%d" % TURN[0]
-
     def greatest(src, a, b):
         for x in range(a, b, SL):
             y = min(b, x + SL)
             scan(lane(2, x, y), ap("MK", 0, 16 * (y - x)), src(x, y), 0.0, A.add, A.max)
 
-    if (s, p) in ZP or any("S" in MODE[c] for c in md):
-        zt = ap(bank(), 0, 128, 1, 0, n)
-        mm([(zt, ap(Z, t0, t0 + n), ap("I3"))])
-        lin(ap("ZT", 2 * t0, 2 * t0 + 128, 1, 0, n), zt, -1.0)
+    def minus_z(d, x):
+        a, r = TURNED[t0 + x]
+        return (d, ap("ZT", 2 * a, 2 * a + 128, 1, r, r + 32), ap("EX", 0, 512, 1, r, r + 32))
+
+    for a, b in spans(md, [c for c in MODE if c != "S"], 32) if (s, p) in ZG else ():
+        for r in range(4):
+            gcopy(ap("Z4", 4 * (t0 + a) + r, 4 * (t0 + b), 4), ap(Z, t0 + a, t0 + b))
+        for r in range(4):
+            gcopy(ap("ZR", 16 * (t0 + a) + r, 16 * (t0 + b), 4), ap("Z4", 4 * (t0 + a), 4 * (t0 + b)))
     for a, b in spans(md, [c for c in MODE if c != "S"], DW) if (s, p) in ZP else ():
         bk = bank()
-        mm([(ap(bk, 16 * (x - a), 16 * (x - a) + 512), ap("ZT", 2 * t0, 2 * t0 + 128, 1, x, x + 32), ap("EX", 0, 512, 1, x, x + 32))
-            for x in range(a, b, 32)], each=1)
+        mm([minus_z(ap(bk, 16 * (x - a), 16 * (x - a) + 512), x) for x in range(a, b, 32)], each=1)
         lin(flat("ZR", a, b), ap(bk, 0, 16 * (b - a)), -1.0)
-    for a, b in spans(md, [c for c in MODE if c != "S"], NZ) if (s, p) not in ZP else ():
+    for a, b in spans(md, [c for c in MODE if c != "S"], NZ) if (s, p) not in ZP + ZG else ():
         z0 = TURN[1] if TURN[1] + 16 * (b - a) <= 16 * NZ else 0
         TURN[1] = z0 + 16 * (b - a)
-        (gcopy if s and ZG else cp)(ap("ZS", z0, TURN[1], 16), ap(Z, t0 + a, t0 + b))
+        cp(ap("ZS", z0, TURN[1], 16), ap(Z, t0 + a, t0 + b))
         for x in range(a, b, SL):
             y = min(b, x + SL)
             scan(flat("ZR", x, y), ap("MK", 0, 16 * (y - x)), ap("ZS", z0 + 16 * (x - a), z0 + 16 * (y - a)), 0.0, A.add, A.max)
@@ -461,8 +488,7 @@ def bulk(s, p, md):
                 lst = []
                 for x in range(x0, y0, 32):
                     d = ap(bk, 16 * (x - x0), 16 * (x - x0) + 512)
-                    lst += [(d, ap("ZT", 2 * t0, 2 * t0 + 128, 1, x, x + 32), ap("EX", 0, 512, 1, x, x + 32)),
-                            (d, ap("I3"), flat(raw, x, x + 32))]
+                    lst += [minus_z(d, x), (d, ap("I3"), flat(raw, x, x + 32))]
                 mm(lst, each=2)
                 act(lane(k, x0, y0), ap(bk, 0, 16 * (y0 - x0)), F.Abs)
             if k:
@@ -500,7 +526,7 @@ def spread(out, zname, z0, rhs, c0, cols, n):
 KEYS = []
 
 
-def tail(s, p, md):
+def tail(s, p, md, halves, nxt):
     n = 32 * len(md)
     t0, m = 64 * p, n // 16
     K = "pK#%d" % len(KEYS)
@@ -536,10 +562,12 @@ def tail(s, p, md):
         za, z0 = "ZL", 0
         KEYS.append(scan(sl("SL", 0, 408), sl("M51", 0, 408), sl(K, 0, 408), 0.0, A.add, A.min))
         tt(sl("KI", 0, 8), sl("SL", 16, 408, 51), sl("SL", 33, 408, 51), A.min)
-        tt(sl("KI", 8, 16), sl("SL", 15, 408, 51), sl("SL", 33, 408, 51), A.max)
-        cp(sl("KI", 16, 24), sl("SL", 50, 408, 51))
-        ts(sl("KC6", 0, 24), sl("KI", 0, 24), 63, A.bitwise_and)
-        cp(sl("ZL", 0, 256, 16), sl("KC6", 0, 16))
+        tt(sl("KI", 9, 17), sl("SL", 15, 408, 51), sl("SL", 33, 408, 51), A.max)
+        tt(sl("CW", 0, 8), sl("SL", 33, 408, 51), sl("SL", 16, 408, 51), A.is_lt)
+        cp(sl("KI", 18, 26), sl("SL", 50, 408, 51))
+        ts(sl("KC6", 0, 26), sl("KI", 0, 26), 63, A.bitwise_and)
+        cp(sl("ZL", 0, 272, 16), sl("KC6", 0, 17))
+        tt(sl("ZL", 288, 416, 16), sl("KC6", 18, 26), sl("CW", 0, 8), A.mult)
     shift = 23.0 if p else -1.0
     ow = 48 * s + 12 * p
     pw = 48 + ow
@@ -548,83 +576,80 @@ def tail(s, p, md):
        + spread(ap("pH", pw, pw + 3 * m), za, z0, "RB%d" % m, 0, 3 * m, n))
     ts(ap("OW", ow, ow + 3 * m), ap("pH", pw, pw + 3 * m), shift, A.add)
     last = s == RO - 1
-    act(ap("ZN%d" % s, t0, t0 + n), ind(ap("B", 48 * t0, 48 * (t0 + n)), ap("OW", ow, ow + m)), F.Abs,
-        bias=(0.0 if last else col(C15)), scale=col(ZSC))
-    a, b, c_ = 2 * t0, 2 * t0 + n, 2 * t0 + 2 * n
-    nm = 512 * (s % 2)
-    tt(ap("MN", a, c_), ind(ap("OH"), ap("OW", ow + m, ow + 3 * m)), ap("NM", nm + a, nm + c_), A.mult)
-    if not last:
-        pq = ap("pQ", t0, t0 + n)
-        lst = [(pq, ap("GB"), ap("MN", a, b)), (pq, ap("GB"), ap("MN", b, c_))]
-        if (QS >> (1 if p else 0)) & 1:
-            mm([(pq, ap("I3"), ap("M0", 0, n))] + lst)
-            lin(ap("QN%d" % s, t0, t0 + n), pq, 1.0, 4096.0)
+    a, nm = 2 * t0, 512 * (s % 2)
+    tt(ap("MN", a, a + 2 * n), ind(ap("OH"), ap("OW", ow + m, ow + 3 * m)), ap("NM", nm + a, nm + a + 2 * n), A.mult)
+    for x, q, k, _ in runs(halves, 0, nxt, False):
+        act(ap("ZN%d" % s, 64 * q, 64 * (q + k)), ind(ap("B", 48 * t0, 48 * (t0 + n)), ap("OW", ow + 4 * x, ow + 4 * (x + k))),
+            F.Abs, scale=col(ZSC))
+    rows = 8 if last else 128
+    for _, q, k, _ in runs(sorted(halves, key=nxt.index), 0, nxt, False):
+        pq = ap("pQ", 64 * q, 64 * (q + k), 1, 0, rows)
+        sums = [(ap("pQ", 64 * y, 64 * y + 64, 1, 0, rows), ap("G8" if last else "GB"), ap("MN", c, c + 64))
+                for y in range(q, q + k) for c in (a + 64 * halves.index(nxt[y]), a + n + 64 * halves.index(nxt[y]))]
+        if last:
+            mm(sums, each=2)
+            lin(ap("YQ", 64 * q, 64 * (q + k), 1, 0, 8), pq, 1.0)
         else:
-            mm(lst)
-            tt(ap("QN%d" % s, t0, t0 + n), pq, ap("MO", 0, n), A.add)
-    else:
-        o = ap("pQ", 320, 320 + n, 1, 0, 8)
-        mm([(o, ap("G8"), ap("MN", a, b)), (o, ap("G8"), ap("MN", b, c_))])
-        act(ap("YQ", t0, t0 + n, 1, 0, 8), o, F.Identity)
+            mm([(pq, ap("I3"), ap("M0", 0, 64 * k))] + sums)
+            lin(ap("QN%d" % s, 64 * q, 64 * (q + k)), pq, 1.0, 4096.0)
     c, c2 = 32 * (s % 2) + 8 * p, 144 * (s % 2)
     if not last or not p:
-        act(sl("NW", c, c + 8) if p else sl("NL", c2, c2 + 128, 16), sl(za, z0, z0 + 128, 16), F.Relu,
-            bias=4096.0 * (shift - 46.0), scale=4096.0)
+        o, x = sl("NW", c, c + 8) if p else sl("NL", c2, c2 + 128, 16), sl(za, z0, z0 + 128, 16)
+        if NV:
+            ts(o, x, 47.0 - shift, A.is_equal, 4096.0, A.mult)
+        else:
+            act(o, x, F.Relu, bias=4096.0 * (shift - 46.0), scale=4096.0)
 
 
 def learn(s, n):
     def sl(name, a, b, st=1):
         return ap(name, a, b, st, 0, 64)
-    ts(sl("K64", 0, 8), sl("KI", 0, 8), 64, A.bitwise_and)
-    tt(sl("ZJ", 0, 128, 16), sl("KC6", 16, 24), sl("K64", 0, 8), A.add)
-    ol = [mm([(ap("pL", c, c + 8), ap("I3"), ap("CT", 8 + 2 * c, 24 + 2 * c, 2))]
-             + spread(ap("pL", c, c + 8), z, z0, "RB4", c, 8, 64)) for c, z, z0 in ((0, "ZL", 128), (8, "ZJ", 0))]
+    for c, z0 in ((0, 144), (8, 288)):
+        mm([(ap("pL", c, c + 8), ap("I3"), ap("CT", 8 + 2 * c, 24 + 2 * c, 2))] + spread(ap("pL", c, c + 8), "ZL", z0, "RB4", c, 8, 64))
     for a, b in ([(0, 8), (8, 12)] if OLS else [(0, 12)]):
         ts(ap("OL", a, b), ap("pL", a, b), -1.0, A.add)
-    tt(ap("SC2", 143, 192, 16), ap("pL", 12, 16), ap("I3I", 48 * s, 48 * s + 4), A.max)
+    tt(ap("SC2", 143, 192, 16), ap("pL", 12, 16), ap("KO"), A.max)
     a = 512 * (s % 2)
     if n == 64:
         tt(ap("ML"), ind(ap("OH"), ap("OL", 0, 8)), ap("NM", a, a + 128), A.mult)
     else:
         tt(ap("ML", 0, 64), ind(ap("OH"), ap("OL", 0, 4)), ap("NM", a, a + 64), A.mult)
         tt(ap("ML", 64, 128), ind(ap("OH"), ap("OL", 4, 8)), ap("NM", a + n, a + n + 64), A.mult)
-    g, c2 = "L%d" % s, 144 * (s % 2)
+    c2, ds = 144 * (s % 2), DS_[s]
     scan(sl("LN", 0, 128), sl("MK", 0, 128), sl("NL", c2, c2 + 128), 0.0, A.add, A.max)
-    for c, own, plain, src, x2, u in ((192, 192, 256, "MN", n, 64), (64, 128, 64, "ML", 64, 0)):
-        mm([(ap("pL", c, c + 128), sl("LN", 0, 128), sl("I2", 0, 128)), (ap("pL", own, own + 64), ap("I3"), ap("M0", 0, 64))]
-           + [(ap("pL", y, y + 64), ap("GB"), ap(src, x, x + 64)) for y in (own, plain) for x in (0, x2)])
-        act(ap("U", u, u + 64), ap("pL", plain, plain + 64), F.Identity)
-    scan(ap("SC2", 0, 128), ap("MK", 0, 128), ap("pL", 128, 256), 0.0, A.add, A.max)
-    if "l" in DS_ or "w" in DS_:
-        lin(ap("NB", 0, 8), ap("SC2", 15, 128, 16), -float(2 ** 20))
+    mm([(ap("pL", 128, 256), sl("LN", 0, 128), sl("WRB4", 0, 128))] * 2
+       + [(ap("pL", y, y + 64), ap("GB"), ap(src, x, x + 64)) for y, src, x2 in ((192, "MN", n), (128, "ML", 64)) for x in (0, x2)])
+    scan(ap("SC2", 0, 128), ap("DG"), ap("pL", 128, 256), 0.0, A.add, A.max)
+    act(ap("U", 0, 128), ap("pL", 128, 256), F.Identity)
+    if "l" in ds or "w" in ds:
+        lin(ap("NB", 0, 8), ap("SC2", 15, 128, 16), -1.0, col(OFF))
     for a, b in LISTS[s]:
         tt(ap("VP", a, b), ap("SC2", 16 * a + 15, 16 * b, 16), ap("DUM", a, b), A.min)
-        cp(ap("OV", a, b), ap("VP", a, b))
-        tt(ap("VT", a, b), ap("VP", a, b), ap("TW", a, b), A.add)
+        ts(ap("OV", a, b), ap("VP", a, b), col(OFF), A.subtract)
+        ts(ap("VT", a, b), ap("VP", a, b), 2.0 ** -20, A.mult, col(SPC), A.add)
         if b == 12:
             (cp if US else lambda o, x: act(o, x, F.Identity))(ap("U", 128, 192), ind(ap("IOT"), ap("OV", 8, 12)))
-            if "k" in DS_:
-                lin(ap("NB", 8, 12), ap("VP", 8, 12), -float(2 ** 20))
+            if "k" in ds:
+                lin(ap("NB", 8, 12), ap("VP", 8, 12), -1.0, col(OFF))
         for k in range(a, b):
-            d, u = ap("DD", 64 * k, 64 * k + 64), ap("U", 64 * (k // 4), 64 * (k // 4) + 64)
-            if "lwk"[k // 4] in DS_:
-                act(d, u, F.Abs, bias=ap("NB", k, k + 1), scale=float(2 ** 20))
+            d, u = ap("DD", 65 * k, 65 * k + 64), ap("U", 64 * (k // 4), 64 * (k // 4) + 64)
+            if "lwk"[k // 4] in ds:
+                act(d, u, F.Abs, bias=ap("NB", k, k + 1))
             else:
-                ts(d, u, ap("VP", k, k + 1) if k >= 8 else ap("SC2", 16 * k + 15, 16 * k + 16), A.not_equal, float(2 ** 20), A.mult)
-        scan(ap("DS", 64 * a, 64 * b), ap("M64", 64 * a, 64 * b), ap("DD", 64 * a, 64 * b), 0.0, A.add, A.min)
-        tt(ap("KP", a, b), ap("VT", a, b), ap("DS", 64 * a + 63, 64 * b, 64), A.subtract)
-        tt(ap("VQ", a, b), ap("KP", a, b), ap("DUM", a, b), A.min)
-        cp(ap("OK%d" % s, a, b), ap("VQ", a, b))
+                ts(d, u, ap("VP", k, k + 1) if k >= 8 else ap("SC2", 16 * k + 15, 16 * k + 16), A.subtract, col(NOFF), A.not_equal)
+        scan(ap("DS", 65 * a, 65 * b), ap("M65", 65 * a, 65 * b), ap("DD", 65 * a, 65 * b), 0.0, A.add, A.min)
+        tt(ap("KP", a, b), ap("VT", a, b), ap("DS", 65 * a + 64, 65 * b, 65), A.subtract)
+        tt(ap("VQ", a, b), ap("KP", a, b), ap("DUS", a, b), A.min)
+        ts(ap("OK%d" % s, a, b), ap("VQ", a, b), 2.0 ** 20, A.mult)
     X = ap("X%d" % (s % 2))
     tt(ap("T1"), ind(X, ap("OV", 4, 8)), ap("Z%d" % s, 0, 64), A.add)
-    if TS:
-        lin(ap("T3"), ap("T1"), col(VS), col(VB))
-        ts(ap("XW%d" % s), ap("T3"), ROUND, A.subtract, col(VMIN), A.min)
-        act(ap("XL%d" % s), ind(X, ap("OV", 0, 4)), F.Relu, bias=col(NI15))
+    lin(ap("T3"), ap("T1"), col(VS), col(VB))
+    if XS:
+        act(ap("T1"), ap("T3"), F.Relu, bias=col(VMAX), scale=-1.0)
+        lin(ap("XW%d" % s), ap("T1"), -1.0, col(VMIN))
     else:
-        ts(ap("T2"), ap("T1"), col(VS), A.mult, col(VB), A.add)
-        ts(ap("XW%d" % s), ap("T2"), col(VMIN), A.min)
-        ts(ap("XL%d" % s), ind(X, ap("OV", 0, 4)), col(IS15), A.subtract, 0.0, A.max)
+        ts(ap("XW%d" % s), ap("T3"), ROUND, A.subtract, col(VMIN), A.min)
+    act(ap("XL%d" % s), ind(X, ap("OV", 0, 4)), F.Relu, bias=col(NI15))
     tt(ap("F1"), ind(ap("FW"), ap("OV", 8, 12)), ap("U", 64, 128), A.subtract)
     tt(ap("F2"), ind(ap("OH"), ap("OL", 8, 12)), ap("F1"), A.mult)
     tt(ind(ap("FW"), ap("OK%d" % s, 8, 12)), ap("F2"), ap("U", 64, 128), A.add)
@@ -651,30 +676,31 @@ def program():
     for s in range(RO):
         places = [PLACE[s].index(u[0]) for u, md in UNITS[s]]
         sizes = [64 * len(u) for u, md in UNITS[s]]
-        w = 4 if s == 0 and F0 else 2
-        for p in range(0, 4, w):
-            front(s, p, 64 * w, [(q, n) for q, n in zip(places, sizes) if p <= q < p + w])
+        for p, w in FRONTS[s]:
+            front(s, p, 64 * w, list(zip(places, sizes)))
         last = s == RO - 1
         nxt = [0, 1, 2, 3] if last else PLACE[s + 1]
         for (u, md), p, n in zip(UNITS[s], places, sizes):
             bulk(s, p, md)
-            tail(s, p, md)
-            for (a, q, k, b) in runs(u, p, nxt, not last):
-                sa, sb, da, db = 64 * a, 64 * (a + k), 64 * q, 64 * (q + k)
-                if last:
-                    dma([], [ap("ZN2", sa, sb)], lambda T, sa=sa, sb=sb, da=da, db=db: (T.yz[:, da:db], T.ZN2[:, sa:sb]), 65536)
-                    dma([], [ap("YQ", sa, sb)], lambda T, sa=sa, sb=sb, da=da, db=db: (T.yq[:, da:db], T.YQ[0:8, sa:sb]), 4096)
-                else:
-                    send(ap("ZN%d" % s, sa, sb), ap("Z%d" % (s + 1), da, db), 1 + b + s)
-                    send(ap("QN%d" % s, sa, sb), ap("Q%d" % (s + 1), da, db), 1 + b + s)
+            tail(s, p, md, u, nxt)
+            for _, q, k, b in runs(sorted(u, key=nxt.index), 0, nxt) if not last else ():
+                x, y = 64 * q, 64 * (q + k)
+                send(ap("ZN%d" % s, x, y), ap("Z%d" % (s + 1), x, y), 1 + b + s)
+                landed = send(ap("QN%d" % s, x, y), ap("Q%d" % (s + 1), x, y), 1 + b + s)
             if p == 0:
                 learn(s, n)
                 update(s, (s + 1) % 2)
                 if last:
-                    i = dma([], [ap("FW")], lambda T: (T.yf[:], T.FW[:, 0:1024]), 2 ** 19)
-                    dma([], [ap("X1")], lambda T: (T.yx[:], T.X1[:, 0:W]), 2 ** 20, i)
-        if not last:
+                    two = [([], [ap("FW")], lambda T: (T.yf[:], T.FW[:, 0:1024]), 2 ** 19),
+                           ([], [ap("X1")], lambda T: (T.yx[:], T.X1[:, 0:W]), 2 ** 20)]
+                    dma(*two[1 - XF], dma(*two[XF]))
+        if not last and XC:
+            dma([ap("X%d" % (s % 2))], [ap("X%d" % (1 - s % 2))], lambda T, s=s: (T["X%d" % (s % 2)][:], T["X%d" % (1 - s % 2)][:]),
+                2 ** 20, None, [landed])
+        elif not last:
             update(s, s % 2)
+    dma([], [ap("ZN2")], lambda T: (T.yz[:], T.ZN2[:]), 65536)
+    dma([], [ap("YQ")], lambda T: (T.yq[:], T.YQ[0:8, :]), 8192, queue="S")
 
 
 def meet(a, b):
@@ -719,12 +745,12 @@ def reduce_deps(order, extra):
 
 def prices(m):
     cost = [o["c"][0] + (o["c"][1] + o["c"][2] * m[1] + o["c"][3] * m[2]) * m[0] + o["c"][4] * m[3]
-            + (m[5] if o["eng"] in "VS" else 0.0) for o in OPS]
-    cost = [o["lat"] / m[7] if o["eng"] == "E" else c for o, c in zip(OPS, cost)]
+            + {"V": m[5], "S": m[10]}.get(o["eng"], 0.0) for o in OPS]
+    cost = [100 + o["lat"] / m[7] if o["eng"] == "E" else {"dma": m[12], "send": m[13]}.get(o["lat"], c) for o, c in zip(OPS, cost)]
     cost[[o["eng"] for o in OPS].index("R") - 1] += m[9]
     lat = [m[8] if o["eng"] == "R" else (m[6] if o["eng"] == "D" else 0.0) for o in OPS]
-    pred = [[(j, lat[j] + (0.0 if o["eng"] in "RDE" or o["eng"] + OPS[j]["eng"] in ("PP", "YY") else m[4]))
-             for j in o["dep"]] for o in OPS]
+    pred = [[(j, lat[j] + (0.0 if o["eng"] in "RDE" or o["eng"] + OPS[j]["eng"] == "PP" or OPS[j]["lat"] == "dma" else
+                           m[11] if o["eng"] == OPS[j]["eng"] else m[4])) for j in o["dep"]] for o in OPS]
     return cost, pred, lat, m[4]
 
 
@@ -822,7 +848,7 @@ def replay(order, edge, cost, pred, lat, wait, a=0, old=None, last=None):
 ENG, DIFF, AFTER, MARK, SINK = [], [], [], [], []
 
 
-def schedule(seed, rounds, tries, moves):
+def schedule(seed, rounds, tries):
     n = len(OPS)
     ENG[:] = [o["eng"] for o in OPS]
     DIFF[:] = [o["diff"] for o in OPS]
@@ -883,58 +909,231 @@ def schedule(seed, rounds, tries, moves):
         new = settle(key, pr[rnd.randint(len(pr))] if rnd.rand() < 0.3 else pr[0])
         if new[0] < best[0]:
             best = new
-    cur = best
-    for k in range(moves):
-        order = cur[1]
-        end, fin, why, i = cur[2][rnd.randint(len(pr))]
-        if rnd.rand() < FILL:
-            a = rnd.randint(n)
+    return best[1]
+
+
+def improve(order, seed, moves, hot, cold):
+    n = len(OPS)
+    reduce_deps(range(n), {})
+    pr = [prices(m) for m in GUESS]
+    rnd = np.random.RandomState(seed)
+    base = [sum(p[0]) / 3.0 for p in pr]
+    anc = [0] * n
+    for i in range(n):
+        for j in OPS[i]["true"]:
+            anc[i] |= anc[j] | 1 << j
+    delay = [[0.0, p[3]] for p in pr]
+    pred, succ = [[] for _ in OPS], [[] for _ in OPS]
+    for i in range(n):
+        for k, (j, d) in enumerate(pr[0][1][i]):
+            pred[i].append((j, len(delay[0])))
+            succ[j].append((i, len(delay[0])))
+            for p, dl in zip(pr, delay):
+                dl.append(p[1][i][k][1])
+    for i in SINK:
+        succ[i].append((n, len(delay[0])))
+        for p, dl in zip(pr, delay):
+            dl.append(p[2][i])
+    cost = [p[0] + [0.0] for p in pr]
+    own = [a[0][0] if a and a[0][1] == 0 else -1 for a in AFTER]
+    other = [[q for q, d in a if d] for a in AFTER]
+    role = [0 if not DIFF[i] else (1 if ENG[i] == "P" else 2) for i in range(n)]
+    mates = [[(x, y) for x in MARK[i][1:] for y in other[i] if (x - 5) // 3 == (y - 5) // 3] for i in range(n)]
+
+    def links(seg, last, w, read):
+        res = []
+        for i in seg:
+            l = pred[i]
+            if own[i] >= 0:
+                l = l + [(last[own[i]], 0)]
+                for x in other[i]:
+                    l.append((last[x], 1))
+                if role[i] == 1:
+                    if w >= ND:
+                        if w - ND >= len(read):
+                            return None
+                        l.append((read[w - ND], 1))
+                    w += 1
+                elif role[i] == 2:
+                    read.append(i)
+                for x in MARK[i]:
+                    last[x] = i
+            res.append(l)
+        return res
+
+    order = list(order)
+    pos = [n] * (n + 1)
+    for k, i in enumerate(order):
+        pos[i] = k
+    read = []
+    ln = dict(zip(order, links(order, [n] * 16, 0, read)))
+    wrote = [i for i in order if role[i] == 1]
+    before, after, wb, rb = [None] * (n + 1), [None] * (n + 1), [0] * (n + 1), [0] * (n + 1)
+    before[0], after[n] = [n] * 16, [n] * 16
+    F, Q, end = [[0.0] * (n + 1) for p in pr], [[0.0] * (n + 1) for p in pr], [0.0] * len(pr)
+    out = [list(s) for s in succ]
+    for i in order:
+        for j, d in ln[i][len(pred[i]):]:
+            if j < n:
+                out[j].append((i, d))
+
+    def marks(a, b):
+        last, w, r, k = before[a][:], wb[a], rb[a], a
+        while k < n:
+            i = order[k]
+            k += 1
+            for x in MARK[i]:
+                last[x] = i
+            w += role[i] == 1
+            r += role[i] == 2
+            if k >= b and before[k] == last:
+                break
+            before[k], wb[k], rb[k] = last[:], w, r
+        nxt, k = after[b][:], b
+        while k > 0:
+            k -= 1
+            for x in MARK[order[k]]:
+                nxt[x] = order[k]
+            if k < a and after[k] == nxt:
+                break
+            after[k] = nxt[:]
+
+    def times(a, b):
+        sc = 0.0
+        for m in range(len(pr)):
+            c, dl = cost[m], delay[m]
+            for f, seq, arcs in ((F[m], order[a:], ln), (Q[m], order[b - 1::-1], out)):
+                for i in seq:
+                    t = 0.0
+                    for j, d in arcs[i]:
+                        x = f[j] + dl[d]
+                        if x > t:
+                            t = x
+                    f[i] = t + c[i]
+            end[m] = max(Q[m])
+            sc += (end[m] + SMOOTH * sum(F[m]) / n) / base[m]
+        return sc / len(pr)
+
+    def relink(ops, new):
+        for i, l in zip(ops, new):
+            for j, d in ln[i][len(pred[i]):]:
+                if j < n:
+                    out[j].remove((i, d))
+            for j, d in l[len(pred[i]):]:
+                if j < n:
+                    out[j].append((i, d))
+            ln[i] = l
+
+    def freed(a, b, rd):
+        return [(rd[r], wrote[r + ND], 1) for r in range(rb[a], min(len(rd), len(wrote) - ND)) if pos[wrote[r + ND]] >= b]
+
+    def change(seg, a, b):
+        last, rd = before[a][:], read[:rb[a]]
+        l2 = links(seg, last, wb[a], rd)
+        if l2 is None:
+            return 1e9, None, None
+        nxt, was, tot = after[b], before[b], 0.0
+        cross = [(last[x], nxt[x], 0) for x in range(5)] + freed(a, b, rd)
+        for j in seg:
+            for i, d in succ[j]:
+                if pos[i] >= b:
+                    cross.append((j, i, d))
+            for x, y in mates[j]:
+                if last[x] == j:
+                    cross.append((j, nxt[y], 1))
+        for c, dl, bs, e, f0, q in zip(cost, delay, base, end, F, Q):
+            f, s, top = f0[:], 0.0, 0.0
+            for i, l in zip(seg, l2):
+                t = 0.0
+                for j, d in l:
+                    x = f[j] + dl[d]
+                    if x > t:
+                        t = x
+                x = f0[i]
+                t += c[i]
+                s += t - x
+                f[i] = t
+                x += q[i] - c[i]
+                if x > top:
+                    top = x
+            t = e if top < e - 1e-6 else 0.0
+            for j, i, d in cross:
+                x = f[j] + dl[d] + q[i]
+                if x > t:
+                    t = x
+            s += (f[last[0]] + f[last[1]] + f[last[2]] - f0[was[0]] - f0[was[1]] - f0[was[2]]) * (n - b) / 6.0
+            tot += (t - e + SMOOTH * s / n) / bs
+        return tot / len(pr), l2, rd
+
+    def take(seg, a, b, l2, rd):
+        touch = set(x for x in after[b] if x < n) | set(x[1] for x in freed(a, b, rd))
+        order[a:b] = seg
+        for k in range(a, b):
+            pos[order[k]] = k
+        read[rb[a]:len(rd)] = rd[rb[a]:]
+        ws = [i for i in seg if role[i] == 1]
+        wrote[wb[a]:wb[a] + len(ws)] = ws
+        marks(a, b)
+        relink(seg, l2)
+        for i in sorted(touch):
+            k = pos[i]
+            relink([i], links([i], before[k][:], wb[k], read[:rb[k]]))
+        return times(a, b)
+
+    def chain(m, i):
+        f, c, dl, res = F[m], cost[m], delay[m], []
+        while f[i] - c[i] > 1e-6:
+            t = f[i] - c[i] - 1e-6
+            for j, d in ln[i]:
+                if f[j] + dl[d] > t:
+                    break
+            if not anc[i] >> j & 1:
+                res.append((j, i))
+            i = j
+        return res
+
+    marks(0, n)
+    best = (times(0, n), order[:], end[:])
+    crit = {}
+    for k, z in enumerate(rnd.rand(moves, 8).tolist()):
+        m = int(z[0] * len(pr))
+        if z[1] < FILL:
+            a = int(z[2] * n)
             j = order[a]
-            if why[j] is None or not anc[j] >> why[j] & 1 or ENG[j] not in "VSP":
+            if not 0 <= own[j] <= 2 or F[m][j] - cost[m][j] - F[m][before[a][own[j]]] < 1.0:
                 continue
-            later = [x for x in order[a + 1:a + 60] if ENG[x] == ENG[j] and not anc[x] >> j & 1][:8]
+            later = [x for x in order[a + 1:a + 60] if own[x] == own[j] and not anc[x] >> j & 1][:8]
             if not later:
                 continue
-            i = later[rnd.randint(len(later))]
-            b = order.index(i) + 1
-            seg = order[a:b]
-            new = [x for x in seg if anc[i] >> x & 1] + [i] + [x for x in seg[:-1] if not anc[i] >> x & 1]
-            new = judge(order[:a] + new + order[b:], a, cur[2])
-            if new[0] < cur[0] - HEAT * (1 - k / moves) * np.log(rnd.rand() + 1e-12):
-                cur = new
-                if cur[0] < best[0]:
-                    best = cur
-            continue
-        if rnd.rand() < 0.3:
-            i = order[rnd.randint(n)]
-        pairs = []
-        while why[i] is not None:
-            if not anc[i] >> why[i] & 1:
-                pairs.append((why[i], i))
-            i = why[i]
-        if not pairs:
-            continue
-        j, i = pairs[rnd.randint(len(pairs))]
-        a, b = order.index(j), order.index(i) + 1
-        far = int(rnd.rand() ** 3 * 40)
-        if rnd.rand() < 0.5:
-            a = max(0, a - far)
-            seg = order[a:b]
-            new = [x for x in seg if anc[i] >> x & 1] + [i] + [x for x in seg[:-1] if not anc[i] >> x & 1]
+            i = later[int(z[3] * len(later))]
+            b, ahead = pos[i] + 1, True
         else:
-            b = min(n, b + far)
-            seg = order[a:b]
-            new = [x for x in seg[1:] if not anc[x] >> j & 1] + [j] + [x for x in seg if anc[x] >> j & 1]
-        new = judge(order[:a] + new + order[b:], a, cur[2])
-        if new[0] < cur[0] - HEAT * (1 - k / moves) * np.log(rnd.rand() + 1e-12):
-            cur = new
-            if cur[0] < best[0]:
-                best = cur
+            if z[2] < 0.3:
+                pairs = chain(m, order[int(z[3] * n)])
+            else:
+                if m not in crit:
+                    crit[m] = chain(m, max((F[m][i] + Q[m][i] - cost[m][i], i) for i in SINK)[1])
+                pairs = crit[m]
+            if not pairs:
+                continue
+            j, i = pairs[int(z[4] * len(pairs))]
+            far, ahead = int(z[5] ** 3 * 40), z[6] < 0.5
+            a, b = (max(0, pos[j] - far), pos[i] + 1) if ahead else (pos[j], min(n, pos[i] + 1 + far))
+        seg = order[a:b]
+        if ahead:
+            seg = [x for x in seg if anc[i] >> x & 1] + [i] + [x for x in seg[:-1] if not anc[i] >> x & 1]
+        else:
+            seg = [x for x in seg[1:] if not anc[x] >> j & 1] + [j] + [x for x in seg if anc[x] >> j & 1]
+        d, l2, rd = change(seg, a, b)
+        if d <= -(hot + (cold - hot) * k / moves) * np.log(z[7] + 1e-12):
+            sc = take(seg, a, b, l2, rd)
+            crit = {}
+            if sc < best[0]:
+                best = (sc, order[:], end[:])
     return best
 
 
 SMOOTH = 0.3
-HEAT = 0.0002
 FILL = 0.5
 
 
@@ -945,8 +1144,9 @@ def build():
     TURN[:] = [0, 0]
     program()
     depend()
-    score, order, res = schedule(*SEEDS)
-    ends = [r[0] for r in res]
+    order, ends = schedule(*SEEDS), []
+    for k, (moves, hot, cold) in enumerate(STAGES):
+        score, order, ends = improve(order, SEEDS[0] + k, moves, hot, cold)
     held, edge = rotate(order)
     extra = dict((i, set([j])) for i, j in edge.items() if j is not None)
     for u, b in held.items():

import numpy as np
from concourse.mybir import AluOpType, ActivationFunctionType

A = AluOpType
F = ActivationFunctionType
NR, W, RO = 4, 4096, 3
UNITS = [[((0,), "SV"), ((1,), "SV"), ((2, 3), "SSSV")],
         [((1, 0), "SSSV"), ((2,), "SV"), ((3,), "SS")],
         [((2, 1), "SSSV"), ((0, 3), "SSSV")]]
PLACE = [[0, 1, 2, 3], [1, 0, 2, 3], [2, 1, 0, 3]]
FRONTS = [[(0, 4)], [(0, 1), (1, 1), (2, 2)], [(0, 1), (1, 2), (3, 1)]]
MODE = {"S": "SS", "V": "VV", "M": "SV", "N": "VS", "H": "HH", "J": "SH", "K": "HV", "L": "VH"}
LISTS = [[(0, 12)], [(0, 12)], [(8, 12), (0, 8)]]
GV = 32
GS = 64
NZ = 64
US = 1
DS_ = ["lw", "w", ""]
OLS = 1
SP3 = 1
PL = 1
DW = 64
ZP = [(0, 0), (0, 1), (0, 2)]
ZG = []
XC = 1
XS = 0
LOADS = "zHasxqfty"
ZV = "ZA"
XF = 0
NV = 0
SL = 32
ROUND = 1.5 * 2 ** 23
ND = 2
BIG = float(2 ** 26)
HUGE = float(2 ** 31)
MAGIC = 1.5 * 2 ** 29

UNITS = [[((0, 1), "SSVV"), ((2, 3), "SSMV")], [((1, 0), "SSVV"), ((2, 3), "SSMV")], [((2,), "VV"), ((1, 0), "SSSM"), ((3,), "SM")]]
GV, US, OLS, XS = 32, 1, 1, 0
PLACE = [[0, 1, 2, 3], [1, 0, 2, 3], [2, 3, 1, 0]]
FRONTS = [[(0, 4)], [(0, 2), (2, 2)], [(0, 2), (2, 2)]]
ZP = [(s, p) for s in range(3) for p in range(4)]
NZ, DS_, SP3, DW, ND, XC, SL = 0, ["lw"] * 3, 0, 32, 4, 0, 64
SCRATCH = {}
SEMAPHORES = ["cV", "cS", "cP", "cG", "ls"]
OPS = []
BANK = {}
SEEDS = (1, 10, 30)
STAGES = [(120000, 0.001, 0.0004), (120000, 0.0004, 0.0)]
GUESS = [(0.87, 1.33, 2.5, 0.32, 210.0, -4.0, 600.0, 550.0, 2400.0, 1000.0, -20.0, 225.0, 410.0, 320.0),
         (0.93, 1.06, 2.5, 0.40, 130.0, 18.0, 900.0, 700.0, 2000.0, 900.0, 10.0, 170.0, 400.0, 650.0),
         (0.83, 1.56, 3.8, 0.38, 150.0, 5.0, 1200.0, 400.0, 2500.0, 1200.0, 0.0, 150.0, 300.0, 500.0),
         (1.13, 2.08, 3.0, 0.48, 245.0, 0.0, 600.0, 410.0, 1900.0, 800.0, -18.0, 250.0, 560.0, 800.0),
         (1.07, 1.8, 4.5, 0.52, 180.0, 10.0, 850.0, 300.0, 4400.0, 800.0, 0.0, 200.0, 470.0, 500.0)]


def buf(name, cols, dtype, where="sbuf"):
    SCRATCH[name] = (where, [128, cols], dtype)


for _n, _c, _d in [
        ("X0", 4160, "bfloat16"), ("X1", 4160, "bfloat16"), ("fwi", 1024, "int32"), ("FW", 1088, "float32"),
        ("swi", 512, "int32"), ("SP", 512, "float32"), ("PW", 512, "float32"), ("awi", 512, "int32"), ("RT", 512, "float32"),
        ("hwi", 1, "int32"), ("thi", 8, "int32"), ("qi", 256, "int32"), ("qf", 256, "float32"),
        ("Z0", 256, "bfloat16"), ("Z1", 256, "bfloat16"), ("Z2", 256, "bfloat16"),
        ("Q0", 256, "float32"), ("Q1", 256, "float32"), ("Q2", 256, "float32"),
        ("ZN0", 256, "bfloat16"), ("ZN1", 256, "bfloat16"), ("ZN2", 256, "bfloat16"),
        ("QN0", 256, "float32"), ("QN1", 256, "float32"), ("YQ", 256, "float32"),
        ("B", 256 * 48, "bfloat16"), ("RS", 4096, "bfloat16"), ("RC", 4096, "bfloat16"), ("LS", 4096, "bfloat16"),
        ("LC", 4096, "bfloat16"), ("ZR", 4096, "bfloat16"), ("IOT", 1088, "float32"), ("IO", 112, "float32"),
        ("UI", 48, "int32"), ("I3I", 144, "int32"), ("O3", 144, "uint16"), ("N1", 512, "int32"), ("PP", 256, "float32"),
        ("AP1", 256, "float32"), ("NM", 1024, "int32"), ("ON", 1024, "uint16"), ("SC", 4 * 288, "float32"), ("SL", 408, "float32"),
        ("KI", 26, "int32"), ("KC6", 26, "int32"), ("CW", 8, "float32"), ("NW", 8 * 8, "bfloat16"),
        ("OW", 144, "uint16"), ("OL", 12, "uint16"), ("MN", 512, "float32"), ("ML", 128, "float32"),
        ("KO", 4, "float32"), ("SC2", 192, "float32"), ("VT", 12, "float32"), ("VP", 12, "float32"), ("OV", 12, "uint16"),
        ("U", 192, "float32"), ("DD", 780, "bfloat16"), ("DS", 780, "bfloat16"), ("KP", 12, "float32"),
        ("VQ", 12, "float32"), ("OK0", 12, "uint16"), ("OK1", 12, "uint16"), ("OK2", 12, "uint16"),
        ("T1", 64, "float32"), ("DG", 128, "bfloat16"), ("XW0", 64, "bfloat16"), ("XW1", 64, "bfloat16"),
        ("XW2", 64, "bfloat16"), ("XL0", 64, "bfloat16"), ("XL1", 64, "bfloat16"), ("XL2", 64, "bfloat16"),
        ("F1", 64, "float32"), ("F2", 64, "float32"), ("TH4", 8, "float32"),
        ("ONE", 384, "bfloat16"), ("ONF", 128, "float32"), ("I3", 128, "bfloat16"),
        ("LN", 144, "bfloat16"), ("STM", 144, "bfloat16"), ("RB8", 48, "bfloat16"), ("RB4", 32, "bfloat16"),
        ("LB", 864, "bfloat16"), ("WRB8", 384, "bfloat16"), ("WRB4", 256, "bfloat16"), ("PI", 4, "int32"), ("CF", 20, "float32"),
        ("OH", 880, "bfloat16"), ("G8", 8, "float32"), ("WR", 24, "bfloat16"),
        ("IG", 128, "float32"), ("GB", 128, "float32"), ("G8T", 128, "float32"), ("IM", 128, "float32"),
        ("M0", 128, "bfloat16"), ("CT", 40, "bfloat16"), ("CR", 8, "bfloat16"), ("DUS", 12, "float32"), ("DUM", 12, "float32"),
        ("KC36", 288, "bfloat16"), ("KC51", 408, "bfloat16"),
        ("M36", 288, "bfloat16"), ("M51", 408, "bfloat16"), ("M65", 780, "bfloat16"), ("T3", 64, "float32"), ("NB", 12, "float32"),
        ("ZT", 512, "bfloat16"), ("Z4", 1024, "bfloat16"), ("I16", 512, "bfloat16"), ("EX", 512, "bfloat16")]:
    buf(_n, _c, _d)
for _n in ["pH", "pK0", "pK1", "pQ"] + ([] if PL else ["pL"]):
    buf(_n, 512, "float32", "psum")
for _n in range(ND):
    buf("pD%d" % _n, 16 * DW, "float32", "psum")
PART = {}
for _n, _c in [("HZ", 144), ("WS", 32), ("DH", 144), ("MK", 16 * SL), ("ZA", 3 * 144), ("ZL", 3 * 144), ("NL", 288), ("ZS", 16 * NZ)]:
    PART[_n] = (sum(c for a, c in PART.values()), _c)
buf("ZZ", sum(c for a, c in PART.values()), "bfloat16")


def spec(name):
    return SCRATCH[name.split("#")[0] + "0"] if "#" in name else SCRATCH[name]


def ap(name, a=0, b=None, step=1, p0=0, p1=128):
    if name == "pL" and PL:
        return ("pH", 192 + a, 192 + b, step, p0, p1)
    if name in PART:
        o, c = PART[name]
        return ("ZZ", o + a, o + (c if b is None else b), step, p0, p1)
    return (name, a, spec(name)[1][1] if b is None else b, step, p0, p1)


def ind(win, off):
    return ("IND", win, off)


def cnt(x):
    return 16 * cnt(x[2]) if x[0] == "IND" else (x[2] - x[1] + x[3] - 1) // x[3]


def wid(x):
    return 2 if spec(x[0])[2] in ("bfloat16", "uint16") else 4


def real(T, x):
    if not isinstance(x, tuple):
        return x
    if x[0] == "IND":
        return real(T, x[1]).indirect(real(T, x[2]))
    t = T[BANK.get(x[0], x[0])]
    if x[3] == 1:
        return t[x[4]:x[5], x[1]:x[2]]
    return t[x[4]:x[5], x[1]:x[2]:x[3]]


def add(eng, cost, outs, ins, fn, sem=None, val=0, after=(), lat=None, grp=None):
    rd, wr = [], []
    for x in ins:
        if isinstance(x, tuple):
            rd.extend([x[1], x[2]] if x[0] == "IND" else [x])
    for x in outs:
        if x[0] == "IND":
            wr.append(x[1])
            rd.append(x[2])
        else:
            wr.append(x)
    OPS.append({"eng": eng, "c": cost, "rd": rd, "wr": wr, "fn": fn, "sem": sem, "val": val, "after": list(after), "lat": lat,
                "grp": grp, "stop": grp is None})
    return len(OPS) - 1


def vcost(out, ins, two=False):
    if out[0] == "IND":
        return (50, 0, 0, cnt(out), 0)
    if ins[0][0] == "IND":
        return (50, 0, cnt(out), 0, 0)
    r = 2.0 if two else (0.5 if all(wid(x) == 2 for x in [out] + ins) else 1.0)
    return (10, max(64, cnt(out) * r), 0, 0, 0)


def tt(out, a, b, op):
    two = a[0] != "IND" and spec(a[0])[0] == "sbuf" and spec(b[0])[0] == "sbuf"
    c = vcost(out, [a, b], two) if (two or a[0] == "IND" or out[0] == "IND") else (10, max(64, cnt(out)), 0, 0, 0)
    return add("V", c, [out], [a, b], lambda g, T, r: [g.vector.tensor_tensor(real(T, out), real(T, a), real(T, b), op)])


def ts(out, a, s1, op0, s2=None, op1=None):
    def fn(g, T, r):
        if op1 is None:
            return [g.vector.tensor_scalar(real(T, out), real(T, a), real(T, s1), None, op0)]
        return [g.vector.tensor_scalar(real(T, out), real(T, a), real(T, s1), real(T, s2), op0, op1)]
    return add("V", vcost(out, [a]), [out], [a, s1, s2], fn)


def cp(out, a):
    return add("V", vcost(out, [a]), [out], [a], lambda g, T, r: [g.vector.tensor_copy(real(T, out), real(T, a))])


def ms(out, v):
    return add("V", vcost(out, [out]), [out], [], lambda g, T, r: [g.vector.memset(real(T, out), v)])


def scan(out, d0, d1, init, op0, op1):
    return add("V", vcost(out, [d0, d1]), [out], [d0, d1],
               lambda g, T, r: [g.vector.tensor_tensor_scan(real(T, out), real(T, d0), real(T, d1), init, op0, op1)])


def act(out, a, func, bias=0.0, scale=1.0):
    c = (65, 0, cnt(out), 0, 0) if a[0] == "IND" else (50, max(64, cnt(out)), 0, 0, 0)
    return add("S", c, [out], [a, bias, scale],
               lambda g, T, r: [g.scalar.activation(real(T, out), real(T, a), func, bias=real(T, bias), scale=real(T, scale))])


def lin(out, a, scale, bias=0.0):
    return act(out, a, F.Identity, bias=bias, scale=scale)


def fill(out, v):
    return lin(out, ap("ONE", 0, cnt(out), 1, out[4], out[5]), v)


def mm(lst, first=True, grp=None, after=(), close=(), each=999):
    c = sum(max(min(64, cnt(l)), cnt(rh)) * (4 if wid(l) == 4 else 1) for o, l, rh in lst)
    ins = [x for o, l, rh in lst + list(close) for x in (l, rh)]
    me = len(OPS)
    def fn(g, T, r):
        stop = OPS[me]["stop"]
        full = lst + list(close) if stop else lst
        return [g.tensor.matmul(real(T, o), real(T, l), real(T, rh), first and i % each == 0,
                                stop and (i == len(full) - 1 or (i + 1) % each == 0))
                for i, (o, l, rh) in enumerate(full)]
    return add("P", (30, 0, 0, 0, c), sorted(set(o for o, l, rh in lst)), ins, fn, grp=grp, after=after)


def iota(out, pat, base=0, cm=0):
    fl = spec(out[0])[2] != "int32"
    def fn(g, T, r):
        if fl:
            return [g.iota(real(T, out), pat, base, cm, allow_small_or_imprecise_dtypes=True)]
        return [g.iota(real(T, out), pat, base, cm)]
    return add("G", (130, 2 * cnt(out), 0, 0, 0), [out], [], fn)


def asel(out, a, pat, op, fill, base, cm):
    return add("G", (170, 2 * cnt(out), 0, 0, 0), [out], [a],
               lambda g, T, r: [g.affine_select(real(T, out), real(T, a), pat, op, fill, base, cm)])


def gfill(out, v):
    return asel(out, ap("ONE", 0, cnt(out), 1, out[4], out[5]), [[0, cnt(out)]], A.is_gt, v, 0, 0)


def gcopy(out, a):
    return asel(out, a, [[0, cnt(out)]], A.is_ge, 0.0, 0, 0)


def dma(outs, ins, fn, nbytes, behind=None, after=(), queue="Y"):
    sem = "d%d" % len(SEMAPHORES)
    SEMAPHORES.append(sem)
    def f2(g, T, r):
        o, i = fn(T)
        (g.sync if queue == "Y" else g.scalar).dma_start(o, i).then_inc(T.sem[sem], 16)
        return []
    same = behind is not None and OPS[behind]["eng"] == queue
    i = add(queue, (0, 0, 0, 0, 0), outs, ins, f2, after=list(after) + ([behind] if same else []), lat="dma")
    j = add("E", (0, 0, 0, 0, 0), [], [], None, after=[i] if behind is None else [i, behind + 1], lat=nbytes)
    add("D", (0, 0, 0, 0, 0), outs, ins, None, sem=sem, val=16, after=[j])
    return i


def send(src, dst, hop):
    sem = "a%d" % len(SEMAPHORES)
    SEMAPHORES.append(sem)
    def fn(g, T, r):
        to = T.cores[(r["rank"] + hop) % NR]
        rid, pid, se = r["topo"].addr(to)
        m = r["topo"].mask(r["core"], to)
        g.remote_dma(real(T, dst), real(T, src), T.sem[sem], T.sem["ls"], pid, rid, m)
        r["ls"] += len(r["topo"].engines(r["core"], to))
        return []
    i = add("G", (0, 0, 0, 0, 0), [], [src], fn, lat="send")
    return add("R", (0, 0, 0, 0, 0), [dst], [], None, sem=sem, val=hop, after=[i])


def col(i, p0=0, p1=128):
    return ap("CF", i, i + 1, 1, p0, p1)


PF, PM, PG, P32, PM3, OFF, ZSC, VS, VB, VMIN, IS15, WCOL, HWF, NI15, NOFF, SPB, SPC, VMAX = range(18)


def setup():
    loads = {"z": (ap("Z0"), lambda T: (T.Z0[:], T.z0[:]), 65536), "h": (ap("hwi"), lambda T: (T.hwi[:], T.hw[:]), 8192),
             "a": (ap("awi"), lambda T: (T.awi[:], T.aw[:]), 262144), "s": (ap("swi"), lambda T: (T.swi[:], T.sw[:]), 262144),
             "q": (ap("qi"), lambda T: (T.qi[0:8, :], T.q0[:]), 8192), "t": (ap("thi"), lambda T: (T.thi[0:1, :], T.th[:]), 32),
             "x": (ap("X0", 0, W), lambda T: (T.X0[:, 0:W], T.lx[:]), 2 ** 20), "f": (ap("fwi"), lambda T: (T.fwi[:], T.fw[:]), 524288),
             "y": (ap("X1", 0, W), lambda T: (T.X1[:, 0:W], T.lx[:]), 2 ** 20)}
    prev = None
    for k in LOADS:
        x, fn, nb = loads[k.lower()]
        prev = dma([x], [], fn, nb, prev, queue="Y" if k.islower() else "S")
    ms(ap("ONE"), 1.0)
    zv = PART[ZV][0]
    ms(ap("HZ"), 0.0)
    ms(ap("ZZ", 144, zv), 0.0)
    for a in range(zv, cnt(ap("ZZ")), 384):
        fill(ap("ZZ", a, min(a + 384, cnt(ap("ZZ")))), 0.0)
    iota(ap("PI", 0, 1), [[0, 1]], 0, 1)
    iota(ap("IO"), [[1, 112]])
    for x in (ap("X0", W), ap("X1", W), ap("FW", 1024)):
        fill(x, 0.0)
    ts(ap("PI", 1, 2), ap("PI", 0, 1), 15, A.bitwise_and)
    ts(ap("PI", 2, 3), ap("PI", 0, 1), 4, A.logical_shift_right)
    ts(ap("PI", 3, 4), ap("PI", 0, 1), 31, A.bitwise_and)
    cp(ap("CF", PF, P32 + 1), ap("PI"))
    ts(col(IS15), col(PM), 15.0, A.is_equal)
    ts(ap("G8"), ap("IO", 0, 8), col(PG), A.is_equal)
    cp(col(HWF), ap("hwi"))
    lin(ap("HZ", 15, 143, 16), ap("G8"), col(HWF))
    for a in (0, 512):
        gcopy(ap("FW", a, a + 512), ap("fwi", a, a + 512))
    ts(ap("PW"), ap("awi"), 32.0, A.add)
    ts(ap("SP"), ap("swi"), 2048.0, A.subtract)
    lin(ap("RT"), ap("PW"), 3232.0, -37888.0 - 51 * 2 ** 17)
    iota(ap("IG"), [[1, 8], [0, 16]])
    iota(ap("IM"), [[0, 8], [1, 16]])
    asel(ap("I3"), ap("ONE", 0, 128), [[-1, 128]], A.is_equal, 0.0, 0, 1)
    iota(ap("I16"), [[1, 32], [0, 16]])
    ts(ap("EX"), ap("I16"), col(P32), A.is_equal)
    ts(ap("G8T", 0, 128, 1, 0, 8), ap("IG", 0, 128, 1, 0, 8), col(PF, 0, 8), A.is_equal)
    ts(ap("M0"), ap("IM"), col(PM), A.not_equal, -16384.0, A.mult)
    asel(ap("qf", 0, 256, 1, 0, 8), ap("qi", 0, 256, 1, 0, 8), [[0, 256]], A.is_ge, 0.0, 0, 0)
    mm([(ap("pQ", 0, 256), ap("G8T", 0, 128, 1, 0, 8), ap("qf", 0, 256, 1, 0, 8))]
       + [(ap("pQ", a, a + 128), ap("I3"), ap("M0")) for a in (0, 128)])
    lin(ap("Q0"), ap("pQ", 0, 256), 1.0, 4096.0)
    ts(ap("GB"), ap("IG"), col(PG), A.is_equal)
    lin(col(PM3), col(PM), 3.0)
    for i, m, a in [(ZSC, -1.0, 1.0), (VMIN, -240.0, 255.0), (WCOL, -69632.0, 4096.0), (VS, 0.5005, 0.4995), (VB, 2.0, ROUND),
                    (NI15, -1.0, 0.0), (OFF, -16384.0, 16384.0), (NOFF, 16384.0, -16384.0), (SPB, 2 / 128, -65 / 128)] + [
                    (VMAX, -240.0, ROUND + 255.0)] * XS:
        lin(col(i), col(IS15), m, a)
    lin(col(SPC), col(PM), 1 / 128, col(SPB))
    lin(ap("DH", 1, 129), ap("M0"), 1.0, 16384.0)
    lin(ap("LN", 0, 128), ap("M0"), -2.0, -32768.0)
    mm([(ap("pQ", 256, 384), ap("I3"), ap(x, 0, 128)) for x in ("LN", "DH")])
    lin(ap("DG"), ap("pQ", 256, 384), 1.0)
    lin(ap("WS", 0, 24, 3), ap("G8"), col(WCOL))
    lin(ap("WS", 2, 24, 3), ap("WS", 0, 24, 3), -1.0)
    lin(ap("WR"), ap("WS", 0, 24), -2.0)
    gfill(ap("MK", 0, None, 16), -32768.0)
    ms(ap("M36"), 0.0)
    gfill(ap("M36", 0, None, 36), BIG)
    gfill(ap("M36", 34, None, 36), MAGIC)
    gfill(ap("M36", 35, None, 36), -MAGIC)
    ms(ap("M51"), 0.0)
    gfill(ap("M51", 0, None, 17), BIG)
    iota(ap("KC36", 0, None, 1, 0, 1), [[0, 8], [65, 2], [3, 18]], -23)
    iota(ap("KC51", 0, None, 1, 0, 1), [[0, 8], [65, 3], [3, 17]], 1)
    for n, a, st in (("KC36", 17, 18), ("KC36", 34, 36), ("KC51", 33, 51), ("KC51", 50, 51)):
        gfill(ap(n, a, None, st, 0, 1), HUGE)
    ts(ap("OH", 0, 48), ap("IO", 0, 48), col(PM3), A.is_equal)
    for a in (48, 96, 192, 384):
        lin(ap("OH", a, 2 * a), ap("OH", 0, a), 1.0)
    ts(ap("OH", 47, 768, 48), ap("IO", 0, 16), col(PM), A.is_equal)
    ts(ap("OH", 768, 816), ap("IO", 0, 48), 1.0, A.subtract, col(PM3), A.is_equal)
    ts(ap("OH", 816, 880), ap("IO", 0, 64), 2.0, A.subtract, col(PM3), A.not_equal)
    ts(ap("CT", 0, 16), ap("ONE", 0, 16), col(PM3), A.mult, 16.0, A.mult)
    for k, v in ((2, 768.0), (3, 816.0)):
        gfill(ap("CT", 8 * k, 8 * k + 8), v)
    lin(ap("CT", 32, 40), ap("ONE", 0, 8), col(OFF), 2048.0)
    iota(ap("CR", 0, 8, 1, 0, 1), [[768, 8]])
    if SP3:
        iota(ap("LN"), [[0, 9], [1, 16]])
        gfill(ap("LN", 0, None, 16), 16.0)
        ts(ap("STM"), ap("LN"), col(PM), A.is_le)
    else:
        asel(ap("WRB8"), ap("ONE"), [[0, 3], [-1, 128]], A.is_equal, 0.0, 0, 1)
        for a, k, v in ((0, 3, 1.0), (192, 1, -2048.0)):
            asel(ap("WRB4", a, a + 64 * k), ap("ZA", 0, 64 * k), [[0, k], [-1, 64]], A.not_equal, v, 0, 1)
    for n, m, k in (("RB8", 8, 3), ("RB4", 4, 4)) if SP3 else ():
        iota(ap(n, m * k), [[0, k], [1, m]])
        ts(ap(n, 0, m * k), ap(n, m * k), col(PG), A.is_equal)
        if m == 4:
            lin(ap(n, 12, 16), ap(n, 12, 16), -2048.0)
        lin(ap(n, m * k), ap(n, 0, m * k), -1.0)
    iota(ap("ONF", 0, 128, 1, 0, 1), [[0, 128]], 1)
    ts(ap("TH4", 0, 8, 1, 0, 1), ap("thi", 0, 8, 1, 0, 1), 4096.0, A.mult, 129.0 + 240 * 4096, A.subtract)
    iota(ap("KI"), [[0, 26]])
    iota(ap("VT"), [[0, 3], [16, 4]])
    iota(ap("KP", 0, 8), [[0, 2], [16, 4]], 4096)
    iota(ap("KP", 8, 12), [[16, 4]], 1024)
    lin(ap("VQ"), ap("KP"), 1.0, col(PM))
    lin(ap("DUM"), ap("VQ"), 1.0, col(OFF))
    lin(ap("DUS"), ap("VQ"), 2.0 ** -20)
    for a in (0, 390):
        ms(ap("M65", a, a + 390), -1 / 128)
    gfill(ap("M65", 0, None, 65), HUGE)
    lin(ap("M65", 64, None, 65), ap("VT"), -1 / 128)
    gfill(ap("DD", 64, None, 65), HUGE)
    iota(ap("IOT", 0, 544), [[1, 544]])
    for a in (0, 272):
        ts(ap("IOT", 544 + a, 816 + a), ap("IOT", a, 272 + a), 544.0, A.add)


def front(s, p, n, units):
    t0, m, hc = 64 * p, n // 16, 16 * s + 4 * p
    Z, Q = "Z%d" % s, "Q%d" % s
    mm([(ap("pH", hc, hc + m), ap("HZ", 15 - r, 143 - r), ap(Z, t0 + r, t0 + n, 16)) for r in range(16)])
    ui = ap("UI", hc, hc + m)
    cp(ui, ap("pH", hc, hc + m))
    o = 3 * hc
    ts(ap("I3I", o, o + m), ui, 2, A.logical_shift_right, 1023, A.bitwise_and)
    ts(ap("I3I", o + m, o + 2 * m), ui, 511, A.bitwise_and)
    ts(ap("I3I", o + 2 * m, o + 3 * m), ui, 3, A.logical_shift_right, 511, A.bitwise_and)
    cp(ap("O3", o, o + 3 * m), ap("I3I", o, o + 3 * m))
    ok, os_, oa = [ap("O3", o + k * m, o + k * m + m) for k in range(3)]
    if p == 0:
        ts(ap("KO"), ap("I3I", o, o + 4), col(OFF), A.add)
    lin(ap("PP", t0, t0 + n), ind(ap("PW"), oa), 1.0)
    tt(ap("AP1", t0, t0 + n), ind(ap("SP"), os_), ap("PP", t0, t0 + n), A.mult)
    tt(ap("N1", 256 + t0, 256 + t0 + n), ind(ap("RT"), oa), ap("AP1", t0, t0 + n), A.add)
    tt(ap("N1", t0, t0 + n), ind(ap("FW" if s else "fwi", 0, 1024), ok), ap(Q, t0, t0 + n), A.max)
    for q, k in units:
        x, y, a = max(t0, 64 * q), min(t0 + n, 64 * q + k), 512 * (s % 2) + 64 * q
        if x < y:
            ts(ap("NM", a + k + x, a + k + y), ap("N1", 256 + x, 256 + y), 5, A.arith_shift_right, 4095, A.bitwise_and)
            cp(ap("ON", a + k + x, a + k + y), ap("NM", a + k + x, a + k + y))
            ts(ap("NM", a + x, a + y), ap("N1", x, y), 4095, A.bitwise_and)
            cp(ap("ON", a + x, a + y), ap("NM", a + x, a + y))
    for a in range(t0, t0 + n, 128):
        k = min(n, 128)
        zt = ap(bank(), 0, 128, 1, 0, k)
        mm([(zt, ap(Z, a, a + k), ap("I3"))])
        lin(ap("ZT", 2 * a, 2 * a + 128, 1, 0, k), zt, -1.0)
        for x in range(0, k, 32):
            TURNED[a + x] = (a, x)


TURN = [0, 0]
TURNED = {}


def bank():
    TURN[0] += 1
    return "pD#%d" % TURN[0]


def spans(md, letters, most):
    out = []
    for k, c in enumerate(md):
        if c in letters:
            if out and out[-1][1] == 32 * k and out[-1][1] - out[-1][0] < most and (32 * k % most or most > 64):
                out[-1] = (out[-1][0], 32 * k + 32)
            else:
                out.append((32 * k, 32 * k + 32))
    return out


def bulk(s, p, md):
    t0, n = 64 * p, 32 * len(md)
    X = ap("X%d" % (s % 2))
    on = 512 * (s % 2) + 2 * t0
    Z = "Z%d" % s

    def lane(k, a, b):
        return ap("B", 48 * (t0 + a) + k, 48 * (t0 + b), 3)

    def flat(name, a, b):
        return ap(name, 16 * (t0 + a), 16 * (t0 + b))

    def greatest(src, a, b):
        for x in range(a, b, SL):
            y = min(b, x + SL)
            scan(lane(2, x, y), ap("MK", 0, 16 * (y - x)), src(x, y), 0.0, A.add, A.max)

    def minus_z(d, x):
        a, r = TURNED[t0 + x]
        return (d, ap("ZT", 2 * a, 2 * a + 128, 1, r, r + 32), ap("EX", 0, 512, 1, r, r + 32))

    for a, b in spans(md, [c for c in MODE if c != "S"], 32) if (s, p) in ZG else ():
        for r in range(4):
            gcopy(ap("Z4", 4 * (t0 + a) + r, 4 * (t0 + b), 4), ap(Z, t0 + a, t0 + b))
        for r in range(4):
            gcopy(ap("ZR", 16 * (t0 + a) + r, 16 * (t0 + b), 4), ap("Z4", 4 * (t0 + a), 4 * (t0 + b)))
    for a, b in spans(md, [c for c in MODE if c != "S"], DW) if (s, p) in ZP else ():
        bk = bank()
        mm([minus_z(ap(bk, 16 * (x - a), 16 * (x - a) + 512), x) for x in range(a, b, 32)], each=1)
        lin(flat("ZR", a, b), ap(bk, 0, 16 * (b - a)), -1.0)
    for a, b in spans(md, [c for c in MODE if c != "S"], NZ) if (s, p) not in ZP + ZG else ():
        z0 = TURN[1] if TURN[1] + 16 * (b - a) <= 16 * NZ else 0
        TURN[1] = z0 + 16 * (b - a)
        cp(ap("ZS", z0, TURN[1], 16), ap(Z, t0 + a, t0 + b))
        for x in range(a, b, SL):
            y = min(b, x + SL)
            scan(flat("ZR", x, y), ap("MK", 0, 16 * (y - x)), ap("ZS", z0 + 16 * (x - a), z0 + 16 * (y - a)), 0.0, A.add, A.max)
    for k, raw, low in ((1, "RC", "LC"), (0, "RS", "LS")):
        o, mine = on + k * n, by(k, "S")
        for a, b in spans(md, by(k, "H"), GV):
            tt(flat(low, a, b), ind(X, ap("ON", o + a, o + b)), flat("ZR", a, b), A.subtract)
            act(lane(k, a, b), flat(low, a, b), F.Abs)
            if k:
                greatest(lambda x, y: flat("LC", x, y), a, b)
        for a, b in spans(md, mine, GS):
            act(flat(raw, a, b), ind(X, ap("ON", o + a, o + b)), F.Identity)
            for x0 in range(a, b, DW):
                y0, bk = min(b, x0 + DW), bank()
                lst = []
                for x in range(x0, y0, 32):
                    d = ap(bk, 16 * (x - x0), 16 * (x - x0) + 512)
                    lst += [minus_z(d, x), (d, ap("I3"), flat(raw, x, x + 32))]
                mm(lst, each=2)
                act(lane(k, x0, y0), ap(bk, 0, 16 * (y0 - x0)), F.Abs)
            if k:
                greatest(lambda x, y: flat("RC", x, y), a, b)
        if k:
            for a, b in spans(md, mine, 128):
                top = ap("B", 48 * (t0 + a) + 47, 48 * (t0 + b), 48)
                tt(top, top, ap(Z, t0 + a, t0 + b), A.subtract)
        for a, b in spans(md, by(k, "V"), GV):
            for x in range(a, b, GV):
                y = min(b, x + GV)
                tt(lane(k, x, y), ind(X, ap("ON", o + x, o + y)), flat("ZR", x, y), A.subtract)
            ts(flat(low, a, b), lane(k, a, b), 0.0, A.min)
            if k:
                greatest(lambda x, y: lane(1, x, y), a, b)


def by(k, who):
    return [c for c in MODE if MODE[c][k] == who]


def spread(out, zname, z0, rhs, c0, cols, n):
    z = ap(zname, z0, z0 + 129, 1, 0, n)
    if not SP3:
        return [(out, ("ZZ", z[1] - r, z[1] - r + 128, 1, 0, n), ap("W" + rhs, 16 * c0 + r, 16 * (c0 + cols), 16, 0, n))
                for r in range(16)]
    y = z[1] - PART["ZA"][0]
    scan(ap("LB", y, y + 129, 1, 0, n), ap("STM", 0, 129, 1, 0, n), z, 0.0, A.mult, A.add)
    w = cnt(ap(rhs)) // 2
    pos, neg = ap(rhs, c0, c0 + cols, 1, 0, n), ap(rhs, w + c0, w + c0 + cols, 1, 0, n)
    return [(out, ap(zname, z0 + 1, z0 + 129, 1, 0, n), pos), (out, ap("LB", y, y + 128, 1, 0, n), pos),
            (out, ap("LB", y + 1, y + 129, 1, 0, n), neg)]


KEYS = []


def tail(s, p, md, halves, nxt):
    n = 32 * len(md)
    t0, m = 64 * p, n // 16
    K = "pK#%d" % len(KEYS)
    BANK[K] = "pK%d" % (len(KEYS) % 2)
    L, H = (36, 18) if p else (51, 17)
    def sl(name, a, b, st=1):
        return ap(name, a, b, st, 0, n)
    mm([(sl(K, 0, 8 * L), ap("ONE", 0, n, 1, 0, 1), ap("KC%d" % L, 0, None, 1, 0, 1))], True, K, KEYS[-2:-1])
    lst = [(sl(K, 16, 8 * L, L), ap("ONF", 0, n, 1, 0, 1), ap("TH4", 0, 8, 1, 0, 1))]
    if s > 0:
        for u, x in UNITS[s - 1]:
            q = PLACE[s - 1].index(u[0])
            c, k = 32 * ((s - 1) % 2) + 8 * q, 64 * len(u)
            c2 = 144 * ((s - 1) % 2)
            lst.append((sl(K, 16, 8 * L, L), ap("ONE", 0, n, 1, 0, k),
                        ap("NW", c, c + 8, 1, 0, k) if q else ap("NL", c2, c2 + 128, 16, 0, k)))
    mm(lst, False, K)
    for k, low in ((1, "LC"), (0, "LS")):
        st, ws = (L, 3) if k or p else (H, 1)
        other = by(k, "V")
        d = mm([(sl(K, H * k + i, 8 * L, st), ap("B", 48 * t0 + 3 * i + k, 48 * (t0 + n), 48), ap("WS", 0, 24, ws))
                for i in range(16)], False, K)
        for a, b in spans(md, other, 128):
            for x, y in ([(a, 64), (64, b)] if a == 32 and b > 64 else [(a, b)]):
                mm([(ap(K, H * k + i, 8 * L, st, x, y), ap(low, 16 * (t0 + x) + i, 16 * (t0 + y), 16), ap("WR", 0, 24, ws))
                    for i in range(16)], False, K, [d],
                   [(sl(K, 0, 8), ap("ONE", 0, n, 1, 0, 1), ap("WS", 24, 32, 1, 0, 1))] if y - x < n else [])
    if p:
        c0, za, z0 = 288 * p, "ZA", 144 * (p - 1)
        KEYS.append(scan(sl("SC", c0, c0 + 288), sl("M36", 0, 288), sl(K, 0, 288), 0.0, A.add, A.min))
        tt(sl("ZA", z0, z0 + 128, 16), sl("SC", c0 + 33, c0 + 288, 36), sl("SC", c0 + 35, c0 + 288, 36), A.subtract)
    else:
        za, z0 = "ZL", 0
        KEYS.append(scan(sl("SL", 0, 408), sl("M51", 0, 408), sl(K, 0, 408), 0.0, A.add, A.min))
        tt(sl("KI", 0, 8), sl("SL", 16, 408, 51), sl("SL", 33, 408, 51), A.min)
        tt(sl("KI", 9, 17), sl("SL", 15, 408, 51), sl("SL", 33, 408, 51), A.max)
        tt(sl("CW", 0, 8), sl("SL", 33, 408, 51), sl("SL", 16, 408, 51), A.is_lt)
        cp(sl("KI", 18, 26), sl("SL", 50, 408, 51))
        ts(sl("KC6", 0, 26), sl("KI", 0, 26), 63, A.bitwise_and)
        cp(sl("ZL", 0, 272, 16), sl("KC6", 0, 17))
        tt(sl("ZL", 288, 416, 16), sl("KC6", 18, 26), sl("CW", 0, 8), A.mult)
    shift = 23.0 if p else -1.0
    ow = 48 * s + 12 * p
    pw = 48 + ow
    mm([(ap("pH", pw, pw + 3 * m), ap("I3"), ap("CT", 0, 24, 8 // m)),
        (ap("pH", pw, pw + m), ap("ONE", 0, 128, 1, 0, 1), ap("CR", 0, m, 1, 0, 1))]
       + spread(ap("pH", pw, pw + 3 * m), za, z0, "RB%d" % m, 0, 3 * m, n))
    ts(ap("OW", ow, ow + 3 * m), ap("pH", pw, pw + 3 * m), shift, A.add)
    last = s == RO - 1
    a, nm = 2 * t0, 512 * (s % 2)
    tt(ap("MN", a, a + 2 * n), ind(ap("OH"), ap("OW", ow + m, ow + 3 * m)), ap("NM", nm + a, nm + a + 2 * n), A.mult)
    for x, q, k, _ in runs(halves, 0, nxt, False):
        act(ap("ZN%d" % s, 64 * q, 64 * (q + k)), ind(ap("B", 48 * t0, 48 * (t0 + n)), ap("OW", ow + 4 * x, ow + 4 * (x + k))),
            F.Abs, scale=col(ZSC))
    rows = 8 if last else 128
    for _, q, k, _ in runs(sorted(halves, key=nxt.index), 0, nxt, False):
        pq = ap("pQ", 64 * q, 64 * (q + k), 1, 0, rows)
        sums = [(ap("pQ", 64 * y, 64 * y + 64, 1, 0, rows), ap("G8" if last else "GB"), ap("MN", c, c + 64))
                for y in range(q, q + k) for c in (a + 64 * halves.index(nxt[y]), a + n + 64 * halves.index(nxt[y]))]
        if last:
            mm(sums, each=2)
            lin(ap("YQ", 64 * q, 64 * (q + k), 1, 0, 8), pq, 1.0)
        else:
            mm([(pq, ap("I3"), ap("M0", 0, 64 * k))] + sums)
            lin(ap("QN%d" % s, 64 * q, 64 * (q + k)), pq, 1.0, 4096.0)
    c, c2 = 32 * (s % 2) + 8 * p, 144 * (s % 2)
    if not last or not p:
        o, x = sl("NW", c, c + 8) if p else sl("NL", c2, c2 + 128, 16), sl(za, z0, z0 + 128, 16)
        if NV:
            ts(o, x, 47.0 - shift, A.is_equal, 4096.0, A.mult)
        else:
            act(o, x, F.Relu, bias=4096.0 * (shift - 46.0), scale=4096.0)


def learn(s, n):
    def sl(name, a, b, st=1):
        return ap(name, a, b, st, 0, 64)
    for c, z0 in ((0, 144), (8, 288)):
        mm([(ap("pL", c, c + 8), ap("I3"), ap("CT", 8 + 2 * c, 24 + 2 * c, 2))] + spread(ap("pL", c, c + 8), "ZL", z0, "RB4", c, 8, 64))
    for a, b in ([(0, 8), (8, 12)] if OLS else [(0, 12)]):
        ts(ap("OL", a, b), ap("pL", a, b), -1.0, A.add)
    tt(ap("SC2", 143, 192, 16), ap("pL", 12, 16), ap("KO"), A.max)
    a = 512 * (s % 2)
    if n == 64:
        tt(ap("ML"), ind(ap("OH"), ap("OL", 0, 8)), ap("NM", a, a + 128), A.mult)
    else:
        tt(ap("ML", 0, 64), ind(ap("OH"), ap("OL", 0, 4)), ap("NM", a, a + 64), A.mult)
        tt(ap("ML", 64, 128), ind(ap("OH"), ap("OL", 4, 8)), ap("NM", a + n, a + n + 64), A.mult)
    c2, ds = 144 * (s % 2), DS_[s]
    scan(sl("LN", 0, 128), sl("MK", 0, 128), sl("NL", c2, c2 + 128), 0.0, A.add, A.max)
    mm([(ap("pL", 128, 256), sl("LN", 0, 128), sl("WRB4", 0, 128))] * 2
       + [(ap("pL", y, y + 64), ap("GB"), ap(src, x, x + 64)) for y, src, x2 in ((192, "MN", n), (128, "ML", 64)) for x in (0, x2)])
    scan(ap("SC2", 0, 128), ap("DG"), ap("pL", 128, 256), 0.0, A.add, A.max)
    act(ap("U", 0, 128), ap("pL", 128, 256), F.Identity)
    if "l" in ds or "w" in ds:
        lin(ap("NB", 0, 8), ap("SC2", 15, 128, 16), -1.0, col(OFF))
    for a, b in LISTS[s]:
        tt(ap("VP", a, b), ap("SC2", 16 * a + 15, 16 * b, 16), ap("DUM", a, b), A.min)
        ts(ap("OV", a, b), ap("VP", a, b), col(OFF), A.subtract)
        ts(ap("VT", a, b), ap("VP", a, b), 2.0 ** -20, A.mult, col(SPC), A.add)
        if b == 12:
            (cp if US else lambda o, x: act(o, x, F.Identity))(ap("U", 128, 192), ind(ap("IOT"), ap("OV", 8, 12)))
            if "k" in ds:
                lin(ap("NB", 8, 12), ap("VP", 8, 12), -1.0, col(OFF))
        for k in range(a, b):
            d, u = ap("DD", 65 * k, 65 * k + 64), ap("U", 64 * (k // 4), 64 * (k // 4) + 64)
            if "lwk"[k // 4] in ds:
                act(d, u, F.Abs, bias=ap("NB", k, k + 1))
            else:
                ts(d, u, ap("VP", k, k + 1) if k >= 8 else ap("SC2", 16 * k + 15, 16 * k + 16), A.subtract, col(NOFF), A.not_equal)
        scan(ap("DS", 65 * a, 65 * b), ap("M65", 65 * a, 65 * b), ap("DD", 65 * a, 65 * b), 0.0, A.add, A.min)
        tt(ap("KP", a, b), ap("VT", a, b), ap("DS", 65 * a + 64, 65 * b, 65), A.subtract)
        tt(ap("VQ", a, b), ap("KP", a, b), ap("DUS", a, b), A.min)
        ts(ap("OK%d" % s, a, b), ap("VQ", a, b), 2.0 ** 20, A.mult)
    X = ap("X%d" % (s % 2))
    tt(ap("T1"), ind(X, ap("OV", 4, 8)), ap("Z%d" % s, 0, 64), A.add)
    lin(ap("T3"), ap("T1"), col(VS), col(VB))
    if XS:
        act(ap("T1"), ap("T3"), F.Relu, bias=col(VMAX), scale=-1.0)
        lin(ap("XW%d" % s), ap("T1"), -1.0, col(VMIN))
    else:
        ts(ap("XW%d" % s), ap("T3"), ROUND, A.subtract, col(VMIN), A.min)
    act(ap("XL%d" % s), ind(X, ap("OV", 0, 4)), F.Relu, bias=col(NI15))
    tt(ap("F1"), ind(ap("FW"), ap("OV", 8, 12)), ap("U", 64, 128), A.subtract)
    tt(ap("F2"), ind(ap("OH"), ap("OL", 8, 12)), ap("F1"), A.mult)
    tt(ind(ap("FW"), ap("OK%d" % s, 8, 12)), ap("F2"), ap("U", 64, 128), A.add)


def update(s, x):
    cp(ind(ap("X%d" % x), ap("OK%d" % s, 0, 4)), ap("XL%d" % s))
    cp(ind(ap("X%d" % x), ap("OK%d" % s, 4, 8)), ap("XW%d" % s))


def runs(u, p, nxt, blocks=True):
    out = []
    for k, h in enumerate(u):
        q = nxt.index(h)
        if out and (out[-1][3] == h // 2 or not blocks) and out[-1][1] + out[-1][2] == q:
            out[-1] = (out[-1][0], out[-1][1], out[-1][2] + 1, out[-1][3])
        else:
            out.append((p + k, q, 1, h // 2))
    return out


def program():
    setup()
    for s in range(RO):
        places = [PLACE[s].index(u[0]) for u, md in UNITS[s]]
        sizes = [64 * len(u) for u, md in UNITS[s]]
        for p, w in FRONTS[s]:
            front(s, p, 64 * w, list(zip(places, sizes)))
        last = s == RO - 1
        nxt = [0, 1, 2, 3] if last else PLACE[s + 1]
        for (u, md), p, n in zip(UNITS[s], places, sizes):
            bulk(s, p, md)
            tail(s, p, md, u, nxt)
            for _, q, k, b in runs(sorted(u, key=nxt.index), 0, nxt) if not last else ():
                x, y = 64 * q, 64 * (q + k)
                send(ap("ZN%d" % s, x, y), ap("Z%d" % (s + 1), x, y), 1 + b + s)
                landed = send(ap("QN%d" % s, x, y), ap("Q%d" % (s + 1), x, y), 1 + b + s)
            if p == 0:
                learn(s, n)
                update(s, (s + 1) % 2)
                if last:
                    two = [([], [ap("FW")], lambda T: (T.yf[:], T.FW[:, 0:1024]), 2 ** 19),
                           ([], [ap("X1")], lambda T: (T.yx[:], T.X1[:, 0:W]), 2 ** 20)]
                    dma(*two[1 - XF], dma(*two[XF]))
        if not last and XC:
            dma([ap("X%d" % (s % 2))], [ap("X%d" % (1 - s % 2))], lambda T, s=s: (T["X%d" % (s % 2)][:], T["X%d" % (1 - s % 2)][:]),
                2 ** 20, None, [landed])
        elif not last:
            update(s, s % 2)
    dma([], [ap("ZN2")], lambda T: (T.yz[:], T.ZN2[:]), 65536)
    dma([], [ap("YQ")], lambda T: (T.yq[:], T.YQ[0:8, :]), 8192, queue="S")


def meet(a, b):
    if a[1] >= b[2] or b[1] >= a[2]:
        return False
    s = min(a[3], b[3])
    if s > 1 and a[3] % s == 0 and b[3] % s == 0 and (a[1] - b[1]) % s:
        return False
    return True


def depend():
    hist, head = {}, {}
    for i, o in enumerate(OPS):
        d = set(o["after"])
        g = o["grp"]
        if g is not None and head.setdefault(g, i) != i:
            d.add(head[g])
        use = [(x, False) for x in o["rd"]] + [(x, True) for x in o["wr"]]
        for x, w in use:
            for j, y, wj in hist.get(x[0], []):
                if (w or wj) and (g is None or OPS[j]["grp"] != g) and meet(x, y):
                    d.add(j)
        for x, w in use:
            hist.setdefault(x[0], []).append((i, x, w))
        o["true"] = d
        names = set(x[0] for x, w in use)
        o["shared"] = sorted(names & set(["pH", "pL", "pQ"]))
        o["diff"] = ([x for x in names if x[:3] == "pD#"] + [None])[0]


def reduce_deps(order, extra):
    reach = [0] * len(OPS)
    for i in order:
        dep = OPS[i]["true"] | extra.get(i, set())
        cover = 0
        for j in dep:
            cover |= reach[j]
        OPS[i]["dep"] = sorted(j for j in dep if not cover >> j & 1)
        reach[i] = 0 if OPS[i]["eng"] == "R" else cover | sum(1 << j for j in OPS[i]["dep"])


def prices(m):
    cost = [o["c"][0] + (o["c"][1] + o["c"][2] * m[1] + o["c"][3] * m[2]) * m[0] + o["c"][4] * m[3]
            + {"V": m[5], "S": m[10]}.get(o["eng"], 0.0) for o in OPS]
    cost = [100 + o["lat"] / m[7] if o["eng"] == "E" else {"dma": m[12], "send": m[13]}.get(o["lat"], c) for o, c in zip(OPS, cost)]
    cost[[o["eng"] for o in OPS].index("R") - 1] += m[9]
    lat = [m[8] if o["eng"] == "R" else (m[6] if o["eng"] == "D" else 0.0) for o in OPS]
    pred = [[(j, lat[j] + (0.0 if o["eng"] in "RDE" or o["eng"] + OPS[j]["eng"] == "PP" or OPS[j]["lat"] == "dma" else
                           m[11] if o["eng"] == OPS[j]["eng"] else m[4])) for j in o["dep"]] for o in OPS]
    return cost, pred, lat, m[4]


def slot(iv, t, c):
    k = len(iv)
    while k > 0 and iv[k - 1][1] > t:
        k -= 1
    while k < len(iv) and iv[k][0] < t + c:
        t = max(t, iv[k][1])
        k += 1
    iv.insert(k, (t, t + c))
    return t


def place(seq, cost, pred, rel, wait=None):
    t0 = [0.0] * len(OPS)
    gaps = {"V": [], "S": [], "P": [], "G": [], "Y": []}
    free = [(0.0, b, None) for b in range(ND)]
    held, edge = {}, {}
    done = [False] * len(OPS)
    late = []
    todo = list(seq)[::-1]
    while todo:
        i = todo.pop()
        u = DIFF[i] if wait is not None else None
        t = rel[i]
        ok = not (u and ENG[i] == "P" and not free)
        for j, d in pred[i]:
            if not done[j]:
                ok = False
                break
            x = t0[j] + cost[j] + d
            if x > t:
                t = x
        if not ok:
            late.append(i)
            continue
        if u and ENG[i] == "P":
            f = min(free)
            free.remove(f)
            held[u] = f[1]
            edge[i] = f[2]
            t = max(t, f[0])
        if ENG[i] in gaps:
            t = slot(gaps[ENG[i]], t, cost[i])
        t0[i] = t
        done[i] = True
        if u and ENG[i] != "P":
            free.append((t + cost[i] + wait, held[u], i))
            todo.extend(late[::-1])
            late = []
    return t0


def rotate(order):
    free = [(b, None) for b in range(ND)]
    held, edge = {}, {}
    for i in order:
        u = DIFF[i]
        if u:
            if ENG[i] != "P":
                free.append((held[u], i))
            elif not free:
                return None, None
            else:
                held[u], edge[i] = free.pop(0)
    return held, edge


def replay(order, edge, cost, pred, lat, wait, a=0, old=None, last=None):
    fin = list(old[1]) if old else [0.0] * len(OPS)
    why = list(old[2]) if old else [None] * len(OPS)
    last = list(last or [None] * 16)
    for i in order[a:]:
        t, w = 0.0, None
        for q, d in AFTER[i]:
            j = last[q]
            if j is not None and fin[j] + d * wait > t:
                t, w = fin[j] + d * wait, j
        for j, d in pred[i]:
            if fin[j] + d > t:
                t, w = fin[j] + d, j
        j = edge.get(i)
        if j is not None and fin[j] + wait > t:
            t, w = fin[j] + wait, j
        t += cost[i]
        fin[i] = t
        why[i] = w
        for q in MARK[i]:
            last[q] = i
    end, top = max((fin[i] + lat[i], i) for i in SINK)
    return end, fin, why, top


ENG, DIFF, AFTER, MARK, SINK = [], [], [], [], []


def schedule(seed, rounds, tries):
    n = len(OPS)
    ENG[:] = [o["eng"] for o in OPS]
    DIFF[:] = [o["diff"] for o in OPS]
    slots = dict((x, k) for k, x in enumerate(list("VSPGY") + [b + e for b in ("pH", "pL", "pQ") for e in "VSP"]))
    MARK[:] = [[slots[x] for x in [o["eng"]] + [b + o["eng"] for b in o["shared"]] if x in slots] for o in OPS]
    AFTER[:] = [([(slots[o["eng"]], 0)] if o["eng"] in slots else [])
                + [(slots[b + e], 1) for b in o["shared"] for e in "VSP" if e != o["eng"]] for o in OPS]
    reduce_deps(range(n), {})
    anc = [0] * n
    for i in range(n):
        for j in OPS[i]["true"]:
            anc[i] |= anc[j] | 1 << j
    rnd = np.random.RandomState(seed)
    pr = [prices(m) for m in GUESS]
    cost, pred, lat, wait = pr[0]
    succ = [[] for _ in OPS]
    for i in range(n):
        for j, d in pred[i]:
            succ[j].append((i, d))
    zero = [0.0] * n
    base = [sum(p[0]) / 3.0 for p in pr]

    SINK[:] = [i for i in range(n) if not succ[i]]

    def judge(order, a=0, old=None):
        held, edge = rotate(order)
        if edge is None:
            return (1e9, order, None)
        last = [None] * 16
        for i in order[:a]:
            for q in MARK[i]:
                last[q] = i
        res = [replay(order, edge, *p, a, old and old[k], last) for k, p in enumerate(pr)]
        return (sum((r[0] + SMOOTH * sum(r[1]) / n) / b for r, b in zip(res, base)) / len(pr), order, res)

    def settle(key, m):
        key = list(key)
        for i in range(n):
            for j, d in pred[i]:
                if key[j] >= key[i]:
                    key[i] = key[j] + 1e-3
        t1 = place(sorted(range(n), key=lambda i: key[i]), m[0], m[1], zero, m[3])
        return judge(sorted(range(n), key=lambda i: (t1[i], i)))

    best = cur = settle(range(n), pr[0])
    for k in range(rounds):
        c2 = [c * (1 + 0.25 * x) for c, x in zip(cost, rnd.rand(n))] if k % 3 == 2 else cost
        back = place(sorted(range(n), key=lambda i: (-cur[2][0][1][i], -i)), c2, succ, lat)
        new = settle([-(back[i] + c2[i]) for i in range(n)], pr[0])
        cur = new if new[2] else best
        if cur[0] < best[0]:
            best = cur
        elif k % 3 == 1:
            cur = best
    for k in range(tries):
        a, w, sg = rnd.rand() * best[2][0][0], [3e3, 8e3, 20e3][rnd.randint(3)], [300.0, 1000.0, 3000.0][rnd.randint(3)]
        key = [t - c + z if a < t < a + w else t - c for t, c, z in zip(best[2][0][1], cost, (rnd.randn(n) * sg).tolist())]
        new = settle(key, pr[rnd.randint(len(pr))] if rnd.rand() < 0.3 else pr[0])
        if new[0] < best[0]:
            best = new
    return best[1]


def improve(order, seed, moves, hot, cold):
    n = len(OPS)
    reduce_deps(range(n), {})
    pr = [prices(m) for m in GUESS]
    rnd = np.random.RandomState(seed)
    base = [sum(p[0]) / 3.0 for p in pr]
    anc = [0] * n
    for i in range(n):
        for j in OPS[i]["true"]:
            anc[i] |= anc[j] | 1 << j
    delay = [[0.0, p[3]] for p in pr]
    pred, succ = [[] for _ in OPS], [[] for _ in OPS]
    for i in range(n):
        for k, (j, d) in enumerate(pr[0][1][i]):
            pred[i].append((j, len(delay[0])))
            succ[j].append((i, len(delay[0])))
            for p, dl in zip(pr, delay):
                dl.append(p[1][i][k][1])
    for i in SINK:
        succ[i].append((n, len(delay[0])))
        for p, dl in zip(pr, delay):
            dl.append(p[2][i])
    cost = [p[0] + [0.0] for p in pr]
    own = [a[0][0] if a and a[0][1] == 0 else -1 for a in AFTER]
    other = [[q for q, d in a if d] for a in AFTER]
    role = [0 if not DIFF[i] else (1 if ENG[i] == "P" else 2) for i in range(n)]
    mates = [[(x, y) for x in MARK[i][1:] for y in other[i] if (x - 5) // 3 == (y - 5) // 3] for i in range(n)]

    def links(seg, last, w, read):
        res = []
        for i in seg:
            l = pred[i]
            if own[i] >= 0:
                l = l + [(last[own[i]], 0)]
                for x in other[i]:
                    l.append((last[x], 1))
                if role[i] == 1:
                    if w >= ND:
                        if w - ND >= len(read):
                            return None
                        l.append((read[w - ND], 1))
                    w += 1
                elif role[i] == 2:
                    read.append(i)
                for x in MARK[i]:
                    last[x] = i
            res.append(l)
        return res

    order = list(order)
    pos = [n] * (n + 1)
    for k, i in enumerate(order):
        pos[i] = k
    read = []
    ln = dict(zip(order, links(order, [n] * 16, 0, read)))
    wrote = [i for i in order if role[i] == 1]
    before, after, wb, rb = [None] * (n + 1), [None] * (n + 1), [0] * (n + 1), [0] * (n + 1)
    before[0], after[n] = [n] * 16, [n] * 16
    F, Q, end = [[0.0] * (n + 1) for p in pr], [[0.0] * (n + 1) for p in pr], [0.0] * len(pr)
    out = [list(s) for s in succ]
    for i in order:
        for j, d in ln[i][len(pred[i]):]:
            if j < n:
                out[j].append((i, d))

    def marks(a, b):
        last, w, r, k = before[a][:], wb[a], rb[a], a
        while k < n:
            i = order[k]
            k += 1
            for x in MARK[i]:
                last[x] = i
            w += role[i] == 1
            r += role[i] == 2
            if k >= b and before[k] == last:
                break
            before[k], wb[k], rb[k] = last[:], w, r
        nxt, k = after[b][:], b
        while k > 0:
            k -= 1
            for x in MARK[order[k]]:
                nxt[x] = order[k]
            if k < a and after[k] == nxt:
                break
            after[k] = nxt[:]

    def times(a, b):
        sc = 0.0
        for m in range(len(pr)):
            c, dl = cost[m], delay[m]
            for f, seq, arcs in ((F[m], order[a:], ln), (Q[m], order[b - 1::-1], out)):
                for i in seq:
                    t = 0.0
                    for j, d in arcs[i]:
                        x = f[j] + dl[d]
                        if x > t:
                            t = x
                    f[i] = t + c[i]
            end[m] = max(Q[m])
            sc += (end[m] + SMOOTH * sum(F[m]) / n) / base[m]
        return sc / len(pr)

    def relink(ops, new):
        for i, l in zip(ops, new):
            for j, d in ln[i][len(pred[i]):]:
                if j < n:
                    out[j].remove((i, d))
            for j, d in l[len(pred[i]):]:
                if j < n:
                    out[j].append((i, d))
            ln[i] = l

    def freed(a, b, rd):
        return [(rd[r], wrote[r + ND], 1) for r in range(rb[a], min(len(rd), len(wrote) - ND)) if pos[wrote[r + ND]] >= b]

    def change(seg, a, b):
        last, rd = before[a][:], read[:rb[a]]
        l2 = links(seg, last, wb[a], rd)
        if l2 is None:
            return 1e9, None, None
        nxt, was, tot = after[b], before[b], 0.0
        cross = [(last[x], nxt[x], 0) for x in range(5)] + freed(a, b, rd)
        for j in seg:
            for i, d in succ[j]:
                if pos[i] >= b:
                    cross.append((j, i, d))
            for x, y in mates[j]:
                if last[x] == j:
                    cross.append((j, nxt[y], 1))
        for c, dl, bs, e, f0, q in zip(cost, delay, base, end, F, Q):
            f, s, top = f0[:], 0.0, 0.0
            for i, l in zip(seg, l2):
                t = 0.0
                for j, d in l:
                    x = f[j] + dl[d]
                    if x > t:
                        t = x
                x = f0[i]
                t += c[i]
                s += t - x
                f[i] = t
                x += q[i] - c[i]
                if x > top:
                    top = x
            t = e if top < e - 1e-6 else 0.0
            for j, i, d in cross:
                x = f[j] + dl[d] + q[i]
                if x > t:
                    t = x
            s += (f[last[0]] + f[last[1]] + f[last[2]] - f0[was[0]] - f0[was[1]] - f0[was[2]]) * (n - b) / 6.0
            tot += (t - e + SMOOTH * s / n) / bs
        return tot / len(pr), l2, rd

    def take(seg, a, b, l2, rd):
        touch = set(x for x in after[b] if x < n) | set(x[1] for x in freed(a, b, rd))
        order[a:b] = seg
        for k in range(a, b):
            pos[order[k]] = k
        read[rb[a]:len(rd)] = rd[rb[a]:]
        ws = [i for i in seg if role[i] == 1]
        wrote[wb[a]:wb[a] + len(ws)] = ws
        marks(a, b)
        relink(seg, l2)
        for i in sorted(touch):
            k = pos[i]
            relink([i], links([i], before[k][:], wb[k], read[:rb[k]]))
        return times(a, b)

    def chain(m, i):
        f, c, dl, res = F[m], cost[m], delay[m], []
        while f[i] - c[i] > 1e-6:
            t = f[i] - c[i] - 1e-6
            for j, d in ln[i]:
                if f[j] + dl[d] > t:
                    break
            if not anc[i] >> j & 1:
                res.append((j, i))
            i = j
        return res

    marks(0, n)
    best = (times(0, n), order[:], end[:])
    crit = {}
    for k, z in enumerate(rnd.rand(moves, 8).tolist()):
        m = int(z[0] * len(pr))
        if z[1] < FILL:
            a = int(z[2] * n)
            j = order[a]
            if not 0 <= own[j] <= 2 or F[m][j] - cost[m][j] - F[m][before[a][own[j]]] < 1.0:
                continue
            later = [x for x in order[a + 1:a + 60] if own[x] == own[j] and not anc[x] >> j & 1][:8]
            if not later:
                continue
            i = later[int(z[3] * len(later))]
            b, ahead = pos[i] + 1, True
        else:
            if z[2] < 0.3:
                pairs = chain(m, order[int(z[3] * n)])
            else:
                if m not in crit:
                    crit[m] = chain(m, max((F[m][i] + Q[m][i] - cost[m][i], i) for i in SINK)[1])
                pairs = crit[m]
            if not pairs:
                continue
            j, i = pairs[int(z[4] * len(pairs))]
            far, ahead = int(z[5] ** 3 * 40), z[6] < 0.5
            a, b = (max(0, pos[j] - far), pos[i] + 1) if ahead else (pos[j], min(n, pos[i] + 1 + far))
        seg = order[a:b]
        if ahead:
            seg = [x for x in seg if anc[i] >> x & 1] + [i] + [x for x in seg[:-1] if not anc[i] >> x & 1]
        else:
            seg = [x for x in seg[1:] if not anc[x] >> j & 1] + [j] + [x for x in seg if anc[x] >> j & 1]
        d, l2, rd = change(seg, a, b)
        if d <= -(hot + (cold - hot) * k / moves) * np.log(z[7] + 1e-12):
            sc = take(seg, a, b, l2, rd)
            crit = {}
            if sc < best[0]:
                best = (sc, order[:], end[:])
    return best


SMOOTH = 0.3
FILL = 0.5


def build():
    del OPS[:]
    del SEMAPHORES[5:]
    del KEYS[:]
    TURN[:] = [0, 0]
    program()
    depend()
    order, ends = schedule(*SEEDS), []
    for k, (moves, hot, cold) in enumerate(STAGES):
        score, order, ends = improve(order, SEEDS[0] + k, moves, hot, cold)
    held, edge = rotate(order)
    extra = dict((i, set([j])) for i, j in edge.items() if j is not None)
    for u, b in held.items():
        BANK[u] = "pD%d" % b
    hist, last = {}, {}
    for i in order:
        for b in OPS[i]["shared"]:
            extra.setdefault(i, set()).update(j for j in hist.get(b, []) if ENG[j] != ENG[i])
            hist.setdefault(b, []).append(i)
        if OPS[i]["grp"] is not None:
            last[OPS[i]["grp"]] = i
    for i in last.values():
        OPS[i]["stop"] = True
    reduce_deps(order, extra)
    return order, ends


ORDER, EST = build()


def rank_program(g, core, T, topo):
    rank = T.rank_of(core)
    if rank is None:
        return
    r = {"rank": rank, "core": core, "topo": topo, "ls": 0}
    queue = {"V": g.vector, "S": g.scalar, "P": g.tensor, "G": g, "Y": g.sync}
    count = {"cV": 0, "cS": 0, "cP": 0, "cG": 0}
    done = {}
    seen = {}
    for i in ORDER:
        o = OPS[i]
        e = o["eng"]
        if e == "R":
            done[i] = (o["sem"], len(topo.engines(T.cores[(rank - o["val"]) % NR], core)))
            continue
        if e in "DE":
            done[i] = (o["sem"], o["val"]) if e == "D" else None
            continue
        need = {}
        for j in o["dep"]:
            if done[j] is None or (e == "P" and OPS[j]["eng"] == "P"):
                continue
            need[done[j][0]] = max(need.get(done[j][0], 0), done[j][1])
        for sem, v in need.items():
            if seen.get((e, sem), 0) < v:
                queue[e].wait_ge(T.sem[sem], v)
                seen[(e, sem)] = v
        ins = o["fn"](g, T, r)
        for x in ins:
            x.then_inc(T.sem["c" + e], 1)
        if ins:
            count["c" + e] += len(ins)
        done[i] = ("c" + e, count["c" + e]) if ins else None
    final = dict(count)
    final["ls"] = r["ls"]
    for i in ORDER:
        if OPS[i]["sem"] is not None:
            final[done[i][0]] = done[i][1]
    for sem, v in final.items():
        if v and seen.get(("G", sem), 0) < v:
            g.wait_ge(T.sem[sem], v)
